import numpy as np, ml_dtypes
CORES = [3,11,19,27,35,43,51,59]
N = 8
import mx_ref
BF = ml_dtypes.bfloat16
def gentries(a):
    return np.ascontiguousarray(a.reshape(8, 16, -1).transpose(0, 2, 1)).reshape(8, -1)
def gtable(e):
    e = np.asarray(e); return np.ascontiguousarray(e.reshape(8, -1, 16).transpose(0, 2, 1)).reshape(128, -1).astype(np.int32)
def gcols(t, e):
    v = np.concatenate([t.reshape(8, 16, -1, 4), np.zeros((8, 16, 1, 4), BF)], axis=2)
    return np.ascontiguousarray(np.stack([v[g][:, e[g]] for g in range(8)])).reshape(128, -1)
def tile(rs):
    return np.stack(rs, axis=2).reshape(128, -1).astype(BF)
def pick(q, e):
    c = np.concatenate([q[0].reshape(128, -1, 4), np.zeros((128, 1, 4), np.uint8)], axis=1); s = np.concatenate([q[1], np.ones((16, 1), np.uint8)], axis=1)
    return (np.ascontiguousarray(c[:, e].reshape(128, -1)), np.ascontiguousarray(s[:, e]))
def join(*qs):
    return (np.concatenate([q[0] for q in qs], axis=1), np.concatenate([q[1] for q in qs], axis=1))
def put(q, e, v):
    c, s = q[0].reshape(128, -1, 4).copy(), q[1].copy(); c[:, e] = v[0].reshape(128, -1, 4); s[:, e] = v[1]
    return (c.reshape(128, -1), s)
def pk(c, s):
    return (np.ascontiguousarray(c), mx_ref.live(s))
def emit(q):
    return q[0], q[1]
def packed(v, rng):
    q = [mx_ref.quantize(np.ascontiguousarray(v[r])) for r in range(N)]
    return np.stack([a for a, b in q]), np.stack([mx_ref.plane(b, rng) for a, b in q])
def values_of_codes():
    e, c = np.zeros((128, 128, 4), np.float32), np.zeros((128, 2, 4), np.uint8)
    e[np.arange(128), np.arange(128), 0] = 1
    c[:127, :, 0] = np.arange(256).reshape(2, 128).T[:127]
    return mx_ref.matmul(mx_ref.quantize(e.reshape(128, 512).astype(BF)), (c.reshape(128, 8), np.full((16, 2), 127, np.uint8))).T.reshape(-1).astype(np.float64)
CODE_VALUE, SCALE_VALUE = values_of_codes(), 2.0 ** (np.arange(256) - 127.0)
def decode(q):
    return (CODE_VALUE[q[0]].reshape(16, 8, -1, 4) * SCALE_VALUE[q[1]][:, None, :, None] + 0.0).reshape(128, -1).astype(np.float32)
def f(rng, *shape):
    return mx_ref.flush((rng.standard_normal(shape, dtype=np.float32) * np.exp2(rng.integers(-2, 3, shape[:-1] + (1,)))).astype(BF))
def wide(rng, *shape, cols=0):
    v = rng.standard_normal(shape, dtype=np.float32) * np.exp2(rng.integers(-12, 13, shape)).astype(np.float32)
    if cols: v *= np.repeat(np.exp2(rng.integers(-cols, cols + 1, shape[:-2] + (1, shape[-1] // 4))) * (rng.random(shape[:-2] + (1, shape[-1] // 4)) > 0.0625), 4, axis=-1).astype(np.float32)
    return mx_ref.flush(v.astype(BF))
C, DOUBLINGS = 320, 9
STEP = [1, 2, 4]
def numbers_of(rng):
    return {"x": np.array(f(rng, N, 128, 4 * C)), "u": np.array(f(rng, N, 128, 512)), "v": np.array(f(rng, N, 128, 512))}
def links(rng, far=False):
    l = rng.permuted(np.tile(np.arange(C), (N, 8, 2, 1)), axis=3)
    if far:
        for r in range(N):
            for i, g in enumerate(rng.permutation(8)[:6]):
                o = rng.permutation(C)
                l[r, g, 0, o] = np.append(o[1:], o[[0, C - 1, C // 2][i % 3]])
                if i < 3: l[r, g, 1] = l[r, g, 0]
    return l
def stored(l):
    return {"la": np.stack([gtable(l[r, :, 0]) for r in range(N)]), "lb": np.stack([gtable(l[r, :, 1]) for r in range(N)])}
def layers(rng, still=[]):
    w = np.array(f(rng, N, 128, 2048)).reshape(N, 8, 16, 4, 8, 16, 4)
    for i in still:
        w[:, :, i] = 0
        w[:, :, :, :, :, i] = 0
    return w
def weights(rng, w):
    c, p = packed(np.ascontiguousarray(w).reshape(N, 128, 2048), rng)
    return {"wc": c, "ws": p}
def setup_inputs(rng):
    return {**numbers_of(rng), **stored(links(rng)), **weights(rng, layers(rng))}
def setup_inputs_ties(rng):
    d = numbers_of(rng)
    o = rng.permutation(N)
    k = rng.integers(-2, 3, (N, 8, C))
    k[o[1]] = -rng.integers(1, 5, (8, C))
    far = rng.permutation(8)
    k[o[2], far[:4]] = 1
    k[o[3], rng.permutation(8)[:4]] = -1
    l = links(rng, True)
    way = rng.permutation(C)
    way[-2:] = np.sort(way[-2:])
    for g, end, top in ((far[4], way[-1], way[-1]), (far[5], way[0], 0)):
        l[o[2], g, 0, way] = np.append(way[1:], end)
        l[o[2], g, 1] = np.arange(C)
        k[o[2], g] = 1
        k[o[2], g, top] = 2
    x = d["x"].reshape(N, 8, 16, C, 4)
    x[:, :, 0] = 0
    x[:, :, 0, :, 0] = k.astype(np.float32).astype(BF)
    u = d["u"].reshape(N, 128, 128, 4)
    u[:, :, ::16] = 0
    for r in range(N):
        for h in range(0, 128, 16): u[r, h, h, 0] = 0.0 if r == o[0] else 1.0
    return {"x": x.reshape(N, 128, 4 * C), "u": u.reshape(N, 128, 512), "v": d["v"], **stored(l), **weights(rng, layers(rng, [0]))}
def setup_inputs_near(rng):
    d = numbers_of(rng)
    x = d["x"].astype(np.float32).reshape(N, 8, 16, C, 4)
    x[:, :, 0] = 0
    x[:, :, 8:] = 0
    u = d["u"].reshape(N, 128, 128, 4)
    u[:, :, ::16] = 0
    w = layers(rng, [0, 8, 9, 10, 11, 12, 13, 14, 15])
    o = rng.permutation(N) % 4
    for r in range(N):
        s = rng.integers(0, 16, (8, C))
        digits = ((s[:, :, None] >> np.arange(4)) & 1) * np.exp2(np.arange(4) - 23.0)
        if o[r] < 3: x[r, :, 12, :, 0] = rng.choice([-1.0, 1.0], (8, C)) * 2.0 ** -20
        if o[r] < 2:
            x[r, :, 0, :, 0] = np.where(rng.permutation(8) < 4, -1.0, 1.0)[:, None]
            x[r, :, 8] = digits
            x[r, :, 11, :, 0] = 2.0 ** -10
        elif o[r] == 2: x[r, :, 8] = digits * rng.choice([-1.0, 1.0], (8, C, 1))
        else:
            e = rng.integers(-1, 2, (8, C)) * 2.0 ** -30
            x[r, :, 8, :, 0] = 1.25 * e
            x[r, :, 9, :, 0] = -1.125 * e
            x[r, :, 15, :, 0] = 2.0 ** -30
            for g in range(8):
                w[r, g, 12, 0, g, 10, 0] = 2.0 ** -18
                w[r, g, 14, 0, g, 10, 0] = 2.0 ** -8
        at = [0, C - 1, int(rng.integers(C)), int(rng.integers(C))]
        for g, j in zip(rng.permutation(8)[:4], at): x[r, g, 0, j, 0] = 2.0 ** 29 * rng.choice([-1.0, 1.0])
        k = 1.0 if o[r] == 0 else 2.0 ** -30
        for h in range(0, 128, 16):
            u[r, h, h, 0] = k if o[r] < 2 else 1.0
            if o[r] < 2: u[r, h + 11, h, 0] = k
            if o[r] < 3: u[r, h + 8, h] = k
            else:
                u[r, h + 8, h, 0] = k
                u[r, h + 9, h, 0] = 1.125 * k
                u[r, h + 10, h, 0] = k
    return {"x": x.reshape(N, 128, 4 * C).astype(BF), "u": u.reshape(N, 128, 512), "v": d["v"], **stored(links(rng, True)), **weights(rng, w)}
def setup_inputs_odd(rng):
    d = numbers_of(rng)
    x = (1.0 + (2 * rng.integers(0, 64, (N, 16, 8, C, 4)) + 1) * 2.0 ** -7) * np.exp2(-rng.integers(0, 7, (N, 16, 8, C, 4)).astype(np.float64)) * rng.choice([-1.0, 1.0], (N, 16, 8, C, 4))
    x[:, :, 0, :, 0] = np.where(rng.random((N, 16, C)) < 0.25, 1.875, 1.96875) * 2.0 ** 8
    x[:, ::2, 1, :, 0] = rng.choice([-1.0, 1.0], (N, 8, C)) * (8 + rng.integers(0, 2, (N, 8, C))) * 2.0 ** -8
    u = d["u"].reshape(N, 16, 8, 128, 4)
    u[:, :, :, ::16] = 0
    for g in range(8): u[:, 2 * g, 1, 16 * g, 0] = 1.0
    return {"x": x.astype(np.float32).reshape(N, 128, 4 * C).astype(BF), "u": u.reshape(N, 128, 512), "v": d["v"], **stored(links(rng)), **weights(rng, layers(rng, [0, 8]))}
def setup_inputs_ends(rng):
    d = numbers_of(rng)
    o, e = rng.permutation(N) % 4, rng.permutation(N) % 4
    m = int(rng.integers(8))
    l = links(rng, True)
    small = -(1.0 + 0.125 * rng.integers(0, 8, (N, 8, 16, C, 4)))
    x = -(0.88 + 0.08 * rng.random((N, 8, 16, C, 4))) * 2.0 ** 30
    x[o == 1] *= rng.choice([-1.0, 1.0], (N, 1, 1, C, 1))[o == 1]
    x[o == 2] = small[o == 2] * 2.0 ** -30
    x[o == 3] = d["x"].astype(np.float32).reshape(N, 8, 16, C, 4)[o == 3][:, :, :, :1]
    x[:, m] = small[:, m] * 2.0 ** -20
    u = d["u"].astype(np.float32).reshape(N, 8, 16, 128, 4)
    v = rng.choice([-1.0, 1.0], (N, 128, 512)) * np.where(o < 2, 2.0 ** 30, 2.0 ** -30)[:, None, None]
    w = np.zeros((N, 128, 4, 128, 4), np.float32)
    i = np.arange(128)
    for r in range(N):
        h = rng.permutation(8)
        c = np.where(h < 2, 0.0, h % 2 * 2.0 - 1.0)[:, None]
        if o[r] < 2: u[r, :, :, ::16] = c * (0.9 + 0.1 * rng.random((8, 16, 8, 4))) * 2.0 ** 30
        if o[r] == 2: u[r, :, :, ::16] = c * (1.0 + 0.125 * rng.integers(0, 8, (8, 16, 8, 4))) * 2.0 ** -30
        if o[r] == 3: u[r, :, :, ::16] *= np.abs(c).astype(np.float32)
        k = np.zeros(8)
        if o[r] < 2: k = rng.choice([-1.0, 1.0], 8) * np.array([0.75, 0.5, 2.0 ** -8])[rng.permutation(8) % 3]
        k[m] = 2.0 ** 8
        for b in range(4): w[r, i, b, i, b] = k[i // 16]
        if e[r] < 2:
            l[r, :, e[r]] = C - 1
            l[r, :, 1 - e[r]] = 0
        if e[r] == 2: l[r] = rng.integers(0, C, (8, 2, C))
    u[:, m, :, ::16] = 0
    return {"x": x.astype(np.float32).reshape(N, 128, 4 * C).astype(BF), "u": u.reshape(N, 128, 512).astype(BF), "v": v.astype(np.float32).astype(BF), **stored(l), **weights(rng, w.astype(BF))}
def setup_inputs_spread(rng):
    d = setup_inputs(rng)
    d["x"] = wide(rng, N, 128, 4 * C, cols=6)
    return d
def check_inputs(d):
    b = []
    for k in ("x", "u", "v"):
        a = np.abs(d[k].astype(np.float32))
        if not (np.isfinite(a).all() and ((a == 0) | (a >= 2.0 ** -30) & (a <= 2.0 ** 30)).all()): b.append("a value of " + k)
    for k in ("la", "lb"):
        if not ((d[k] >= 0) & (d[k] < C)).all(): b.append("an entry of " + k)
    none, least, most = [emit(mx_ref.quantize(np.full((128, 16), k, np.float32).astype(BF)))[1][0, 0] for k in (0.0, 2.0 ** -8, 2.0 ** 8)]
    for r in range(N):
        if ((d["wc"][r] == 0x7F) | (d["wc"][r] == 0xFF)).any(): b.append("wc: a code that is no number")
        s = mx_ref.live(d["ws"][r])
        if ((s != none) & ((s < least) | (s > most))).any(): b.append("ws: a scale out of range")
        if (((d["wc"][r].reshape(16, 8, 512, 4) & 0x7F) != 0) & (s == none)[:, None, :, None]).any(): b.append("wc: a code other than zero under the scale of zeros")
    return b
def look(t, e):
    return np.take_along_axis(t, e, axis=1)
def leaders(p):
    low, at = np.tile(np.arange(C), (8, 1)), p
    for k in range(DOUBLINGS):
        low = np.minimum(low, look(low, at))
        at = look(at, at)
    return look(low, at)
def reference(x, u, v, la, lb, wc, ws):
    qu = [mx_ref.quantize(u[r]) for r in range(N)]
    lay = [pk(wc[r], ws[r]) for r in range(N)]
    l0, l1 = [gentries(la[r]) for r in range(N)], [gentries(lb[r]) for r in range(N)]
    now = [x[r] for r in range(N)]
    for step in STEP:
        own, torn, sent = [], [], []
        for r in range(N):
            q = mx_ref.quantize(now[r])
            s = mx_ref.matmul(qu[r], q)[::16] + np.float32(0.0)
            p = np.where(s < 0, l1[r], l0[r])
            lead = leaders(p)
            e = np.where(lead == np.arange(C), lead, p)
            own.append(decode(q).astype(BF))
            torn.append(e)
            z = own[r]
            for k in range(3):
                z = ((z.astype(np.float32) + gcols(z, e).astype(np.float32)) * np.float32(0.5)).astype(BF)
                e = look(e, e)
            sent.append(mx_ref.quantize(z))
            change = look(s, lead) > s
            l0[r], l1[r] = np.where(change, l1[r], l0[r]), np.where(change, l0[r], l1[r])
        for r in range(N):
            z = sent[(r - step) % N]
            h = tile([mx_ref.matmul(pick(lay[r], np.arange(128 * b, 128 * b + 128)), z) * np.float32(0.03125) for b in range(4)])
            now[r] = (own[r].astype(np.float32) + gcols(h, torn[r]).astype(np.float32)).astype(BF)
    y, ls = np.zeros((N, 128, C), np.float32), np.zeros((N, 8, 2 * C), np.float32)
    oc, osc = np.zeros((N, 128, 4 * C), np.uint8), np.zeros((N, 16, C), np.uint8)
    for r in range(N):
        q = mx_ref.quantize(now[r])
        y[r] = mx_ref.matmul(mx_ref.quantize(v[r]), q)
        ls[r] = np.concatenate([l0[r], l1[r]], axis=1)
        oc[r], osc[r] = emit(q)
    return {"y": y, "ls": ls, "oc": oc, "osc": osc}

@@ -1,0 +1,284 @@
+from concourse.mybir import dt, AluOpType, ActivationFunctionType
+
+C = 320
+H = 160
+STEP = [1, 2, 4]
+BF, F32, I32, U16 = "bfloat16", "float32", "int32", "uint16"
+
+SCRATCH = {}
+
+
+def _sb(dtype, **kw):
+    for k, n in kw.items():
+        SCRATCH[k] = ("sbuf", [128, n], dtype)
+
+
+_sb(BF, xin=1280, uin=512, vin=512, e8=516, e1=516, iot=320, tpos=320, n0=320, n1=320, kk=320, sca=320, mm=320,
+    aw=320 * 8, low=320 * 9, tf=960, bw=960, fw=1280, fo=1280, hw=1280, z1=1280, z2=1280, z3=1280, xt=1280, tmp=640,
+    fl=320, ld=320 * 9, fd=640, d1=1280, d2=1280)
+_sb(F32, iof=320, dj=128, m16=20, kf=1, k1=1, scl=1, scm=1, thr=1, inv=1, cw=20, cb=20, sf=320, l0w=20, l1w=20,
+    dw=20, ss=20, sg=320, tp=20, pw=20, dcp=20, ew=20, ed=20, eg=20, tw=20, lsf=640, yf=320)
+_sb(I32, lai=20, lbi=20, pi=1, ki=1, lwi=20)
+_sb(U16, uo=8, offs=180, l0o=20, l1o=20)
+_sb("float8_e4m3fn_x4", wq=512, qu=128, qup=128, qv=128, qe8=512, qe1=512, qz=320)
+_sb("uint8", wsq=512, su=128, sup=128, sv=128, se8=512, se1=512, sz=320)
+for _i in range(4):
+    SCRATCH["q%d" % _i] = ("sbuf", [128, C], "float8_e4m3fn_x4")
+    SCRATCH["s%d" % _i] = ("sbuf", [128, C], "uint8")
+for _i in range(3):
+    SCRATCH["lq%d" % _i] = ("sbuf", [128, C], "float8_e4m3fn_x4")
+    SCRATCH["lp%d" % _i] = ("sbuf", [128, C], "uint8")
+    for _k in ("ta", "tb", "tc", "la_", "lb_", "lc_"):
+        SCRATCH["%s%d" % (_k, _i)] = ("sbuf", [128, 20], U16)
+SCRATCH["psa"] = ("psum", [128, 2048], F32)
+SCRATCH["psf"] = ("psum", [128, 1536], F32)
+SCRATCH["pss"] = ("psum", [128, 512], F32)
+
+SEMAPHORES = ["cv", "cs", "ct", "cg", "left", "ldx", "ldy", "ldu", "ldv", "ldl", "ldw", "sto", "stc"]
+SEMAPHORES += ["%s%d" % (k, i) for k in ("aq", "at", "ab", "ac") for i in range(3)]
+
+
+def rank_program(g, core, T, topo):
+    rank = T.rank_of(core)
+    if rank is None:
+        return
+    N = len(T.cores)
+    A = AluOpType
+    COPY = ActivationFunctionType.Copy
+    eng = {"v": g.vector, "s": g.scalar, "t": g.tensor, "g": g, "y": g.sync}
+    cnt = {"v": 0, "s": 0, "t": 0, "g": 0}
+    seen = {}
+
+    def need(q, *toks):
+        most = {}
+        for name, n in toks:
+            most[name] = max(n, most.get(name, 0))
+        for name, n in most.items():
+            if seen.get((q, name), 0) < n:
+                eng[q].wait_ge(T.sem[name], n)
+                seen[(q, name)] = n
+
+    def run(q, deps, fn, *a, **kw):
+        need(q, *deps)
+        ins = fn(*a, **kw)
+        cnt[q] += 1
+        ins.then_inc(T.sem["c" + q], 1)
+        return ("c" + q, cnt[q])
+
+    V, S, TE = g.vector, g.scalar, g.tensor
+
+    def w20(buf):
+        return buf[:, 15:C:16]
+
+    def blk(buf, b):
+        return buf[:, C * b:C * b + C]
+
+    def mov(buf, b):
+        return buf[:, 128 * b:128 * b + 128]
+
+    g.sync.dma_start(T.xin[:, 0:640], T.x[:, 0:640]).then_inc(T.sem.ldx, 16)
+    g.scalar.dma_start(T.uin[:], T.u[:, :]).then_inc(T.sem.ldu, 16)
+    g.scalar.dma_start(T.xin[:, 640:1280], T.x[:, 640:1280]).then_inc(T.sem.ldy, 16)
+    g.sync.dma_start(T.lai[:], T.la[:, :]).then_inc(T.sem.ldl, 16)
+    g.sync.dma_start(T.lbi[:], T.lb[:, :]).then_inc(T.sem.ldl, 16)
+    need("y", ("ldx", 16), ("ldy", 16))
+    g.sync.dma_start(T.wq[:, 0:512].bitcast(dt.uint8), T.wc[:, :]).then_inc(T.sem.ldw, 16)
+    g.sync.dma_start(T.wsq[:, 0:512], T.ws[:, :]).then_inc(T.sem.ldw, 16)
+    g.sync.dma_start(T.vin[:], T.v[:, :]).then_inc(T.sem.ldv, 16)
+
+    SMALL = {"allow_small_or_imprecise_dtypes": True}
+    k_m16 = run("g", [], g.iota, T.m16[:], [[16, 20]], 0, 0, **SMALL)
+    k_pi = run("g", [], g.iota, T.pi[:], [[0, 1]], 0, 1)
+    k_tp = run("g", [], g.iota, T.tpos[:], [[0, 20], [1, 16]], 0, 0, **SMALL)
+    k_dj = run("g", [], g.iota, T.dj[:], [[1, 128]], 0, -1, **SMALL)
+    k_io = run("g", [], g.iota, T.iot[:], [[1, C]], -160, 0, **SMALL)
+
+    m8 = run("v", [], V.memset, T.e8[:], 0.0)
+    uo = run("v", [k_m16], V.tensor_copy, T.uo[:], T.m16[:, 0:8])
+    ki = run("v", [k_pi], V.tensor_scalar, T.ki[:], T.pi[:], 15, None, A.bitwise_and)
+    kf = run("v", [ki], V.tensor_copy, T.kf[:], T.ki[:])
+    k1 = run("v", [kf], V.tensor_scalar, T.k1[:], T.kf[:], 1.0, None, A.add)
+    a = run("v", [kf], V.tensor_scalar, T.scl[:], T.kf[:], 15.0, 1.0 - 2.0 ** -15, A.is_equal, A.mult)
+    b = run("v", [kf], V.tensor_scalar, T.inv[:], T.kf[:], 15.0, 1.0 - 2.0 ** 15, A.is_equal, A.mult)
+    sc = run("v", [a], V.tensor_scalar, T.scl[:], T.scl[:], 2.0 ** -15, None, A.add)
+    b = run("v", [b], V.tensor_scalar, T.inv[:], T.inv[:], 2.0 ** 15, None, A.add)
+    n0 = run("v", [k_tp, kf], V.tensor_scalar, T.n0[:], T.tpos[:], T.kf[:, 0:1], None, A.not_equal)
+    n1 = run("v", [k_tp, k1], V.tensor_scalar, T.n1[:], T.tpos[:], T.k1[:, 0:1], 2.0 ** 15, A.is_equal, A.mult)
+    cw = run("v", [k_m16, kf], V.tensor_scalar, T.cw[:], T.m16[:], T.kf[:, 0:1], None, A.add)
+    cb = run("v", [k_m16, kf], V.tensor_scalar, T.cb[:], T.m16[:], T.kf[:, 0:1], 0.25, A.add, A.add)
+    kk = run("v", [n0, n1], V.tensor_tensor, T.kk[:], T.n0[:], T.n1[:], A.max)
+    d8 = run("v", [k_dj, m8], V.tensor_scalar, T.e8[:, 3:515:4], T.dj[:], 0.0, 0.125, A.is_equal, A.mult)
+    run("v", [sc], V.tensor_scalar, T.scm[:], T.scl[:], -2.0, None, A.mult)
+    run("v", [b], V.tensor_scalar, T.thr[:], T.inv[:], 0.5, None, A.mult)
+
+    a = run("v", [("ldu", 16)], V.quantize_mx, T.qu[:, 0:128], T.su[:, 0:128], T.uin[:])
+    qup = run("v", [a, uo], V.tensor_copy, T.qup[:, 0:128].bitcast(dt.uint32), T.qu[:, 0:128].bitcast(dt.uint32).indirect(T.uo[:, 0:8]))
+    qus = run("s", [a, uo], S.activation, T.sup[:, 0:128], T.su[:, 0:128].indirect(T.uo[:, 0:8]), COPY)
+
+    def quant(tile, i, deps):
+        return [run("v", deps[h], V.quantize_mx, T["q%d" % i][:, H * h:H * h + H], T["s%d" % i][:, H * h:H * h + H],
+                    tile[:, 4 * H * h:4 * H * h + 4 * H]) for h in (0, 1)]
+
+    tq = quant(T.xin, 0, [[("ldx", 16)], [("ldy", 16)]])
+    l0 = run("v", [("ldl", 32)], V.tensor_scalar, T.l0w[:], T.lai[:], 0.25, None, A.add)
+    l1 = run("v", [("ldl", 32)], V.tensor_scalar, T.l1w[:], T.lbi[:], 0.25, None, A.add)
+    a = run("v", [l0, l1], V.tensor_tensor, T.dw[:], T.l1w[:], T.l0w[:], A.subtract)
+    ss = run("v", [l0, l1], V.tensor_tensor, T.ss[:], T.l1w[:], T.l0w[:], A.add)
+    dw = run("v", [a, sc], V.tensor_scalar, T.dw[:], T.dw[:], T.scl[:, 0:1], None, A.mult)
+
+    def scan(src, deps):
+        return run("v", list(deps) + [kk, ("cv", cnt["v"])], V.tensor_tensor_scan, T.sca[:], T.kk[:], src, 0.0, A.mult, A.add)
+
+    def conv(src, dep, out):
+        a = scan(src, [dep])
+        return run("v", [a, sc], V.tensor_scalar, out, w20(T.sca), T.scl[:, 0:1], 160.25, A.mult, A.add)
+
+    def off(k):
+        return T.offs[:, 20 * k:20 * k + 20]
+
+    left = 0
+    for i, d in enumerate(STEP):
+        q, s = T["q%d" % i], T["s%d" % i]
+        lq, lp = T["lq%d" % i], T["lp%d" % i]
+        ta, tb, tc = [T["%s%d" % (k, i)] for k in ("ta", "tb", "tc")]
+        la, lb, lc = [T["%s%d" % (k, i)] for k in ("la_", "lb_", "lc_")]
+        dst = T.cores[(rank + d) % N]
+        src = T.cores[(rank - d) % N]
+        rid, pid, _ = topo.addr(dst)
+        mask = topo.mask(core, dst)
+        ne, na = len(topo.engines(core, dst)), len(topo.engines(src, core))
+
+        def send(out, in_, sem, dep):
+            need("g", dep)
+            g.remote_dma(out, in_, T.sem["%s%d" % (sem, i)], T.sem.left, pid, rid, mask)
+
+        send(lq[:, 0:C].bitcast(dt.uint8), q[:, 0:C].bitcast(dt.uint8), "aq", tq[1])
+        send(lp[:, 0:C], s[:, 0:C], "aq", tq[1])
+        if i == 0:
+            k_if = run("g", [], g.iota, T.iof[:], [[1, C]], 0, 0, **SMALL)
+
+        sbank = [T.pss[:, 0:H], T.psf[:, 0:H]]
+        ts = [run("t", [tq[h], qup, qus], TE.matmul_mx, sbank[h], T.qup[:, 0:128], T.sup[:, 0:128],
+                  q[:, H * h:H * h + H], s[:, H * h:H * h + H], True, True) for h in (0, 1)]
+        m = []
+        for h in (0, 1):
+            half = slice(H * h, H * h + H)
+            m.append(run("v", [ts[h]], V.tensor_scalar, T.mm[:, half], sbank[h], 0.0, None, A.is_lt))
+            if i and h:
+                dw = run("v", [eg], V.tensor_tensor, T.dw[:], T.dw[:], T.eg[:], A.add)
+            a = run("v", [m[h], kk], V.tensor_tensor_scan, T.sca[:, half], T.kk[:, half], T.mm[:, half], 0.0, A.mult, A.add)
+        a = run("v", [a, dw], V.tensor_tensor, T.tp[:], w20(T.sca), T.dw[:], A.mult)
+        pw = run("v", [a, l0], V.tensor_tensor, T.pw[:], T.tp[:], T.l0w[:], A.add)
+        o = run("v", [pw], V.tensor_copy, off(0), T.pw[:])
+        sf = [run("s", [m[h]], S.activation, T.sf[:, H * h:H * h + H], sbank[h], COPY) for h in (0, 1)]
+        dcp = run("v", [pw, cb], V.tensor_tensor, T.dcp[:], T.cb[:], T.pw[:], A.subtract)
+
+        ak = run("s", [o, k_io], S.activation, blk(T.aw, 0), T.iot[:, 0:C].indirect(off(0)), COPY)
+        low, lowt = blk(T.aw, 0), ak
+        dup = run("v", [o, k_io], V.tensor_copy, blk(T.ld, 0), T.iot[:, 0:C].indirect(off(0)))
+        if i == 0:
+            qe8 = [run("v", [d8], V.quantize_mx, mov(T.qe8, b), mov(T.se8, b), T.e8[:, 3 - b:515 - b]) for b in range(4)][3]
+        for k in range(7):
+            an = run("s", [ak, o], S.activation, blk(T.aw, k + 1), blk(T.aw, k).indirect(off(k)), COPY)
+            lowt = run("v", [lowt, o, ak, dup], V.tensor_tensor, blk(T.low, k), low.indirect(off(k)), blk(T.ld, k), A.min)
+            low = blk(T.low, k)
+            dup = run("s", [lowt], S.activation, blk(T.ld, k + 1), low, COPY)
+            o = conv(blk(T.aw, k + 1), an, off(k + 1))
+            ak = an
+        lowt = run("v", [lowt, o, dup], V.tensor_tensor, blk(T.low, 7), low.indirect(off(7)), blk(T.ld, 7), A.min)
+        low = blk(T.low, 7)
+        lowt = run("v", [lowt], V.tensor_tensor, blk(T.low, 8), low.indirect(off(6)), blk(T.ld, 7), A.min)
+        low = blk(T.low, 8)
+        a = conv(low, lowt, T.lwi[:])
+        a = run("v", [a, cw], V.tensor_tensor, T.ew[:], T.lwi[:], T.cw[:], A.is_equal)
+        a = run("v", [a, dcp], V.tensor_tensor, T.ed[:], T.ew[:], T.dcp[:], A.mult)
+        a = run("v", [a], V.tensor_tensor, T.tw[:], T.ed[:], T.pw[:], A.add)
+        tt = run("v", [a], V.tensor_copy, ta[:, 0:20], T.tw[:])
+        send(la[:, 0:20], ta[:, 0:20], "at", tt)
+
+        f8 = [run("t", [("aq%d" % i, 2 * na), qe8, sf[1]], TE.matmul_mx, T.psa[:, 512 * b:512 * b + C], mov(T.qe8, b), mov(T.se8, b),
+                  lq[:, 0:C], lp[:, 0:C], True, True) for b in range(4)]
+        fw = []
+        for b in range(4):
+            if b == 3:
+                b1 = run("s", [lowt], S.activation, blk(T.bw, 0), low.indirect(off(7)), COPY)
+            fw.append(run("s", [f8[b]], S.activation, blk(T.fw, b), T.psa[:, 512 * b:512 * b + C], COPY))
+
+        t1 = run("s", [tt], S.activation, blk(T.tf, 0), T.iot[:, 0:C].indirect(ta[:, 0:20]), COPY)
+        t2 = run("s", [t1], S.activation, blk(T.tf, 1), blk(T.tf, 0).indirect(ta[:, 0:20]), COPY)
+        b2 = run("v", [b1], V.tensor_copy, blk(T.bw, 1), blk(T.bw, 0).indirect(off(7)))
+        b3 = run("v", [b2], V.tensor_copy, blk(T.bw, 2), blk(T.bw, 1).indirect(off(6)))
+        o2 = conv(blk(T.tf, 1), t2, tb[:, 0:20])
+        send(lb[:, 0:20], tb[:, 0:20], "ab", o2)
+        t4 = run("s", [t2, o2], S.activation, blk(T.tf, 2), blk(T.tf, 1).indirect(tb[:, 0:20]), COPY)
+        ro = conv(blk(T.bw, 2), b3, off(8))
+        fd = [run("v", [fw[b]], V.tensor_copy, blk(T.fd, b), blk(T.fw, b)) for b in (0, 1)]
+        sg = run("s", [ro, sf[1]], S.activation, T.sg[:], T.sf[:, 0:C].indirect(off(8)), COPY)
+        o4 = conv(blk(T.tf, 2), t4, tc[:, 0:20])
+        send(lc[:, 0:20], tc[:, 0:20], "ac", o4)
+        left += 5 * ne
+        if i == 0:
+            qv = run("v", [("ldv", 16)], V.quantize_mx, T.qv[:, 0:128], T.sv[:, 0:128], T.vin[:])
+
+        at, ab, ac = [("%s%d" % (k, i), na) for k in ("at", "ab", "ac")]
+        zs = [run("s", [at, fw[b]], S.activation, blk(T.tmp, b - 2), blk(T.fw, b).indirect(la[:, 0:20]), COPY) for b in (2, 3)]
+        z1 = [run("v", [at, fw[b], fd[b]], V.tensor_tensor, blk(T.z1, b), blk(T.fw, b).indirect(la[:, 0:20]), blk(T.fd, b), A.add) for b in (0, 1)]
+        z1 += [run("v", [zs[b - 2]], V.tensor_tensor, blk(T.z1, b), blk(T.tmp, b - 2), T.psa[:, 512 * b:512 * b + C], A.add) for b in (2, 3)]
+        d1 = [run("s", [z1[b]], S.activation, blk(T.d1, b), blk(T.z1, b), COPY) for b in range(4)]
+        z2 = [run("v", [ab, z1[b], d1[b]], V.tensor_tensor, blk(T.z2, b), blk(T.z1, b).indirect(lb[:, 0:20]), blk(T.d1, b), A.add) for b in range(4)]
+        d2 = [run("s", [z2[b]], S.activation, blk(T.d2, b), blk(T.z2, b), COPY) for b in range(4)]
+        z3 = [run("v", [ac, z2[b], d2[b]], V.tensor_tensor, T.z3[:, b:1280:4], blk(T.z2, b).indirect(lc[:, 0:20]), blk(T.d2, b), A.add) for b in range(4)]
+        tz = [run("v", z3, V.quantize_mx, T.qz[:, H * h:H * h + H], T.sz[:, H * h:H * h + H], T.z3[:, 4 * H * h:4 * H * h + 4 * H]) for h in (0, 1)]
+
+        fbank = [T.psf[:, 512:512 + C], T.psf[:, 1024:1024 + C]]
+        ff, fo = [], []
+        for b in range(4):
+            ff.append(run("t", [qe8] + fo[b - 2:b - 1], TE.matmul_mx, fbank[b % 2], mov(T.qe8, b), mov(T.se8, b), q[:, 0:C], s[:, 0:C], True, True))
+            fo.append(run("s", [ff[b]], S.activation, blk(T.fo, b), fbank[b % 2], COPY, scale=8.0))
+
+        hbank = [T.psa[:, 0:H], T.psf[:, 512:512 + H]]
+        hh = [run("t", [tz[h], ("ldw", 32), fw[3], fo[2]], TE.matmul_mx, hbank[h], mov(T.wq, 0), mov(T.wsq, 0),
+                  T.qz[:, H * h:H * h + H], T.sz[:, H * h:H * h + H], True, True) for h in (0, 1)]
+        hh += [run("t", [tz[1]], TE.matmul_mx, T.psa[:, 512 * b:512 * b + C], mov(T.wq, b), mov(T.wsq, b),
+                   T.qz[:, 0:C], T.sz[:, 0:C], True, True) for b in (1, 2, 3)]
+        hw = [run("s", [hh[h]], S.activation, T.hw[:, H * h:H * h + H], hbank[h], COPY, scale=0.03125) for h in (0, 1)][1:]
+        hw += [run("s", [hh[b + 1]], S.activation, blk(T.hw, b), T.psa[:, 512 * b:512 * b + C], COPY, scale=0.03125) for b in (1, 2, 3)]
+
+        a = [run("v", [sg], V.tensor_tensor, T.fl[:, H * h:H * h + H], T.sg[:, H * h:H * h + H], sbank[h], A.is_gt) for h in (0, 1)]
+        a = scan(T.fl[:], a)
+        e = run("v", [a], V.tensor_scalar, T.ew[:], w20(T.sca), T.thr[:, 0:1], T.inv[:, 0:1], A.is_gt, A.mult)
+
+        tx = []
+        for b in range(4):
+            tx.append(run("v", [hw[b], fo[b], tt], V.tensor_tensor, T.xt[:, b:1280:4], blk(T.hw, b).indirect(ta[:, 0:20]), blk(T.fo, b), A.add))
+            if i == 2 and b == 0:
+                e = run("v", [e], V.tensor_tensor, T.ed[:], T.ew[:], T.dw[:], A.mult)
+            if i == 2 and b == 1:
+                l0 = run("v", [e], V.tensor_tensor, T.l0w[:], T.l0w[:], T.ed[:], A.add)
+            if i == 2 and b == 2:
+                l1 = run("v", [l0, ss], V.tensor_tensor, T.l1w[:], T.ss[:], T.l0w[:], A.subtract)
+                l0 = run("v", [l0], V.tensor_copy, T.l0o[:], T.l0w[:])
+                l1 = run("v", [l1], V.tensor_copy, T.l1o[:], T.l1w[:])
+                lsd = [run("s", [k_if, t], S.activation, T.lsf[:, C * h:C * h + C], T.iof[:, 0:C].indirect(o[:, 0:20]), COPY)
+                       for h, t, o in ((0, l0, T.l0o), (1, l1, T.l1o))]
+        tq = quant(T.xt, i + 1, [tx, tx])
+        if i < 2:
+            e = run("v", [e], V.tensor_tensor, T.ed[:], T.ew[:], T.dw[:], A.mult)
+            l0 = run("v", [e], V.tensor_tensor, T.l0w[:], T.l0w[:], T.ed[:], A.add)
+            eg = run("v", [e], V.tensor_scalar, T.eg[:], T.ed[:], T.scm[:, 0:1], None, A.mult)
+
+    need("y", *lsd)
+    g.sync.dma_start(T.ls[:, :], T.lsf[0:128:16, :]).then_inc(T.sem.sto, 16)
+    need("y", *tq)
+    g.sync.dma_start(T.oc[:, :], T.q3[:, 0:C].bitcast(dt.uint8)).then_inc(T.sem.sto, 16)
+    yy = [run("t", [tq[h], qv, hw[3]], TE.matmul_mx, T.psa[:, 512 * h:512 * h + H], T.qv[:, 0:128], T.sv[:, 0:128],
+              T.q3[:, H * h:H * h + H], T.s3[:, H * h:H * h + H], True, True) for h in (0, 1)]
+    ya = run("v", [yy[0]], V.tensor_copy, T.yf[:, 0:H], T.psa[:, 0:H])
+    yb = run("s", [yy[1]], S.activation, T.yf[:, H:C], T.psa[:, 512:512 + H], COPY)
+    need("y", ya)
+    g.sync.dma_start(T.y[:, 0:H], T.yf[:, 0:H]).then_inc(T.sem.sto, 16)
+    need("s", yb)
+    g.scalar.dma_start(T.y[:, H:C], T.yf[:, H:C]).then_inc(T.sem.stc, 16)
+    for k in range(4):
+        g.sync.dma_start(T.osc[4 * k:4 * k + 4, :], T.s3[32 * k:32 * k + 4, 0:C]).then_inc(T.sem.sto, 16)
+    need("g", ("cv", cnt["v"]), ("cs", cnt["s"]), ("ct", cnt["t"]), ("cg", cnt["g"]), ("left", left), ("sto", 112), ("stc", 16))

@@ -1,9 +1,20 @@
 from concourse.mybir import dt, AluOpType, ActivationFunctionType
 
 C = 320
-H = 160
+W = 2 * C
+CUT = 192
+PART = {"": (0, C), "a": (0, CUT), "b": (CUT, C)}
+RADIX = [3, 3, 3, 3, 2]
 STEP = [1, 2, 4]
+BIG = 2.0 ** 24
+MID = 159
 BF, F32, I32, U16 = "bfloat16", "float32", "int32", "uint16"
+
+ORDER = dict(v="lw g1 w2 d1 g2 sb pb fl sc a0 pc a2 a1 a3 sx b0 b1 c0 c1a c1b za zb ex e1 qv e2 h0b e3 x0 e4 e5 x1 e6 e7 x2 x3a x3b ya yb",
+             s="w1 w0 w3 t1 t2 t3 t4 u2 u3 A0 A1 o0 B0 B1 o1 o2 o3 h0a h1 h2 h3 l0 l1",
+             t="F1 F0 F3 F2 O0 O1 O2 O3 H0a H0b H1 H2 H3",
+             g=">a d0 >b >c")
+DV = 112
 
 SCRATCH = {}
 
@@ -13,23 +24,23 @@ def _sb(dtype, **kw):
         SCRATCH[k] = ("sbuf", [128, n], dtype)
 
 
-_sb(BF, xin=1280, uin=512, vin=512, e8=516, e1=516, iot=320, tpos=320, n0=320, n1=320, kk=320, sca=320, mm=320,
-    aw=320 * 8, low=320 * 9, tf=960, bw=960, fw=1280, fo=1280, hw=1280, z1=1280, z2=1280, z3=1280, xt=1280, tmp=640,
-    fl=320, ld=320 * 9, fd=640, d1=1280, d2=1280)
-_sb(F32, iof=320, dj=128, m16=20, kf=1, k1=1, scl=1, scm=1, thr=1, inv=1, cw=20, cb=20, sf=320, l0w=20, l1w=20,
-    dw=20, ss=20, sg=320, tp=20, pw=20, dcp=20, ew=20, ed=20, eg=20, tw=20, lsf=640, yf=320)
-_sb(I32, lai=20, lbi=20, pi=1, ki=1, lwi=20)
-_sb(U16, uo=8, offs=180, l0o=20, l1o=20)
-_sb("float8_e4m3fn_x4", wq=512, qu=128, qup=128, qv=128, qe8=512, qe1=512, qz=320)
-_sb("uint8", wsq=512, su=128, sup=128, sv=128, se8=512, se1=512, sz=320)
+_sb(BF, xin=1280, uin=512, vin=512, e8=516, iot=C, kd=128, ke=128, kk=C, kp=C, sca=C, scb=C, scc=C, scd=C, mm=C,
+    aw=3 * C, low=2 * C, ld=C, t1=C, t2=C, t4=C, fw=1280, fd=W, fo=1280, hw=1280, tmp=W, z1=1280, z2=1280,
+    d1=1280, d2=1280, z3=1280, xt=1280, fl=C)
+_sb(F32, iof=C, dj=128, m16=20, kf=1, scl=1, thr=1, sc2=1, b2=1, tiny=1, cw=20, cx=20, sf=C, l0w=20, l1w=20,
+    sg=2 * C, sa=40, sb=40, so=40, ex=20, lsf=2 * C, yf=C, ed=20, dw=20, mid=20, tp=20)
+_sb(I32, lai=20, lbi=20, pi=20, ki=3)
+_sb(U16, uo=8, ko=20, offs=20 * len(RADIX) + 20, lwo=20, l0o=20, l1o=20)
+_sb("float8_e4m3fn_x4", wq=512, qu=128, qup=128, qv=128, qe8=512, qz=C)
+_sb("uint8", wsq=512, su=128, sup=128, sv=128, se8=512, sz=C)
 for _i in range(4):
     SCRATCH["q%d" % _i] = ("sbuf", [128, C], "float8_e4m3fn_x4")
     SCRATCH["s%d" % _i] = ("sbuf", [128, C], "uint8")
 for _i in range(3):
     SCRATCH["lq%d" % _i] = ("sbuf", [128, C], "float8_e4m3fn_x4")
     SCRATCH["lp%d" % _i] = ("sbuf", [128, C], "uint8")
-    for _k in ("ta", "tb", "tc", "la_", "lb_", "lc_"):
-        SCRATCH["%s%d" % (_k, _i)] = ("sbuf", [128, 20], U16)
+    for _k, _n in (("ta", 20), ("tb", 40), ("tc", 40), ("la_", 20), ("lb_", 40), ("lc_", 40)):
+        SCRATCH["%s%d" % (_k, _i)] = ("sbuf", [128, _n], U16)
 SCRATCH["psa"] = ("psum", [128, 2048], F32)
 SCRATCH["psf"] = ("psum", [128, 1536], F32)
 SCRATCH["pss"] = ("psum", [128, 512], F32)
@@ -44,7 +55,7 @@ def rank_program(g, core, T, topo):
         return
     N = len(T.cores)
     A = AluOpType
-    COPY = ActivationFunctionType.Copy
+    COPY, SIGN = ActivationFunctionType.Copy, ActivationFunctionType.Sign
     eng = {"v": g.vector, "s": g.scalar, "t": g.tensor, "g": g, "y": g.sync}
     cnt = {"v": 0, "s": 0, "t": 0, "g": 0}
     seen = {}
@@ -73,65 +84,92 @@ def rank_program(g, core, T, topo):
     def blk(buf, b):
         return buf[:, C * b:C * b + C]
 
+    def two(buf, k):
+        return buf[:, W * k:W * k + W]
+
+    def one(buf, b):
+        return buf[:, W * (b % 2) + b // 2:W * (b % 2) + W:2]
+
     def mov(buf, b):
         return buf[:, 128 * b:128 * b + 128]
 
-    g.sync.dma_start(T.xin[:, 0:640], T.x[:, 0:640]).then_inc(T.sem.ldx, 16)
+    def bank(buf, b, n=C):
+        return buf[:, 512 * b:512 * b + n]
+
+    def pick(q, deps, out, in_, scale=None):
+        if q == "g":
+            return run(q, deps, g.affine_select, out, in_, [[0, C]], A.is_equal, 0.0, 0, 0)
+        if scale is None:
+            return run(q, deps, V.tensor_copy, out, in_) if q == "v" else run(q, deps, S.activation, out, in_, COPY)
+        return run(q, deps, V.tensor_scalar, out, in_, scale, None, A.mult) if q == "v" else run(q, deps, S.activation, out, in_, COPY, scale=scale)
+
+    def mm(q, deps, out, side, plane, codes, scales, part):
+        lo, hi = PART[part]
+        return run(q, deps, TE.matmul_mx, out, side, plane, codes[:, lo:hi], scales[:, lo:hi], True, True)
+
+    def quant(q, deps, codes, plane, tile, part):
+        lo, hi = PART[part]
+        return run(q, deps, V.quantize_mx, codes[:, lo:hi], plane[:, lo:hi], tile[:, 4 * lo:4 * hi])
+
+    g.sync.dma_start(T.xin[:, 0:4 * CUT], T.x[:, 0:4 * CUT]).then_inc(T.sem.ldx, 16)
     g.scalar.dma_start(T.uin[:], T.u[:, :]).then_inc(T.sem.ldu, 16)
-    g.scalar.dma_start(T.xin[:, 640:1280], T.x[:, 640:1280]).then_inc(T.sem.ldy, 16)
+    g.scalar.dma_start(T.xin[:, 4 * CUT:1280], T.x[:, 4 * CUT:1280]).then_inc(T.sem.ldy, 16)
+    LX = [("ldx", 16), ("ldy", 16)]
     g.sync.dma_start(T.lai[:], T.la[:, :]).then_inc(T.sem.ldl, 16)
-    g.sync.dma_start(T.lbi[:], T.lb[:, :]).then_inc(T.sem.ldl, 16)
-    need("y", ("ldx", 16), ("ldy", 16))
+    g.scalar.dma_start(T.lbi[:], T.lb[:, :]).then_inc(T.sem.ldl, 16)
+    need("y", *LX)
     g.sync.dma_start(T.wq[:, 0:512].bitcast(dt.uint8), T.wc[:, :]).then_inc(T.sem.ldw, 16)
     g.sync.dma_start(T.wsq[:, 0:512], T.ws[:, :]).then_inc(T.sem.ldw, 16)
     g.sync.dma_start(T.vin[:], T.v[:, :]).then_inc(T.sem.ldv, 16)
 
     SMALL = {"allow_small_or_imprecise_dtypes": True}
+
+    def factors(buf, pattern, zero, big):
+        a = run("g", [], g.iota, buf[:], [[0, 128]], 1, 0, **SMALL)
+        for fill, at in [(0.0, k) for k in zero] + [(BIG, k) for k in big]:
+            a = run("g", [a], g.affine_select, buf[:], buf[:], pattern, A.not_equal, fill, -at, -1)
+        return a
+
+    k_pi = run("g", [], g.iota, T.pi[:], [[0, 20]], 0, 1)
     k_m16 = run("g", [], g.iota, T.m16[:], [[16, 20]], 0, 0, **SMALL)
-    k_pi = run("g", [], g.iota, T.pi[:], [[0, 1]], 0, 1)
-    k_tp = run("g", [], g.iota, T.tpos[:], [[0, 20], [1, 16]], 0, 0, **SMALL)
     k_dj = run("g", [], g.iota, T.dj[:], [[1, 128]], 0, -1, **SMALL)
-    k_io = run("g", [], g.iota, T.iot[:], [[1, C]], -160, 0, **SMALL)
+    kk = factors(T.kd, [[1, 128]], [0], [1])
+    k_io = run("g", [], g.iota, T.iot[:], [[1, C]], -MID, 0, **SMALL)
 
     m8 = run("v", [], V.memset, T.e8[:], 0.0)
+    ki = [run("v", [k_pi], V.tensor_scalar, T.ki[:, j:j + 1], T.pi[:, 0:1], bits, None, A.bitwise_and) for j, bits in enumerate((15, 14, 1))]
+    ko = run("v", [k_pi], V.tensor_copy, T.ko[:], T.pi[:])
     uo = run("v", [k_m16], V.tensor_copy, T.uo[:], T.m16[:, 0:8])
-    ki = run("v", [k_pi], V.tensor_scalar, T.ki[:], T.pi[:], 15, None, A.bitwise_and)
-    kf = run("v", [ki], V.tensor_copy, T.kf[:], T.ki[:])
-    k1 = run("v", [kf], V.tensor_scalar, T.k1[:], T.kf[:], 1.0, None, A.add)
-    a = run("v", [kf], V.tensor_scalar, T.scl[:], T.kf[:], 15.0, 1.0 - 2.0 ** -15, A.is_equal, A.mult)
-    b = run("v", [kf], V.tensor_scalar, T.inv[:], T.kf[:], 15.0, 1.0 - 2.0 ** 15, A.is_equal, A.mult)
-    sc = run("v", [a], V.tensor_scalar, T.scl[:], T.scl[:], 2.0 ** -15, None, A.add)
-    b = run("v", [b], V.tensor_scalar, T.inv[:], T.inv[:], 2.0 ** 15, None, A.add)
-    n0 = run("v", [k_tp, kf], V.tensor_scalar, T.n0[:], T.tpos[:], T.kf[:, 0:1], None, A.not_equal)
-    n1 = run("v", [k_tp, k1], V.tensor_scalar, T.n1[:], T.tpos[:], T.k1[:, 0:1], 2.0 ** 15, A.is_equal, A.mult)
+    tiny = run("v", [], V.memset, T.tiny[:], 2.0 ** -100)
+    run("v", [], V.memset, T.sa[:], 0.0)
+    kf = run("v", ki, V.tensor_copy, T.kf[:], T.ki[:, 0:1])
+    run("v", ki, V.tensor_scalar, T.b2[:], T.ki[:, 2:3], 2 * MID + 0.25, None, A.add)
+    last = [(T.scl, 0, 15.0, 1.0, 1 / BIG), (T.sc2, 1, 14.0, 2.0, 2 / BIG), (T.thr, 0, 15.0, 0.5, BIG / 2)]
+    a = [run("v", ki, V.tensor_scalar, buf[:], T.ki[:, j:j + 1], at, x - y, A.is_equal, A.mult) for buf, j, at, x, y in last]
     cw = run("v", [k_m16, kf], V.tensor_scalar, T.cw[:], T.m16[:], T.kf[:, 0:1], None, A.add)
-    cb = run("v", [k_m16, kf], V.tensor_scalar, T.cb[:], T.m16[:], T.kf[:, 0:1], 0.25, A.add, A.add)
-    kk = run("v", [n0, n1], V.tensor_tensor, T.kk[:], T.n0[:], T.n1[:], A.max)
+    sc = [run("v", a, V.tensor_scalar, buf[:], buf[:], y, None, A.add) for buf, j, at, x, y in last][2]
     d8 = run("v", [k_dj, m8], V.tensor_scalar, T.e8[:, 3:515:4], T.dj[:], 0.0, 0.125, A.is_equal, A.mult)
-    run("v", [sc], V.tensor_scalar, T.scm[:], T.scl[:], -2.0, None, A.mult)
-    run("v", [b], V.tensor_scalar, T.thr[:], T.inv[:], 0.5, None, A.mult)
+    a = run("v", [cw, sc], V.tensor_scalar, T.cx[:], T.cw[:], float(MID), T.thr[:, 0:1], A.subtract, A.mult)
+    run("v", [a], V.tensor_scalar, T.cx[:], T.cx[:], 2.0, None, A.mult)
+    kk = pick("s", [kk, ko], T.kk[:], T.kd[:, 0:128].indirect(T.ko[:, 0:20]))
+
+    def unpacker(b):
+        return run("v", [d8], V.quantize_mx, mov(T.qe8, b), mov(T.se8, b), T.e8[:, 3 - b:515 - b])
 
     a = run("v", [("ldu", 16)], V.quantize_mx, T.qu[:, 0:128], T.su[:, 0:128], T.uin[:])
+    unpacker(0)
     qup = run("v", [a, uo], V.tensor_copy, T.qup[:, 0:128].bitcast(dt.uint32), T.qu[:, 0:128].bitcast(dt.uint32).indirect(T.uo[:, 0:8]))
     qus = run("s", [a, uo], S.activation, T.sup[:, 0:128], T.su[:, 0:128].indirect(T.uo[:, 0:8]), COPY)
-
-    def quant(tile, i, deps):
-        return [run("v", deps[h], V.quantize_mx, T["q%d" % i][:, H * h:H * h + H], T["s%d" % i][:, H * h:H * h + H],
-                    tile[:, 4 * H * h:4 * H * h + 4 * H]) for h in (0, 1)]
-
-    tq = quant(T.xin, 0, [[("ldx", 16)], [("ldy", 16)]])
-    l0 = run("v", [("ldl", 32)], V.tensor_scalar, T.l0w[:], T.lai[:], 0.25, None, A.add)
-    l1 = run("v", [("ldl", 32)], V.tensor_scalar, T.l1w[:], T.lbi[:], 0.25, None, A.add)
-    a = run("v", [l0, l1], V.tensor_tensor, T.dw[:], T.l1w[:], T.l0w[:], A.subtract)
-    ss = run("v", [l0, l1], V.tensor_tensor, T.ss[:], T.l1w[:], T.l0w[:], A.add)
-    dw = run("v", [a, sc], V.tensor_scalar, T.dw[:], T.dw[:], T.scl[:, 0:1], None, A.mult)
-
-    def scan(src, deps):
-        return run("v", list(deps) + [kk, ("cv", cnt["v"])], V.tensor_tensor_scan, T.sca[:], T.kk[:], src, 0.0, A.mult, A.add)
-
-    def conv(src, dep, out):
-        a = scan(src, [dep])
-        return run("v", [a, sc], V.tensor_scalar, out, w20(T.sca), T.scl[:, 0:1], 160.25, A.mult, A.add)
+    unpacker(1)
+    tq = [quant("v", [LX[h]], T.q0, T.s0, T.xin, "ab"[h]) for h in (0, 1)]
+    DW, DWA, MIDL, P = T.dw[:], T.dw[:, 0:CUT // 16], T.mid[:], T.sb[:, 1:40:2]
+    a = run("v", [("ldl", 32)], V.tensor_tensor, DW, T.lai[:], T.lbi[:], A.subtract)
+    b = run("v", [("ldl", 32)], V.tensor_tensor, MIDL, T.lai[:], T.lbi[:], A.add)
+    unpacker(2)
+    a = run("v", [a], V.tensor_scalar, DW, DW, T.scl[:, 0:1], None, A.mult)
+    run("v", [b], V.tensor_scalar, MIDL, MIDL, 0.5, 0.25, A.mult, A.add)
+    qe8 = unpacker(3)
+    dw = run("v", [a], V.tensor_scalar, DWA, DWA, 0.5, None, A.mult)
 
     def off(k):
         return T.offs[:, 20 * k:20 * k + 20]
@@ -148,137 +186,142 @@ def rank_program(g, core, T, topo):
         mask = topo.mask(core, dst)
         ne, na = len(topo.engines(core, dst)), len(topo.engines(src, core))
 
-        def send(out, in_, sem, dep):
+        def send(dep, out, in_, sem):
             need("g", dep)
             g.remote_dma(out, in_, T.sem["%s%d" % (sem, i)], T.sem.left, pid, rid, mask)
 
-        send(lq[:, 0:C].bitcast(dt.uint8), q[:, 0:C].bitcast(dt.uint8), "aq", tq[1])
-        send(lp[:, 0:C], s[:, 0:C], "aq", tq[1])
+        send(tq[1], lq[:, 0:C].bitcast(dt.uint8), q[:, 0:C].bitcast(dt.uint8), "aq")
+        send(tq[1], lp[:, 0:C], s[:, 0:C], "aq")
         if i == 0:
+            kp = factors(T.ke, [[16, 8], [0, 2], [2, 8]], [0, -1], [1, 2])
             k_if = run("g", [], g.iota, T.iof[:], [[1, C]], 0, 0, **SMALL)
 
-        sbank = [T.pss[:, 0:H], T.psf[:, 0:H]]
-        ts = [run("t", [tq[h], qup, qus], TE.matmul_mx, sbank[h], T.qup[:, 0:128], T.sup[:, 0:128],
-                  q[:, H * h:H * h + H], s[:, H * h:H * h + H], True, True) for h in (0, 1)]
-        m = []
-        for h in (0, 1):
-            half = slice(H * h, H * h + H)
-            m.append(run("v", [ts[h]], V.tensor_scalar, T.mm[:, half], sbank[h], 0.0, None, A.is_lt))
-            if i and h:
-                dw = run("v", [eg], V.tensor_tensor, T.dw[:], T.dw[:], T.eg[:], A.add)
-            a = run("v", [m[h], kk], V.tensor_tensor_scan, T.sca[:, half], T.kk[:, half], T.mm[:, half], 0.0, A.mult, A.add)
-        a = run("v", [a, dw], V.tensor_tensor, T.tp[:], w20(T.sca), T.dw[:], A.mult)
-        pw = run("v", [a, l0], V.tensor_tensor, T.pw[:], T.tp[:], T.l0w[:], A.add)
-        o = run("v", [pw], V.tensor_copy, off(0), T.pw[:])
-        sf = [run("s", [m[h]], S.activation, T.sf[:, H * h:H * h + H], sbank[h], COPY) for h in (0, 1)]
-        dcp = run("v", [pw, cb], V.tensor_tensor, T.dcp[:], T.cb[:], T.pw[:], A.subtract)
+        sbank = [bank(T.pss, 0, CUT), bank(T.psf, 0, C - CUT)]
+        ts = [mm("t", [tq[h], qup, qus], sbank[h], T.qup[:, 0:128], T.sup[:, 0:128], q, s, "ab"[h]) for h in (0, 1)]
+        m = [run("s", [ts[0], tiny], S.activation, T.mm[:, 0:CUT], sbank[0], SIGN, bias=T.tiny[:, 0:1]),
+             run("v", [ts[1]], V.tensor_scalar, T.mm[:, CUT:C], sbank[1], 0.0, 0.5, A.is_ge, A.subtract)]
+        a = [run("v", [m[h], kk], V.tensor_tensor_scan, T.sca[:, lo:hi], T.kk[:, lo:hi], T.mm[:, lo:hi], 0.0, A.mult, A.add)
+             for h, (lo, hi) in enumerate((PART["a"], PART["b"]))][1]
+        a = run("v", [a, dw], V.tensor_tensor, T.tp[:], w20(T.sca), DW, A.mult)
+        a = run("v", [a], V.tensor_tensor, P, T.tp[:], MIDL, A.add)
+        o = pick("v", [a], off(0), P)
+        sf = [pick("s", [m[h]], T.sf[:, PART["ab"[h]][0]:PART["ab"[h]][1]], sbank[h]) for h in (0, 1)][1]
 
-        ak = run("s", [o, k_io], S.activation, blk(T.aw, 0), T.iot[:, 0:C].indirect(off(0)), COPY)
-        low, lowt = blk(T.aw, 0), ak
-        dup = run("v", [o, k_io], V.tensor_copy, blk(T.ld, 0), T.iot[:, 0:C].indirect(off(0)))
+        ak = pick("s", [o, k_io], blk(T.aw, 0), T.iot[:, 0:C].indirect(off(0)))
+        dup = pick("v", [o, k_io], T.ld[:], T.iot[:, 0:C].indirect(off(0)))
+        run("v", [], V.tensor_tensor, T.sa[:, 1:40:2], T.cw[:], P, A.subtract)
+        low, lowt, n = blk(T.aw, 0), ak, 0
+        for k, r in enumerate(RADIX):
+            for j in range(r - 1):
+                ak = pick("s", [ak, o], blk(T.aw, (n + 1) % 3), blk(T.aw, n % 3).indirect(off(k)))
+                lowt = run("v", [lowt, o, dup], V.tensor_tensor, blk(T.low, n % 2), low.indirect(off(k)), T.ld[:], A.min)
+                low, at, n = blk(T.low, n % 2), C * (n % 2), n + 1
+            dup = pick("s", [lowt], T.ld[:, DV:C], T.low[:, at + DV:at + C])
+            a = run("v", [ak, kk], V.tensor_tensor_scan, T.sca[:], T.kk[:], blk(T.aw, n % 3), 0.0, A.mult, A.add)
+            pick("v", [lowt], T.ld[:, 0:DV], T.low[:, at:at + DV])
+            o = run("v", [a], V.tensor_scalar, off(k + 1), w20(T.sca), T.scl[:, 0:1], MID + 0.25, A.mult, A.add)
+        far = off(len(RADIX))
+        lowt = run("v", [lowt, o, dup], V.tensor_tensor, blk(T.low, n % 2), low.indirect(far), T.ld[:], A.min)
+        a = run("v", [lowt], V.tensor_tensor_scan, T.sca[:], T.kk[:], blk(T.low, n % 2), 0.0, A.mult, A.add)
+        a = run("v", [a], V.tensor_tensor, T.sb[:, 0:40:2], w20(T.sca), T.cx[:], A.is_equal)
+        a = run("v", [a], V.tensor_tensor_scan, T.so[:], T.sa[:], T.sb[:], 0.0, A.mult, A.add)
+        tt = run("v", [a], V.tensor_scalar, ta[:, 0:20], T.so[:, 1:40:2], 0.125, None, A.add)
         if i == 0:
-            qe8 = [run("v", [d8], V.quantize_mx, mov(T.qe8, b), mov(T.se8, b), T.e8[:, 3 - b:515 - b]) for b in range(4)][3]
-        for k in range(7):
-            an = run("s", [ak, o], S.activation, blk(T.aw, k + 1), blk(T.aw, k).indirect(off(k)), COPY)
-            lowt = run("v", [lowt, o, ak, dup], V.tensor_tensor, blk(T.low, k), low.indirect(off(k)), blk(T.ld, k), A.min)
-            low = blk(T.low, k)
-            dup = run("s", [lowt], S.activation, blk(T.ld, k + 1), low, COPY)
-            o = conv(blk(T.aw, k + 1), an, off(k + 1))
-            ak = an
-        lowt = run("v", [lowt, o, dup], V.tensor_tensor, blk(T.low, 7), low.indirect(off(7)), blk(T.ld, 7), A.min)
-        low = blk(T.low, 7)
-        lowt = run("v", [lowt], V.tensor_tensor, blk(T.low, 8), low.indirect(off(6)), blk(T.ld, 7), A.min)
-        low = blk(T.low, 8)
-        a = conv(low, lowt, T.lwi[:])
-        a = run("v", [a, cw], V.tensor_tensor, T.ew[:], T.lwi[:], T.cw[:], A.is_equal)
-        a = run("v", [a, dcp], V.tensor_tensor, T.ed[:], T.ew[:], T.dcp[:], A.mult)
-        a = run("v", [a], V.tensor_tensor, T.tw[:], T.ed[:], T.pw[:], A.add)
-        tt = run("v", [a], V.tensor_copy, ta[:, 0:20], T.tw[:])
-        send(la[:, 0:20], ta[:, 0:20], "at", tt)
-
-        f8 = [run("t", [("aq%d" % i, 2 * na), qe8, sf[1]], TE.matmul_mx, T.psa[:, 512 * b:512 * b + C], mov(T.qe8, b), mov(T.se8, b),
-                  lq[:, 0:C], lp[:, 0:C], True, True) for b in range(4)]
-        fw = []
-        for b in range(4):
-            if b == 3:
-                b1 = run("s", [lowt], S.activation, blk(T.bw, 0), low.indirect(off(7)), COPY)
-            fw.append(run("s", [f8[b]], S.activation, blk(T.fw, b), T.psa[:, 512 * b:512 * b + C], COPY))
-
-        t1 = run("s", [tt], S.activation, blk(T.tf, 0), T.iot[:, 0:C].indirect(ta[:, 0:20]), COPY)
-        t2 = run("s", [t1], S.activation, blk(T.tf, 1), blk(T.tf, 0).indirect(ta[:, 0:20]), COPY)
-        b2 = run("v", [b1], V.tensor_copy, blk(T.bw, 1), blk(T.bw, 0).indirect(off(7)))
-        b3 = run("v", [b2], V.tensor_copy, blk(T.bw, 2), blk(T.bw, 1).indirect(off(6)))
-        o2 = conv(blk(T.tf, 1), t2, tb[:, 0:20])
-        send(lb[:, 0:20], tb[:, 0:20], "ab", o2)
-        t4 = run("s", [t2, o2], S.activation, blk(T.tf, 2), blk(T.tf, 1).indirect(tb[:, 0:20]), COPY)
-        ro = conv(blk(T.bw, 2), b3, off(8))
-        fd = [run("v", [fw[b]], V.tensor_copy, blk(T.fd, b), blk(T.fw, b)) for b in (0, 1)]
-        sg = run("s", [ro, sf[1]], S.activation, T.sg[:], T.sf[:, 0:C].indirect(off(8)), COPY)
-        o4 = conv(blk(T.tf, 2), t4, tc[:, 0:20])
-        send(lc[:, 0:20], tc[:, 0:20], "ac", o4)
-        left += 5 * ne
-        if i == 0:
-            qv = run("v", [("ldv", 16)], V.quantize_mx, T.qv[:, 0:128], T.sv[:, 0:128], T.vin[:])
+            kp = pick("s", [kp], T.kp[:], T.ke[:, 0:128].indirect(T.ko[:, 0:20]))
 
         at, ab, ac = [("%s%d" % (k, i), na) for k in ("at", "ab", "ac")]
-        zs = [run("s", [at, fw[b]], S.activation, blk(T.tmp, b - 2), blk(T.fw, b).indirect(la[:, 0:20]), COPY) for b in (2, 3)]
-        z1 = [run("v", [at, fw[b], fd[b]], V.tensor_tensor, blk(T.z1, b), blk(T.fw, b).indirect(la[:, 0:20]), blk(T.fd, b), A.add) for b in (0, 1)]
-        z1 += [run("v", [zs[b - 2]], V.tensor_tensor, blk(T.z1, b), blk(T.tmp, b - 2), T.psa[:, 512 * b:512 * b + C], A.add) for b in (2, 3)]
-        d1 = [run("s", [z1[b]], S.activation, blk(T.d1, b), blk(T.z1, b), COPY) for b in range(4)]
-        z2 = [run("v", [ab, z1[b], d1[b]], V.tensor_tensor, blk(T.z2, b), blk(T.z1, b).indirect(lb[:, 0:20]), blk(T.d1, b), A.add) for b in range(4)]
-        d2 = [run("s", [z2[b]], S.activation, blk(T.d2, b), blk(T.z2, b), COPY) for b in range(4)]
-        z3 = [run("v", [ac, z2[b], d2[b]], V.tensor_tensor, T.z3[:, b:1280:4], blk(T.z2, b).indirect(lc[:, 0:20]), blk(T.d2, b), A.add) for b in range(4)]
-        tz = [run("v", z3, V.quantize_mx, T.qz[:, H * h:H * h + H], T.sz[:, H * h:H * h + H], T.z3[:, 4 * H * h:4 * H * h + 4 * H]) for h in (0, 1)]
+        calls = {}
 
-        fbank = [T.psf[:, 512:512 + C], T.psf[:, 1024:1024 + C]]
-        ff, fo = [], []
+        def call(name, deps, fn, *a):
+            calls[name] = (deps, fn, a)
+
+        def vec(name, deps, fn, *a):
+            calls[name] = (deps, lambda q, deps: run(q, deps, fn, *a), ())
+
         for b in range(4):
-            ff.append(run("t", [qe8] + fo[b - 2:b - 1], TE.matmul_mx, fbank[b % 2], mov(T.qe8, b), mov(T.se8, b), q[:, 0:C], s[:, 0:C], True, True))
-            fo.append(run("s", [ff[b]], S.activation, blk(T.fo, b), fbank[b % 2], COPY, scale=8.0))
-
-        hbank = [T.psa[:, 0:H], T.psf[:, 512:512 + H]]
-        hh = [run("t", [tz[h], ("ldw", 32), fw[3], fo[2]], TE.matmul_mx, hbank[h], mov(T.wq, 0), mov(T.wsq, 0),
-                  T.qz[:, H * h:H * h + H], T.sz[:, H * h:H * h + H], True, True) for h in (0, 1)]
-        hh += [run("t", [tz[1]], TE.matmul_mx, T.psa[:, 512 * b:512 * b + C], mov(T.wq, b), mov(T.wsq, b),
-                   T.qz[:, 0:C], T.sz[:, 0:C], True, True) for b in (1, 2, 3)]
-        hw = [run("s", [hh[h]], S.activation, T.hw[:, H * h:H * h + H], hbank[h], COPY, scale=0.03125) for h in (0, 1)][1:]
-        hw += [run("s", [hh[b + 1]], S.activation, blk(T.hw, b), T.psa[:, 512 * b:512 * b + C], COPY, scale=0.03125) for b in (1, 2, 3)]
-
-        a = [run("v", [sg], V.tensor_tensor, T.fl[:, H * h:H * h + H], T.sg[:, H * h:H * h + H], sbank[h], A.is_gt) for h in (0, 1)]
-        a = scan(T.fl[:], a)
-        e = run("v", [a], V.tensor_scalar, T.ew[:], w20(T.sca), T.thr[:, 0:1], T.inv[:, 0:1], A.is_gt, A.mult)
-
-        tx = []
-        for b in range(4):
-            tx.append(run("v", [hw[b], fo[b], tt], V.tensor_tensor, T.xt[:, b:1280:4], blk(T.hw, b).indirect(ta[:, 0:20]), blk(T.fo, b), A.add))
-            if i == 2 and b == 0:
-                e = run("v", [e], V.tensor_tensor, T.ed[:], T.ew[:], T.dw[:], A.mult)
-            if i == 2 and b == 1:
-                l0 = run("v", [e], V.tensor_tensor, T.l0w[:], T.l0w[:], T.ed[:], A.add)
-            if i == 2 and b == 2:
-                l1 = run("v", [l0, ss], V.tensor_tensor, T.l1w[:], T.ss[:], T.l0w[:], A.subtract)
-                l0 = run("v", [l0], V.tensor_copy, T.l0o[:], T.l0w[:])
-                l1 = run("v", [l1], V.tensor_copy, T.l1o[:], T.l1w[:])
-                lsd = [run("s", [k_if, t], S.activation, T.lsf[:, C * h:C * h + C], T.iof[:, 0:C].indirect(o[:, 0:20]), COPY)
-                       for h, t, o in ((0, l0, T.l0o), (1, l1, T.l1o))]
-        tq = quant(T.xt, i + 1, [tx, tx])
+            call("F%d" % b, [("aq%d" % i, 2 * na), qe8], mm, bank(T.psa, b), mov(T.qe8, b), mov(T.se8, b), lq, lp, "")
+            call("w%d" % b, ["F%d" % b], pick, blk(T.fw, b), bank(T.psa, b))
+            call("O%d" % b, [qe8, "o%d" % (b - 2)], mm, bank(T.psf, 1 + b % 2), mov(T.qe8, b), mov(T.se8, b), q, s, "")
+            call("o%d" % b, ["O%d" % b], pick, blk(T.fo, b), bank(T.psf, 1 + b % 2), 8.0)
+        for b in (0, 1):
+            call("d%d" % b, ["w%d" % b], pick, blk(T.fd, b), blk(T.fw, b))
+        for k, (out, win) in enumerate(((T.t1, T.iot), (T.t2, T.t1), (T.t1, T.t2), (T.t4, T.t1))):
+            call("t%d" % (k + 1), [tt, "t%d" % k], pick, out[:], win[:, 0:C].indirect(ta[:, 0:20]))
+        for k, full, dep, sca, lst in (("b", T.t2, "t2", T.scb, tb), ("c", T.t4, "t4", T.scc, tc)):
+            vec("s" + k, [dep, kp], V.tensor_tensor_scan, sca[:], T.kp[:], full[:], 0.0, A.mult, A.add)
+            vec("p" + k, ["s" + k], V.tensor_scalar, lst[:, 0:40], sca[:, 7:C:8], T.sc2[:, 0:1], T.b2[:, 0:1], A.mult, A.add)
+        vec("lw", [], V.tensor_scalar, T.lwo[:], w20(T.sca), T.scl[:, 0:1], MID + 0.25, A.mult, A.add)
+        call("g1", ["lw", sf], pick, blk(T.sg, 0), T.sf[:, 0:C].indirect(T.lwo[:, 0:20]))
+        call("g2", ["g1"], pick, blk(T.sg, 1), blk(T.sg, 0).indirect(far))
+        vec("fl", ["g2"], V.tensor_tensor, T.fl[:], blk(T.sg, 1).indirect(far), T.sf[:], A.is_gt)
+        vec("sx", ["fl"], V.tensor_tensor_scan, T.scd[:], T.kk[:], T.fl[:], 0.0, A.mult, A.add)
+        vec("ex", ["sx"], V.tensor_scalar, T.ex[:], w20(T.scd), T.thr[:, 0:1], 0.5, A.is_le, A.subtract)
+        vec("e1", ["ex"], V.tensor_tensor, DW, DW, T.ex[:], A.mult)
         if i < 2:
-            e = run("v", [e], V.tensor_tensor, T.ed[:], T.ew[:], T.dw[:], A.mult)
-            l0 = run("v", [e], V.tensor_tensor, T.l0w[:], T.l0w[:], T.ed[:], A.add)
-            eg = run("v", [e], V.tensor_scalar, T.eg[:], T.ed[:], T.scm[:, 0:1], None, A.mult)
+            vec("e2", ["e1"], V.tensor_scalar, DW, DW, 2.0, None, A.mult)
+        else:
+            vec("e2", ["e1"], V.tensor_scalar, DWA, DWA, 2.0, None, A.mult)
+            vec("e3", ["e2"], V.tensor_scalar, T.ed[:], DW, T.thr[:, 0:1], 2.0, A.mult, A.mult)
+            vec("e4", ["e3"], V.tensor_tensor, T.l0w[:], MIDL, T.ed[:], A.add)
+            vec("e5", ["e3"], V.tensor_tensor, T.l1w[:], MIDL, T.ed[:], A.subtract)
+            call("e6", ["e4"], pick, T.l0o[:], T.l0w[:])
+            call("e7", ["e5"], pick, T.l1o[:], T.l1w[:])
+            call("l0", ["e6", k_if], pick, blk(T.lsf, 0), T.iof[:, 0:C].indirect(T.l0o[:, 0:20]))
+            call("l1", ["e7", k_if], pick, blk(T.lsf, 1), T.iof[:, 0:C].indirect(T.l1o[:, 0:20]))
+        if i == 0:
+            vec("qv", [("ldv", 16)], V.quantize_mx, T.qv[:, 0:128], T.sv[:, 0:128], T.vin[:])
+        for b in (0, 1):
+            vec("a%d" % b, [at, "d%d" % b], V.tensor_tensor, one(T.z1, b), blk(T.fw, b).indirect(la[:, 0:20]), blk(T.fd, b), A.add)
+            call("u%d" % (b + 2), [at, "w%d" % (b + 2)], pick, blk(T.tmp, b), blk(T.fw, b + 2).indirect(la[:, 0:20]))
+            vec("a%d" % (b + 2), ["u%d" % (b + 2)], V.tensor_tensor, one(T.z1, b + 2), blk(T.tmp, b), bank(T.psa, b + 2), A.add)
+            call("A%d" % b, ["a%d" % b, "a%d" % (b + 2)], pick, two(T.d1, b), two(T.z1, b))
+            vec("b%d" % b, [ab, "A%d" % b], V.tensor_tensor, two(T.z2, b), two(T.z1, b).indirect(lb[:, 0:40]), two(T.d1, b), A.add)
+            call("B%d" % b, ["b%d" % b], pick, two(T.d2, b), two(T.z2, b))
+            for k, (lo, hi) in PART.items():
+                vec("c%d%s" % (b, k), [ac, "B%d" % b], V.tensor_tensor, T.z3[:, 4 * lo + b:4 * hi:2], two(T.z2, b).indirect(lc[:, lo // 8:hi // 8]),
+                    T.d2[:, W * b + 2 * lo:W * b + 2 * hi], A.add)
+        for k in "ab":
+            lo, hi = PART[k]
+            call("z" + k, ["c0", "c0" + k, "c1" + k], quant, T.qz, T.sz, T.z3, k)
+            for b in (0, 1):
+                hb = bank(T.psa, b, CUT) if k == "a" else bank((T.pss, T.psf)[b], 0, C - CUT)
+                call("H%d%s" % (b, k), ["z" + k, ("ldw", 32)], mm, hb, mov(T.wq, b), mov(T.wsq, b), T.qz, T.sz, k)
+                call("h%d%s" % (b, k), ["H%d%s" % (b, k)], pick, T.hw[:, C * b + lo:C * b + hi], hb, 0.03125)
+            call("y" + k, ["x0", "x1", "x2", "x2" + k, "x3" + k], quant, T["q%d" % (i + 1)], T["s%d" % (i + 1)], T.xt, k)
+        for b in range(4):
+            call("H%d" % b, ["zb"], mm, bank(T.psa, b), mov(T.wq, b), mov(T.wsq, b), T.qz, T.sz, "")
+            call("h%d" % b, ["H%d" % b], pick, blk(T.hw, b), bank(T.psa, b), 0.03125)
+            for k, (lo, hi) in PART.items():
+                vec("x%d%s" % (b, k), ["o%d" % b, "h%d" % b, "h%da" % b, "h%db" % b], V.tensor_tensor, T.xt[:, 4 * lo + b:4 * hi:4],
+                    blk(T.hw, b).indirect(ta[:, lo // 16:hi // 16]), T.fo[:, C * b + lo:C * b + hi], A.add)
+        order = {k: [x for x in ORDER[k].split() if x in calls] for k in "vstg"}
+        done = {x: ("c" + k, cnt[k] + 1 + j) for k in "vstg" for j, x in enumerate(order[k])}
+        sends = {">a": (tt, la[:, 0:20], ta[:, 0:20], "at"), ">b": (done["pb"], lb[:, 0:40], tb[:, 0:40], "ab"),
+                 ">c": (done["pc"], lc[:, 0:40], tc[:, 0:40], "ac")}
+        for k in "vstg":
+            for x in ORDER[k].split():
+                if x in sends:
+                    send(*sends[x])
+                elif x in calls:
+                    deps, fn, a = calls[x]
+                    fn(k, [done.get(y, y) for y in deps if y in done or isinstance(y, tuple)], *a)
+        left += 5 * ne
+        dw, tq = done["e2"], [done["ya"], done["yb"]]
+        if i == 0:
+            qv = done["qv"]
 
-    need("y", *lsd)
+    ybank = [bank(T.psa, 0, CUT), bank(T.psa, 1, C - CUT)]
+    yy = [mm("t", [tq[h], qv], ybank[h], T.qv[:, 0:128], T.sv[:, 0:128], T.q3, T.s3, "ab"[h]) for h in (0, 1)]
+    need("y", done["l0"], done["l1"])
     g.sync.dma_start(T.ls[:, :], T.lsf[0:128:16, :]).then_inc(T.sem.sto, 16)
-    need("y", *tq)
+    ya = pick("s", [yy[0]], T.yf[:, 0:CUT], ybank[0])
+    yb = pick("v", [yy[1]], T.yf[:, CUT:C], ybank[1])
+    need("y", tq[1])
     g.sync.dma_start(T.oc[:, :], T.q3[:, 0:C].bitcast(dt.uint8)).then_inc(T.sem.sto, 16)
-    yy = [run("t", [tq[h], qv, hw[3]], TE.matmul_mx, T.psa[:, 512 * h:512 * h + H], T.qv[:, 0:128], T.sv[:, 0:128],
-              T.q3[:, H * h:H * h + H], T.s3[:, H * h:H * h + H], True, True) for h in (0, 1)]
-    ya = run("v", [yy[0]], V.tensor_copy, T.yf[:, 0:H], T.psa[:, 0:H])
-    yb = run("s", [yy[1]], S.activation, T.yf[:, H:C], T.psa[:, 512:512 + H], COPY)
-    need("y", ya)
-    g.sync.dma_start(T.y[:, 0:H], T.yf[:, 0:H]).then_inc(T.sem.sto, 16)
-    need("s", yb)
-    g.scalar.dma_start(T.y[:, H:C], T.yf[:, H:C]).then_inc(T.sem.stc, 16)
     for k in range(4):
         g.sync.dma_start(T.osc[4 * k:4 * k + 4, :], T.s3[32 * k:32 * k + 4, 0:C]).then_inc(T.sem.sto, 16)
-    need("g", ("cv", cnt["v"]), ("cs", cnt["s"]), ("ct", cnt["t"]), ("cg", cnt["g"]), ("left", left), ("sto", 112), ("stc", 16))
+    need("s", ya)
+    g.scalar.dma_start(T.y[:, 0:CUT], T.yf[:, 0:CUT]).then_inc(T.sem.stc, 16)
+    need("s", yb)
+    g.scalar.dma_start(T.y[:, CUT:C], T.yf[:, CUT:C]).then_inc(T.sem.stc, 16)
+    need("g", ("cv", cnt["v"]), ("cs", cnt["s"]), ("ct", cnt["t"]), ("cg", cnt["g"]), ("left", left), ("sto", 96), ("stc", 32))

@@ -2,19 +2,20 @@ from concourse.mybir import dt, AluOpType, ActivationFunctionType
 
 C = 320
 W = 2 * C
-CUT = 192
+CUT = 160
 PART = {"": (0, C), "a": (0, CUT), "b": (CUT, C)}
 RADIX = [3, 3, 3, 3, 2]
 STEP = [1, 2, 4]
 BIG = 2.0 ** 24
 MID = 159
+LOW = -256.0
+DV = 112
 BF, F32, I32, U16 = "bfloat16", "float32", "int32", "uint16"
 
-ORDER = dict(v="lw g1 w2 d1 g2 sb pb fl sc a0 pc a2 a1 a3 sx b0 b1 c0 c1a c1b za zb ex e1 qv e2 h0b e3 x0 e4 e5 x1 e6 e7 x2 x3a x3b ya yb",
-             s="w1 w0 w3 t1 t2 t3 t4 u2 u3 A0 A1 o0 B0 B1 o1 o2 o3 h0a h1 h2 h3 l0 l1",
-             t="F1 F0 F3 F2 O0 O1 O2 O3 H0a H0b H1 H2 H3",
-             g=">a d0 >b >c")
-DV = 112
+ORDER = dict(v="lw g1 d1 g2 sb fl pb a0 a1 a3 a2 b0 b1 b2 b3 c0 c1 c2 c3a c3b za zb sx qv ex e1 h0b e2 e3 x0 e4 e5 x1 e6 e7 x2 x3a x3b ya yb",
+             s="w0 w1 w3 o0 t1 t2 w2 u3 u2 A0 A1 A2 A3 B0 B1 B2 B3 o1 o2 o3 h0a h1 h2 h3 l0 l1",
+             t="F0 F1 F3 F2 O0 O1 O2 O3 H0a H0b H1 H2 H3",
+             g=">a d0 >b")
 
 SCRATCH = {}
 
@@ -24,12 +25,12 @@ def _sb(dtype, **kw):
         SCRATCH[k] = ("sbuf", [128, n], dtype)
 
 
-_sb(BF, xin=1280, uin=512, vin=512, e8=516, iot=C, kd=128, ke=128, kk=C, kp=C, sca=C, scb=C, scc=C, scd=C, mm=C,
-    aw=3 * C, low=2 * C, ld=C, t1=C, t2=C, t4=C, fw=1280, fd=W, fo=1280, hw=1280, tmp=W, z1=1280, z2=1280,
-    d1=1280, d2=1280, z3=1280, xt=1280, fl=C)
-_sb(F32, iof=C, dj=128, m16=20, kf=1, scl=1, thr=1, sc2=1, b2=1, tiny=1, cw=20, cx=20, sf=C, l0w=20, l1w=20,
-    sg=2 * C, sa=40, sb=40, so=40, ex=20, lsf=2 * C, yf=C, ed=20, dw=20, mid=20, tp=20)
-_sb(I32, lai=20, lbi=20, pi=20, ki=3)
+_sb(BF, xin=1280, uin=512, vin=512, e8=516, iot=C, iot2=W, kd=128, kk=C, sca=C, scb=C, scx=C, mm=C,
+    pp=3 * W, l2=2 * W, aw=2 * C, low=2 * C, ld=C, t1=C, t2=C, fl=C,
+    fw=1280, fd=W, fo=1280, hw=1280, tmp=W, z1=1280, z2=1280, y1=1280, y2=1280, z3=1280, xt=1280)
+_sb(F32, iof=C, dj=128, m16=20, kf=1, scl=1, sc2=1, thr=1, tiny=1, cw=20, cx=20, sf=C, sg=2 * C, ps=1008, pk=60, po=60,
+    sa=40, sb=40, so=40, ex=20, ed=20, l0w=20, l1w=20, lsf=2 * C, yf=C)
+_sb(I32, lai=20, lbi=20, pi=20, ki=1)
 _sb(U16, uo=8, ko=20, offs=20 * len(RADIX) + 20, lwo=20, l0o=20, l1o=20)
 _sb("float8_e4m3fn_x4", wq=512, qu=128, qup=128, qv=128, qe8=512, qz=C)
 _sb("uint8", wsq=512, su=128, sup=128, sv=128, se8=512, sz=C)
@@ -39,14 +40,14 @@ for _i in range(4):
 for _i in range(3):
     SCRATCH["lq%d" % _i] = ("sbuf", [128, C], "float8_e4m3fn_x4")
     SCRATCH["lp%d" % _i] = ("sbuf", [128, C], "uint8")
-    for _k, _n in (("ta", 20), ("tb", 40), ("tc", 40), ("la_", 20), ("lb_", 40), ("lc_", 40)):
-        SCRATCH["%s%d" % (_k, _i)] = ("sbuf", [128, _n], U16)
+    for _k in ("ta", "tb", "la_", "lb_"):
+        SCRATCH["%s%d" % (_k, _i)] = ("sbuf", [128, 20], U16)
 SCRATCH["psa"] = ("psum", [128, 2048], F32)
 SCRATCH["psf"] = ("psum", [128, 1536], F32)
 SCRATCH["pss"] = ("psum", [128, 512], F32)
 
-SEMAPHORES = ["cv", "cs", "ct", "cg", "left", "ldx", "ldy", "ldu", "ldv", "ldl", "ldw", "sto", "stc"]
-SEMAPHORES += ["%s%d" % (k, i) for k in ("aq", "at", "ab", "ac") for i in range(3)]
+SEMAPHORES = ["cv", "cs", "ct", "cg", "left", "ldx", "ldu", "ldv", "ldl", "ldw", "sto", "stc"]
+SEMAPHORES += ["%s%d" % (k, i) for k in ("aq", "at", "ab") for i in range(3)]
 
 
 def rank_program(g, core, T, topo):
@@ -81,20 +82,23 @@ def rank_program(g, core, T, topo):
     def w20(buf):
         return buf[:, 15:C:16]
 
-    def blk(buf, b):
-        return buf[:, C * b:C * b + C]
+    def blk(buf, b, lo=0, hi=C):
+        return buf[:, C * b + lo:C * b + hi]
 
-    def two(buf, k):
+    def wide(buf, k):
         return buf[:, W * k:W * k + W]
 
-    def one(buf, b):
-        return buf[:, W * (b % 2) + b // 2:W * (b % 2) + W:2]
+    def even(buf, k, lo=0, hi=C):
+        return buf[:, W * k + 2 * lo:W * k + 2 * hi:2]
 
     def mov(buf, b):
         return buf[:, 128 * b:128 * b + 128]
 
     def bank(buf, b, n=C):
         return buf[:, 512 * b:512 * b + n]
+
+    def off(k, lo=0, hi=C):
+        return T.offs[:, 20 * k + lo // 16:20 * k + hi // 16]
 
     def pick(q, deps, out, in_, scale=None):
         if q == "g":
@@ -111,58 +115,58 @@ def rank_program(g, core, T, topo):
         lo, hi = PART[part]
         return run(q, deps, V.quantize_mx, codes[:, lo:hi], plane[:, lo:hi], tile[:, 4 * lo:4 * hi])
 
-    g.sync.dma_start(T.xin[:, 0:4 * CUT], T.x[:, 0:4 * CUT]).then_inc(T.sem.ldx, 16)
+    def scan(q, deps, out, factors, numbers):
+        return run(q, deps, V.tensor_tensor_scan, out, factors, numbers, 0.0, A.mult, A.add)
+
+    def place(q, deps, out, ends):
+        return run(q, deps, V.tensor_scalar, out, ends, T.scl[:, 0:1], MID + 0.25, A.mult, A.add)
+
     g.scalar.dma_start(T.uin[:], T.u[:, :]).then_inc(T.sem.ldu, 16)
-    g.scalar.dma_start(T.xin[:, 4 * CUT:1280], T.x[:, 4 * CUT:1280]).then_inc(T.sem.ldy, 16)
-    LX = [("ldx", 16), ("ldy", 16)]
+    g.sync.dma_start(T.xin[:], T.x[:, :]).then_inc(T.sem.ldx, 16)
     g.sync.dma_start(T.lai[:], T.la[:, :]).then_inc(T.sem.ldl, 16)
     g.scalar.dma_start(T.lbi[:], T.lb[:, :]).then_inc(T.sem.ldl, 16)
-    need("y", *LX)
+    need("y", ("ldx", 16))
     g.sync.dma_start(T.wq[:, 0:512].bitcast(dt.uint8), T.wc[:, :]).then_inc(T.sem.ldw, 16)
     g.sync.dma_start(T.wsq[:, 0:512], T.ws[:, :]).then_inc(T.sem.ldw, 16)
     g.sync.dma_start(T.vin[:], T.v[:, :]).then_inc(T.sem.ldv, 16)
 
     SMALL = {"allow_small_or_imprecise_dtypes": True}
-
-    def factors(buf, pattern, zero, big):
-        a = run("g", [], g.iota, buf[:], [[0, 128]], 1, 0, **SMALL)
-        for fill, at in [(0.0, k) for k in zero] + [(BIG, k) for k in big]:
-            a = run("g", [a], g.affine_select, buf[:], buf[:], pattern, A.not_equal, fill, -at, -1)
-        return a
-
     k_pi = run("g", [], g.iota, T.pi[:], [[0, 20]], 0, 1)
     k_m16 = run("g", [], g.iota, T.m16[:], [[16, 20]], 0, 0, **SMALL)
     k_dj = run("g", [], g.iota, T.dj[:], [[1, 128]], 0, -1, **SMALL)
-    kk = factors(T.kd, [[1, 128]], [0], [1])
-    k_io = run("g", [], g.iota, T.iot[:], [[1, C]], -MID, 0, **SMALL)
+    kk = run("g", [], g.iota, T.kd[:], [[0, 128]], 1, 0, **SMALL)
+    for fill, at in ((0.0, 0), (BIG, 1)):
+        kk = run("g", [kk], g.affine_select, T.kd[:], T.kd[:], [[1, 128]], A.not_equal, fill, -at, -1)
+    k_io = run("g", [], g.iota, T.iot2[:], [[1, C], [0, 2]], -MID, 0, **SMALL)
 
     m8 = run("v", [], V.memset, T.e8[:], 0.0)
-    ki = [run("v", [k_pi], V.tensor_scalar, T.ki[:, j:j + 1], T.pi[:, 0:1], bits, None, A.bitwise_and) for j, bits in enumerate((15, 14, 1))]
+    gap = run("v", [], V.memset, T.pp[:, 1:3 * W:2], LOW)
+    ki = run("v", [k_pi], V.tensor_scalar, T.ki[:], T.pi[:, 0:1], 15, None, A.bitwise_and)
     ko = run("v", [k_pi], V.tensor_copy, T.ko[:], T.pi[:])
     uo = run("v", [k_m16], V.tensor_copy, T.uo[:], T.m16[:, 0:8])
     tiny = run("v", [], V.memset, T.tiny[:], 2.0 ** -100)
-    run("v", [], V.memset, T.sa[:], 0.0)
-    kf = run("v", ki, V.tensor_copy, T.kf[:], T.ki[:, 0:1])
-    run("v", ki, V.tensor_scalar, T.b2[:], T.ki[:, 2:3], 2 * MID + 0.25, None, A.add)
-    last = [(T.scl, 0, 15.0, 1.0, 1 / BIG), (T.sc2, 1, 14.0, 2.0, 2 / BIG), (T.thr, 0, 15.0, 0.5, BIG / 2)]
-    a = [run("v", ki, V.tensor_scalar, buf[:], T.ki[:, j:j + 1], at, x - y, A.is_equal, A.mult) for buf, j, at, x, y in last]
+    for view in (T.sa[:], T.pk[:], T.ps[:, 29:989:16]):
+        run("v", [], V.memset, view, 0.0)
+    kf = run("v", [ki], V.tensor_copy, T.kf[:], T.ki[:])
+    last = [(T.scl, 1.0, 1 / BIG), (T.sc2, 2.0, 2 / BIG), (T.thr, 0.5, BIG / 2)]
+    a = [run("v", [ki], V.tensor_scalar, buf[:], T.ki[:], 15.0, x - y, A.is_equal, A.mult) for buf, x, y in last]
     cw = run("v", [k_m16, kf], V.tensor_scalar, T.cw[:], T.m16[:], T.kf[:, 0:1], None, A.add)
-    sc = [run("v", a, V.tensor_scalar, buf[:], buf[:], y, None, A.add) for buf, j, at, x, y in last][2]
+    sc = [run("v", a, V.tensor_scalar, buf[:], buf[:], y, None, A.add) for buf, x, y in last][-1]
     d8 = run("v", [k_dj, m8], V.tensor_scalar, T.e8[:, 3:515:4], T.dj[:], 0.0, 0.125, A.is_equal, A.mult)
     a = run("v", [cw, sc], V.tensor_scalar, T.cx[:], T.cw[:], float(MID), T.thr[:, 0:1], A.subtract, A.mult)
-    run("v", [a], V.tensor_scalar, T.cx[:], T.cx[:], 2.0, None, A.mult)
-    kk = pick("s", [kk, ko], T.kk[:], T.kd[:, 0:128].indirect(T.ko[:, 0:20]))
 
     def unpacker(b):
         return run("v", [d8], V.quantize_mx, mov(T.qe8, b), mov(T.se8, b), T.e8[:, 3 - b:515 - b])
 
-    a = run("v", [("ldu", 16)], V.quantize_mx, T.qu[:, 0:128], T.su[:, 0:128], T.uin[:])
     unpacker(0)
+    run("v", [a], V.tensor_scalar, T.cx[:], T.cx[:], 2.0, None, A.mult)
+    a = run("v", [("ldu", 16)], V.quantize_mx, T.qu[:, 0:128], T.su[:, 0:128], T.uin[:])
+    unpacker(1)
     qup = run("v", [a, uo], V.tensor_copy, T.qup[:, 0:128].bitcast(dt.uint32), T.qu[:, 0:128].bitcast(dt.uint32).indirect(T.uo[:, 0:8]))
     qus = run("s", [a, uo], S.activation, T.sup[:, 0:128], T.su[:, 0:128].indirect(T.uo[:, 0:8]), COPY)
-    unpacker(1)
-    tq = [quant("v", [LX[h]], T.q0, T.s0, T.xin, "ab"[h]) for h in (0, 1)]
-    DW, DWA, MIDL, P = T.dw[:], T.dw[:, 0:CUT // 16], T.mid[:], T.sb[:, 1:40:2]
+    kk = pick("s", [kk, ko], T.kk[:], T.kd[:, 0:128].indirect(T.ko[:, 0:20]))
+    tq = [quant("v", [("ldx", 16)], T.q0, T.s0, T.xin, k) for k in "ab"]
+    DW, DWA, MIDL, P = T.pk[:, 2:60:3], T.pk[:, 2:3 * (CUT // 16):3], T.ps[:, 61:1008:48], T.po[:, 2:60:3]
     a = run("v", [("ldl", 32)], V.tensor_tensor, DW, T.lai[:], T.lbi[:], A.subtract)
     b = run("v", [("ldl", 32)], V.tensor_tensor, MIDL, T.lai[:], T.lbi[:], A.add)
     unpacker(2)
@@ -171,15 +175,11 @@ def rank_program(g, core, T, topo):
     qe8 = unpacker(3)
     dw = run("v", [a], V.tensor_scalar, DWA, DWA, 0.5, None, A.mult)
 
-    def off(k):
-        return T.offs[:, 20 * k:20 * k + 20]
-
     left = 0
     for i, d in enumerate(STEP):
         q, s = T["q%d" % i], T["s%d" % i]
         lq, lp = T["lq%d" % i], T["lp%d" % i]
-        ta, tb, tc = [T["%s%d" % (k, i)] for k in ("ta", "tb", "tc")]
-        la, lb, lc = [T["%s%d" % (k, i)] for k in ("la_", "lb_", "lc_")]
+        ta, tb, la, lb = [T["%s%d" % (k, i)] for k in ("ta", "tb", "la_", "lb_")]
         dst = T.cores[(rank + d) % N]
         src = T.cores[(rank - d) % N]
         rid, pid, _ = topo.addr(dst)
@@ -193,43 +193,50 @@ def rank_program(g, core, T, topo):
         send(tq[1], lq[:, 0:C].bitcast(dt.uint8), q[:, 0:C].bitcast(dt.uint8), "aq")
         send(tq[1], lp[:, 0:C], s[:, 0:C], "aq")
         if i == 0:
-            kp = factors(T.ke, [[16, 8], [0, 2], [2, 8]], [0, -1], [1, 2])
+            run("g", [], g.iota, T.iot[:], [[1, C]], -MID, 0, **SMALL)
             k_if = run("g", [], g.iota, T.iof[:], [[1, C]], 0, 0, **SMALL)
 
         sbank = [bank(T.pss, 0, CUT), bank(T.psf, 0, C - CUT)]
         ts = [mm("t", [tq[h], qup, qus], sbank[h], T.qup[:, 0:128], T.sup[:, 0:128], q, s, "ab"[h]) for h in (0, 1)]
         m = [run("s", [ts[0], tiny], S.activation, T.mm[:, 0:CUT], sbank[0], SIGN, bias=T.tiny[:, 0:1]),
              run("v", [ts[1]], V.tensor_scalar, T.mm[:, CUT:C], sbank[1], 0.0, 0.5, A.is_ge, A.subtract)]
-        a = [run("v", [m[h], kk], V.tensor_tensor_scan, T.sca[:, lo:hi], T.kk[:, lo:hi], T.mm[:, lo:hi], 0.0, A.mult, A.add)
-             for h, (lo, hi) in enumerate((PART["a"], PART["b"]))][1]
-        a = run("v", [a, dw], V.tensor_tensor, T.tp[:], w20(T.sca), DW, A.mult)
-        a = run("v", [a], V.tensor_tensor, P, T.tp[:], MIDL, A.add)
-        o = pick("v", [a], off(0), P)
-        sf = [pick("s", [m[h]], T.sf[:, PART["ab"[h]][0]:PART["ab"[h]][1]], sbank[h]) for h in (0, 1)][1]
+        a = [scan("v", [m[h], kk], T.ps[:, 3 * lo:3 * hi:3], T.kk[:, lo:hi], T.mm[:, lo:hi]) for h, (lo, hi) in enumerate((PART["a"], PART["b"]))][1]
+        a = scan("v", [a, dw], T.po[:], T.pk[:], T.ps[:, 29:989:16])
+        o = run("v", [a], V.tensor_scalar, off(0), P, 2.0, 0.25, A.mult, A.subtract)
+        pick("v", [], T.sb[:, 1:40:2], P)
+        sf = [pick("s", [m[h]], blk(T.sf, 0, *PART["ab"[h]]), sbank[h]) for h in (0, 1)][1]
 
-        ak = pick("s", [o, k_io], blk(T.aw, 0), T.iot[:, 0:C].indirect(off(0)))
-        dup = pick("v", [o, k_io], T.ld[:], T.iot[:, 0:C].indirect(off(0)))
-        run("v", [], V.tensor_tensor, T.sa[:, 1:40:2], T.cw[:], P, A.subtract)
-        low, lowt, n = blk(T.aw, 0), ak, 0
-        for k, r in enumerate(RADIX):
-            for j in range(r - 1):
-                ak = pick("s", [ak, o], blk(T.aw, (n + 1) % 3), blk(T.aw, n % 3).indirect(off(k)))
-                lowt = run("v", [lowt, o, dup], V.tensor_tensor, blk(T.low, n % 2), low.indirect(off(k)), T.ld[:], A.min)
-                low, at, n = blk(T.low, n % 2), C * (n % 2), n + 1
-            dup = pick("s", [lowt], T.ld[:, DV:C], T.low[:, at + DV:at + C])
-            a = run("v", [ak, kk], V.tensor_tensor_scan, T.sca[:], T.kk[:], blk(T.aw, n % 3), 0.0, A.mult, A.add)
-            pick("v", [lowt], T.ld[:, 0:DV], T.low[:, at:at + DV])
-            o = run("v", [a], V.tensor_scalar, off(k + 1), w20(T.sca), T.scl[:, 0:1], MID + 0.25, A.mult, A.add)
+        a, win = [o, k_io, gap], T.iot2[:, 0:W]
+        for k in range(3):
+            a = [pick(e, a, even(T.pp, k, lo, hi), win.indirect(off(0, lo, hi))) for e, lo, hi in (("v", 0, C // 2), ("s", C // 2, C))]
+            win = wide(T.pp, k)
+            if k == 0:
+                run("v", [], V.tensor_tensor, T.sa[:, 1:40:2], T.cw[:], P, A.subtract)
+        b = run("v", [], V.tensor_tensor_scan, wide(T.l2, 0), wide(T.pp, 0), wide(T.pp, 1), LOW, A.max, A.min)
+        a = scan("v", a, T.sca[:], T.kk[:], even(T.pp, 2))
+        lowt = run("v", [b], V.tensor_tensor_scan, wide(T.l2, 1), wide(T.l2, 0), wide(T.pp, 2), LOW, A.max, A.min)
+        ak = o = run("v", [a], V.tensor_scalar, off(1), w20(T.sca), T.sc2[:, 0:1], 2 * MID + 0.25, A.mult, A.add)
+        dup = pick("v", [lowt], T.ld[:], even(T.l2, 1))
+        link, low, n = wide(T.pp, 2), wide(T.l2, 1), 0
+        for k in range(1, len(RADIX)):
+            for j in range(RADIX[k] - 1):
+                spaced = k == 1 and j < RADIX[k] - 2
+                ak = pick("s", [ak, o], even(T.pp, 0) if spaced else blk(T.aw, n % 2), link.indirect(off(k)))
+                lowt = run("v", [lowt, o, dup], V.tensor_tensor, even(T.l2, 0) if spaced else blk(T.low, n % 2), low.indirect(off(k)), T.ld[:], A.min)
+                link, low = (wide(T.pp, 0), wide(T.l2, 0)) if spaced else (blk(T.aw, n % 2), blk(T.low, n % 2))
+                n += 1
+            dup = pick("s", [lowt], T.ld[:, DV:C], blk(T.low, (n - 1) % 2, DV, C))
+            a = scan("v", [ak], T.sca[:], T.kk[:], link)
+            pick("v", [lowt], T.ld[:, 0:DV], blk(T.low, (n - 1) % 2, 0, DV))
+            o = place("v", [a], off(k + 1), w20(T.sca))
         far = off(len(RADIX))
-        lowt = run("v", [lowt, o, dup], V.tensor_tensor, blk(T.low, n % 2), low.indirect(far), T.ld[:], A.min)
-        a = run("v", [lowt], V.tensor_tensor_scan, T.sca[:], T.kk[:], blk(T.low, n % 2), 0.0, A.mult, A.add)
+        a = run("v", [lowt, o, dup], V.tensor_tensor, blk(T.low, n % 2), low.indirect(far), T.ld[:], A.min)
+        a = scan("v", [a], T.sca[:], T.kk[:], blk(T.low, n % 2))
         a = run("v", [a], V.tensor_tensor, T.sb[:, 0:40:2], w20(T.sca), T.cx[:], A.is_equal)
-        a = run("v", [a], V.tensor_tensor_scan, T.so[:], T.sa[:], T.sb[:], 0.0, A.mult, A.add)
+        a = scan("v", [a], T.so[:], T.sa[:], T.sb[:])
         tt = run("v", [a], V.tensor_scalar, ta[:, 0:20], T.so[:, 1:40:2], 0.125, None, A.add)
-        if i == 0:
-            kp = pick("s", [kp], T.kp[:], T.ke[:, 0:128].indirect(T.ko[:, 0:20]))
 
-        at, ab, ac = [("%s%d" % (k, i), na) for k in ("at", "ab", "ac")]
+        at, ab = [("%s%d" % (k, i), na) for k in ("at", "ab")]
         calls = {}
 
         def call(name, deps, fn, *a):
@@ -245,17 +252,16 @@ def rank_program(g, core, T, topo):
             call("o%d" % b, ["O%d" % b], pick, blk(T.fo, b), bank(T.psf, 1 + b % 2), 8.0)
         for b in (0, 1):
             call("d%d" % b, ["w%d" % b], pick, blk(T.fd, b), blk(T.fw, b))
-        for k, (out, win) in enumerate(((T.t1, T.iot), (T.t2, T.t1), (T.t1, T.t2), (T.t4, T.t1))):
-            call("t%d" % (k + 1), [tt, "t%d" % k], pick, out[:], win[:, 0:C].indirect(ta[:, 0:20]))
-        for k, full, dep, sca, lst in (("b", T.t2, "t2", T.scb, tb), ("c", T.t4, "t4", T.scc, tc)):
-            vec("s" + k, [dep, kp], V.tensor_tensor_scan, sca[:], T.kp[:], full[:], 0.0, A.mult, A.add)
-            vec("p" + k, ["s" + k], V.tensor_scalar, lst[:, 0:40], sca[:, 7:C:8], T.sc2[:, 0:1], T.b2[:, 0:1], A.mult, A.add)
-        vec("lw", [], V.tensor_scalar, T.lwo[:], w20(T.sca), T.scl[:, 0:1], MID + 0.25, A.mult, A.add)
+        call("t1", [tt, k_if], pick, T.t1[:], T.iot[:, 0:C].indirect(ta[:, 0:20]))
+        call("t2", ["t1"], pick, T.t2[:], T.t1[:, 0:C].indirect(ta[:, 0:20]))
+        call("sb", ["t2"], scan, T.scb[:], T.kk[:], T.t2[:])
+        call("pb", ["sb"], place, tb[:, 0:20], w20(T.scb))
+        call("lw", [], place, T.lwo[:], w20(T.sca))
         call("g1", ["lw", sf], pick, blk(T.sg, 0), T.sf[:, 0:C].indirect(T.lwo[:, 0:20]))
         call("g2", ["g1"], pick, blk(T.sg, 1), blk(T.sg, 0).indirect(far))
         vec("fl", ["g2"], V.tensor_tensor, T.fl[:], blk(T.sg, 1).indirect(far), T.sf[:], A.is_gt)
-        vec("sx", ["fl"], V.tensor_tensor_scan, T.scd[:], T.kk[:], T.fl[:], 0.0, A.mult, A.add)
-        vec("ex", ["sx"], V.tensor_scalar, T.ex[:], w20(T.scd), T.thr[:, 0:1], 0.5, A.is_le, A.subtract)
+        call("sx", ["fl"], scan, T.scx[:], T.kk[:], T.fl[:])
+        vec("ex", ["sx"], V.tensor_scalar, T.ex[:], w20(T.scx), T.thr[:, 0:1], 0.5, A.is_le, A.subtract)
         vec("e1", ["ex"], V.tensor_tensor, DW, DW, T.ex[:], A.mult)
         if i < 2:
             vec("e2", ["e1"], V.tensor_scalar, DW, DW, 2.0, None, A.mult)
@@ -266,38 +272,36 @@ def rank_program(g, core, T, topo):
             vec("e5", ["e3"], V.tensor_tensor, T.l1w[:], MIDL, T.ed[:], A.subtract)
             call("e6", ["e4"], pick, T.l0o[:], T.l0w[:])
             call("e7", ["e5"], pick, T.l1o[:], T.l1w[:])
-            call("l0", ["e6", k_if], pick, blk(T.lsf, 0), T.iof[:, 0:C].indirect(T.l0o[:, 0:20]))
-            call("l1", ["e7", k_if], pick, blk(T.lsf, 1), T.iof[:, 0:C].indirect(T.l1o[:, 0:20]))
+            call("l0", ["e6"], pick, blk(T.lsf, 0), T.iof[:, 0:C].indirect(T.l0o[:, 0:20]))
+            call("l1", ["e7"], pick, blk(T.lsf, 1), T.iof[:, 0:C].indirect(T.l1o[:, 0:20]))
         if i == 0:
             vec("qv", [("ldv", 16)], V.quantize_mx, T.qv[:, 0:128], T.sv[:, 0:128], T.vin[:])
-        for b in (0, 1):
-            vec("a%d" % b, [at, "d%d" % b], V.tensor_tensor, one(T.z1, b), blk(T.fw, b).indirect(la[:, 0:20]), blk(T.fd, b), A.add)
-            call("u%d" % (b + 2), [at, "w%d" % (b + 2)], pick, blk(T.tmp, b), blk(T.fw, b + 2).indirect(la[:, 0:20]))
-            vec("a%d" % (b + 2), ["u%d" % (b + 2)], V.tensor_tensor, one(T.z1, b + 2), blk(T.tmp, b), bank(T.psa, b + 2), A.add)
-            call("A%d" % b, ["a%d" % b, "a%d" % (b + 2)], pick, two(T.d1, b), two(T.z1, b))
-            vec("b%d" % b, [ab, "A%d" % b], V.tensor_tensor, two(T.z2, b), two(T.z1, b).indirect(lb[:, 0:40]), two(T.d1, b), A.add)
-            call("B%d" % b, ["b%d" % b], pick, two(T.d2, b), two(T.z2, b))
+        for b in range(4):
+            if b < 2:
+                vec("a%d" % b, [at, "d%d" % b], V.tensor_tensor, blk(T.z1, b), blk(T.fw, b).indirect(la[:, 0:20]), blk(T.fd, b), A.add)
+            else:
+                call("u%d" % b, [at, "w%d" % b], pick, blk(T.tmp, b - 2), blk(T.fw, b).indirect(la[:, 0:20]))
+                vec("a%d" % b, ["u%d" % b], V.tensor_tensor, blk(T.z1, b), blk(T.tmp, b - 2), bank(T.psa, b), A.add)
+            call("A%d" % b, ["a%d" % b], pick, blk(T.y1, b), blk(T.z1, b).indirect(la[:, 0:20]))
+            vec("b%d" % b, ["A%d" % b], V.tensor_tensor, blk(T.z2, b), blk(T.y1, b).indirect(la[:, 0:20]), blk(T.z1, b), A.add)
+            call("B%d" % b, [ab, "b%d" % b], pick, blk(T.y2, b), blk(T.z2, b).indirect(lb[:, 0:20]))
             for k, (lo, hi) in PART.items():
-                vec("c%d%s" % (b, k), [ac, "B%d" % b], V.tensor_tensor, T.z3[:, 4 * lo + b:4 * hi:2], two(T.z2, b).indirect(lc[:, lo // 8:hi // 8]),
-                    T.d2[:, W * b + 2 * lo:W * b + 2 * hi], A.add)
-        for k in "ab":
-            lo, hi = PART[k]
-            call("z" + k, ["c0", "c0" + k, "c1" + k], quant, T.qz, T.sz, T.z3, k)
-            for b in (0, 1):
-                hb = bank(T.psa, b, CUT) if k == "a" else bank((T.pss, T.psf)[b], 0, C - CUT)
-                call("H%d%s" % (b, k), ["z" + k, ("ldw", 32)], mm, hb, mov(T.wq, b), mov(T.wsq, b), T.qz, T.sz, k)
-                call("h%d%s" % (b, k), ["H%d%s" % (b, k)], pick, T.hw[:, C * b + lo:C * b + hi], hb, 0.03125)
-            call("y" + k, ["x0", "x1", "x2", "x2" + k, "x3" + k], quant, T["q%d" % (i + 1)], T["s%d" % (i + 1)], T.xt, k)
+                vec("c%d%s" % (b, k), [ab, "B%d" % b], V.tensor_tensor, T.z3[:, 4 * lo + b:4 * hi:4], blk(T.y2, b).indirect(lb[:, lo // 16:hi // 16]),
+                    blk(T.z2, b, lo, hi), A.add)
+        for k, hb in (("a", bank(T.psa, 0, CUT)), ("b", bank(T.pss, 0, C - CUT))):
+            call("z" + k, ["c2", "c3" + k], quant, T.qz, T.sz, T.z3, k)
+            call("H0" + k, ["z" + k, ("ldw", 32)], mm, hb, mov(T.wq, 0), mov(T.wsq, 0), T.qz, T.sz, k)
+            call("h0" + k, ["H0" + k], pick, blk(T.hw, 0, *PART[k]), hb, 0.03125)
+            call("y" + k, ["x2", "x3" + k], quant, T["q%d" % (i + 1)], T["s%d" % (i + 1)], T.xt, k)
         for b in range(4):
             call("H%d" % b, ["zb"], mm, bank(T.psa, b), mov(T.wq, b), mov(T.wsq, b), T.qz, T.sz, "")
             call("h%d" % b, ["H%d" % b], pick, blk(T.hw, b), bank(T.psa, b), 0.03125)
             for k, (lo, hi) in PART.items():
                 vec("x%d%s" % (b, k), ["o%d" % b, "h%d" % b, "h%da" % b, "h%db" % b], V.tensor_tensor, T.xt[:, 4 * lo + b:4 * hi:4],
-                    blk(T.hw, b).indirect(ta[:, lo // 16:hi // 16]), T.fo[:, C * b + lo:C * b + hi], A.add)
+                    blk(T.hw, b).indirect(ta[:, lo // 16:hi // 16]), blk(T.fo, b, lo, hi), A.add)
         order = {k: [x for x in ORDER[k].split() if x in calls] for k in "vstg"}
         done = {x: ("c" + k, cnt[k] + 1 + j) for k in "vstg" for j, x in enumerate(order[k])}
-        sends = {">a": (tt, la[:, 0:20], ta[:, 0:20], "at"), ">b": (done["pb"], lb[:, 0:40], tb[:, 0:40], "ab"),
-                 ">c": (done["pc"], lc[:, 0:40], tc[:, 0:40], "ac")}
+        sends = {">a": (tt, la[:, 0:20], ta[:, 0:20], "at"), ">b": (done["pb"], lb[:, 0:20], tb[:, 0:20], "ab")}
         for k in "vstg":
             for x in ORDER[k].split():
                 if x in sends:
@@ -305,23 +309,21 @@ def rank_program(g, core, T, topo):
                 elif x in calls:
                     deps, fn, a = calls[x]
                     fn(k, [done.get(y, y) for y in deps if y in done or isinstance(y, tuple)], *a)
-        left += 5 * ne
+        left += 4 * ne
         dw, tq = done["e2"], [done["ya"], done["yb"]]
         if i == 0:
             qv = done["qv"]
 
     ybank = [bank(T.psa, 0, CUT), bank(T.psa, 1, C - CUT)]
     yy = [mm("t", [tq[h], qv], ybank[h], T.qv[:, 0:128], T.sv[:, 0:128], T.q3, T.s3, "ab"[h]) for h in (0, 1)]
-    need("y", done["l0"], done["l1"])
+    need("y", done["l1"])
     g.sync.dma_start(T.ls[:, :], T.lsf[0:128:16, :]).then_inc(T.sem.sto, 16)
-    ya = pick("s", [yy[0]], T.yf[:, 0:CUT], ybank[0])
-    yb = pick("v", [yy[1]], T.yf[:, CUT:C], ybank[1])
+    yb = [pick("v", [yy[h]], blk(T.yf, 0, *PART["ab"[h]]), ybank[h]) for h in (0, 1)][1]
     need("y", tq[1])
     g.sync.dma_start(T.oc[:, :], T.q3[:, 0:C].bitcast(dt.uint8)).then_inc(T.sem.sto, 16)
+    need("s", tq[1])
     for k in range(4):
-        g.sync.dma_start(T.osc[4 * k:4 * k + 4, :], T.s3[32 * k:32 * k + 4, 0:C]).then_inc(T.sem.sto, 16)
-    need("s", ya)
-    g.scalar.dma_start(T.y[:, 0:CUT], T.yf[:, 0:CUT]).then_inc(T.sem.stc, 16)
+        (g.sync, g.scalar)[k % 2].dma_start(T.osc[4 * k:4 * k + 4, :], T.s3[32 * k:32 * k + 4, 0:C]).then_inc(T.sem[("sto", "stc")[k % 2]], 16)
     need("s", yb)
-    g.scalar.dma_start(T.y[:, CUT:C], T.yf[:, CUT:C]).then_inc(T.sem.stc, 16)
-    need("g", ("cv", cnt["v"]), ("cs", cnt["s"]), ("ct", cnt["t"]), ("cg", cnt["g"]), ("left", left), ("sto", 96), ("stc", 32))
+    g.scalar.dma_start(T.y[:, :], T.yf[:]).then_inc(T.sem.stc, 16)
+    need("g", ("cv", cnt["v"]), ("cs", cnt["s"]), ("ct", cnt["t"]), ("cg", cnt["g"]), ("left", left), ("sto", 64), ("stc", 48))

@@ -2,20 +2,38 @@ from concourse.mybir import dt, AluOpType, ActivationFunctionType
 
 C = 320
 W = 2 * C
-CUT = 160
+CUT = 192
 PART = {"": (0, C), "a": (0, CUT), "b": (CUT, C)}
-RADIX = [3, 3, 3, 3, 2]
+HALF = {"": (0, C), "a": (0, C // 2), "b": (C // 2, C)}
+THIRD = {"a": (0, 128), "b": (128, 256), "c": (256, C)}
+SHARE = {"": (0, C), "a": (0, 32), "b": (32, C)}
+SPLIT = {"": (0, C), "a": (0, 192), "b": (192, C)}
+LINKS = [(6, 3), (9, 3), (18, 9), (27, 9), (54, 27), (81, 27), (162, 81), (324, 162)]
+LAST, FAR = LINKS[-1][1], LINKS[-1][0]
+FUSED = 2
+DIRECT = (2, 3)
+SCANNED = (2,)
+HELD = 1
+HELDP = ["b"]
+OWN, AFTER = {0: 1, 2: 2, 3: 1, 1: 2}, {3: 0, 1: 2}
+FAR_LOW = -2.0 ** 90
 STEP = [1, 2, 4]
 BIG = 2.0 ** 24
 MID = 159
 LOW = -256.0
-DV = 112
 BF, F32, I32, U16 = "bfloat16", "float32", "int32", "uint16"
 
-ORDER = dict(v="lw g1 d1 g2 sb fl pb a0 a1 a3 a2 b0 b1 b2 b3 c0 c1 c2 c3a c3b za zb sx qv ex e1 h0b e2 e3 x0 e4 e5 x1 e6 e7 x2 x3a x3b ya yb",
-             s="w0 w1 w3 o0 t1 t2 w2 u3 u2 A0 A1 A2 A3 B0 B1 B2 B3 o1 o2 o3 h0a h1 h2 h3 l0 l1",
-             t="F0 F1 F3 F2 O0 O1 O2 O3 H0a H0b H1 H2 H3",
-             g=">a d0 >b")
+START = dict(v="gap z4 ki z0 ko uo kl z1 m8 scl big kf sc2 z2 cw qu d8 cx qup E0 ya yb md0 dw0 ms dw1 md1",
+             s="qus kk",
+             g="pi m16 kd0 dj kd1 kd2 iof")
+ORDER = dict(v="sga sgb mh T1a sc ml T1b s2 T1c E2 p0 p1 cp dp T1x z3 T2a dq E3 T3a L2 c3 L3 p3 k3 L6 d1_ L9 c9 k9a p9 E1 T18a L18 T27a L27 c27 k27a p27 "
+               "T54a L54 T81a L81 c81 k81a p81 T162a L162 c162 ca p162 ga fg dd cf cb st mn tt lw c324 g1 p324 fl sb sx pb pc "
+               "a0 a1 a3 a2 b0 b1 b3 b2 c0 c1 c3_ c2a c2b za zb "
+               "ex qv e1 h0b ek e3 x0 x2 e4 e5 x3 e6 e7 x1a x1b ya yb",
+             s="sfa sfb T1y T2b T3b o0 o2 T6 T9 o3 k9b T18b T27b o1 k27b T54b T81b w0 k81b T162b w1 bv T324 w3 "
+               "t1 w2a t2 w2b u3 u2 A0 A1 A3 A2 B0 B1 B3 B2 h0a h2 h3 h1 jb mf df l0 l1",
+             t="Sa Sb O0 O2 O3 O1 F0 F1 F3 F2 H0a H0b H2 H3 H1",
+             g=">q >s far0 far1 d0 d1 >a >b")
 
 SCRATCH = {}
 
@@ -25,13 +43,13 @@ def _sb(dtype, **kw):
         SCRATCH[k] = ("sbuf", [128, n], dtype)
 
 
-_sb(BF, xin=1280, uin=512, vin=512, e8=516, iot=C, iot2=W, kd=128, kk=C, sca=C, scb=C, scx=C, mm=C,
-    pp=3 * W, l2=2 * W, aw=2 * C, low=2 * C, ld=C, t1=C, t2=C, fl=C,
-    fw=1280, fd=W, fo=1280, hw=1280, tmp=W, z1=1280, z2=1280, y1=1280, y2=1280, z3=1280, xt=1280)
-_sb(F32, iof=C, dj=128, m16=20, kf=1, scl=1, sc2=1, thr=1, tiny=1, cw=20, cx=20, sf=C, sg=2 * C, ps=1008, pk=60, po=60,
-    sa=40, sb=40, so=40, ex=20, ed=20, l0w=20, l1w=20, lsf=2 * C, yf=C)
+_sb(BF, xin=1280, uin=512, vin=512, e8=516, kd=128, kk=C, sca=C, scb=C, scc=C, scd=C, sce=C, scx=C, mm=W, ps=992, pt=992, ex=20,
+    f1=W + 16, pp=2 * W, l2=2 * W, aw=2 * C, low=2 * C, ld=C, bv=C, fg=C, t1=C, t2=C, fl=C,
+    fw=1280, fd=W, fo=1280, hw=1280, tmp=3 * C, r1=2 * W, n1=2 * W, n2=2 * W, z1=1280, z2=1280, y1=1280, y2=1280, z3=1280, xt=1280)
+_sb(F32, iof=W, dm=W, dj=128, m16=20, kf=1, scl=1, sc2=1, big=1, kl=1, cw=20, cx=20, mid=20, sf=C, sg=C, pk=120, po=60,
+    so=60, dp=20, ga=20, mn=20, ed=20, l0w=20, l1w=20, lsf=2 * C, yf=C)
 _sb(I32, lai=20, lbi=20, pi=20, ki=1)
-_sb(U16, uo=8, ko=20, offs=20 * len(RADIX) + 20, lwo=20, l0o=20, l1o=20)
+_sb(U16, uo=8, ko=20, offs=140, lwo=20, l0o=20, l1o=20, dko=20, mso=20)
 _sb("float8_e4m3fn_x4", wq=512, qu=128, qup=128, qv=128, qe8=512, qz=C)
 _sb("uint8", wsq=512, su=128, sup=128, sv=128, se8=512, sz=C)
 for _i in range(4):
@@ -41,12 +59,12 @@ for _i in range(3):
     SCRATCH["lq%d" % _i] = ("sbuf", [128, C], "float8_e4m3fn_x4")
     SCRATCH["lp%d" % _i] = ("sbuf", [128, C], "uint8")
     for _k in ("ta", "tb", "la_", "lb_"):
-        SCRATCH["%s%d" % (_k, _i)] = ("sbuf", [128, 20], U16)
+        SCRATCH["%s%d" % (_k, _i)] = ("sbuf", [128, 40 if "b" in _k else 20], U16)
 SCRATCH["psa"] = ("psum", [128, 2048], F32)
 SCRATCH["psf"] = ("psum", [128, 1536], F32)
 SCRATCH["pss"] = ("psum", [128, 512], F32)
 
-SEMAPHORES = ["cv", "cs", "ct", "cg", "left", "ldx", "ldu", "ldv", "ldl", "ldw", "sto", "stc"]
+SEMAPHORES = ["cv", "cs", "ct", "cg", "left", "gone", "ldx", "ldu", "ldv", "ldl", "ldw", "sto", "stc"]
 SEMAPHORES += ["%s%d" % (k, i) for k in ("aq", "at", "ab") for i in range(3)]
 
 
@@ -56,26 +74,42 @@ def rank_program(g, core, T, topo):
         return
     N = len(T.cores)
     A = AluOpType
-    COPY, SIGN = ActivationFunctionType.Copy, ActivationFunctionType.Sign
+    COPY, SAME = ActivationFunctionType.Copy, ActivationFunctionType.Identity
     eng = {"v": g.vector, "s": g.scalar, "t": g.tensor, "g": g, "y": g.sync}
     cnt = {"v": 0, "s": 0, "t": 0, "g": 0}
-    seen = {}
+    seen = {k: {} for k in eng}
+    knew = {}
 
     def need(q, *toks):
-        most = {}
-        for name, n in toks:
-            most[name] = max(n, most.get(name, 0))
-        for name, n in most.items():
-            if seen.get((q, name), 0) < n:
-                eng[q].wait_ge(T.sem[name], n)
-                seen[(q, name)] = n
+        for tok in sorted(set(toks), key=lambda x: -len(knew.get(x, ()))):
+            if seen[q].get(tok[0], 0) < tok[1] and not any(y != tok and knew.get(y, {}).get(tok[0], 0) >= tok[1] for y in toks):
+                eng[q].wait_ge(T.sem[tok[0]], tok[1])
+                for name, n in knew.get(tok, {tok[0]: tok[1]}).items():
+                    seen[q][name] = max(n, seen[q].get(name, 0))
 
     def run(q, deps, fn, *a, **kw):
         need(q, *deps)
-        ins = fn(*a, **kw)
         cnt[q] += 1
-        ins.then_inc(T.sem["c" + q], 1)
-        return ("c" + q, cnt[q])
+        fn(*a, **kw).then_inc(T.sem["c" + q], 1)
+        tok = ("c" + q, cnt[q])
+        knew[tok] = {**knew.get(("c" + q, cnt[q] - 1), {}), **seen[q], tok[0]: tok[1]}
+        return tok
+
+    done = {}
+
+    def issue(order, calls, i=0):
+        before = dict(done)
+        todo = {k: [x for x, _, r in (y.partition("@") for y in order[k].split()) if x in calls and (not r or str(i) in r)] for k in order}
+        named = {x for k in todo for x in todo[k]}
+        for x in named:
+            done.pop(x, None)
+        while any(todo.values()):
+            for k in todo:
+                while todo[k] and all(y in done for y in calls[todo[k][0]][0] if y in named):
+                    x = todo[k].pop(0)
+                    deps, fn, a = calls[x]
+                    toks = [y if isinstance(y, tuple) else before.get(y[1:]) if y[0] == "^" else done.get(y) for y in deps]
+                    done[x] = fn(k, [y for y in toks if y], *a)
 
     V, S, TE = g.vector, g.scalar, g.tensor
 
@@ -94,10 +128,13 @@ def rank_program(g, core, T, topo):
     def mov(buf, b):
         return buf[:, 128 * b:128 * b + 128]
 
-    def bank(buf, b, n=C):
-        return buf[:, 512 * b:512 * b + n]
+    def bank(buf, b, lo=0, hi=C):
+        return buf[:, 512 * b + lo:512 * b + hi]
 
-    def off(k, lo=0, hi=C):
+    LISTS = sorted({1} | {a for n, a in LINKS}) + [FAR]
+
+    def off(a, lo=0, hi=C):
+        k = LISTS.index(a)
         return T.offs[:, 20 * k + lo // 16:20 * k + hi // 16]
 
     def pick(q, deps, out, in_, scale=None):
@@ -121,59 +158,71 @@ def rank_program(g, core, T, topo):
     def place(q, deps, out, ends):
         return run(q, deps, V.tensor_scalar, out, ends, T.scl[:, 0:1], MID + 0.25, A.mult, A.add)
 
+    calls = {}
+
+    def call(name, deps, fn, *a):
+        calls[name] = (deps, fn, a)
+
+    def vec(name, deps, fn, *a, **kw):
+        calls[name] = (deps, lambda q, deps: run(q, deps, fn, *a, **kw), ())
+
     g.scalar.dma_start(T.uin[:], T.u[:, :]).then_inc(T.sem.ldu, 16)
     g.sync.dma_start(T.xin[:], T.x[:, :]).then_inc(T.sem.ldx, 16)
     g.sync.dma_start(T.lai[:], T.la[:, :]).then_inc(T.sem.ldl, 16)
     g.scalar.dma_start(T.lbi[:], T.lb[:, :]).then_inc(T.sem.ldl, 16)
-    need("y", ("ldx", 16))
-    g.sync.dma_start(T.wq[:, 0:512].bitcast(dt.uint8), T.wc[:, :]).then_inc(T.sem.ldw, 16)
-    g.sync.dma_start(T.wsq[:, 0:512], T.ws[:, :]).then_inc(T.sem.ldw, 16)
-    g.sync.dma_start(T.vin[:], T.v[:, :]).then_inc(T.sem.ldv, 16)
 
     SMALL = {"allow_small_or_imprecise_dtypes": True}
-    k_pi = run("g", [], g.iota, T.pi[:], [[0, 20]], 0, 1)
-    k_m16 = run("g", [], g.iota, T.m16[:], [[16, 20]], 0, 0, **SMALL)
-    k_dj = run("g", [], g.iota, T.dj[:], [[1, 128]], 0, -1, **SMALL)
-    kk = run("g", [], g.iota, T.kd[:], [[0, 128]], 1, 0, **SMALL)
-    for fill, at in ((0.0, 0), (BIG, 1)):
-        kk = run("g", [kk], g.affine_select, T.kd[:], T.kd[:], [[1, 128]], A.not_equal, fill, -at, -1)
-    k_io = run("g", [], g.iota, T.iot2[:], [[1, C], [0, 2]], -MID, 0, **SMALL)
+    vec("pi", [], g.iota, T.pi[:], [[0, 20]], 0, 1)
+    vec("m16", [], g.iota, T.m16[:], [[16, 20]], 0, 0, **SMALL)
+    vec("dj", [], g.iota, T.dj[:], [[1, 128]], 0, -1, **SMALL)
+    vec("kd0", [], g.iota, T.kd[:], [[0, 128]], 1, 0, **SMALL)
+    for at, fill in enumerate((0.0, BIG)):
+        vec("kd%d" % (at + 1), ["kd%d" % at], g.affine_select, T.kd[:], T.kd[:], [[1, 128]], A.not_equal, fill, -at, -1)
+    vec("iof", [], g.iota, T.iof[:], [[1, W]], -C, 0, **SMALL)
+    vec("m8", [], V.memset, T.e8[:], 0.0)
+    vec("gap", [], V.memset, T.pp[:, 1:2 * W:2], LOW)
+    vec("ki", ["pi"], V.tensor_scalar, T.ki[:], T.pi[:, 0:1], 15, None, A.bitwise_and)
+    vec("ko", ["pi"], V.tensor_copy, T.ko[:], T.pi[:])
+    vec("uo", ["m16"], V.tensor_copy, T.uo[:], T.m16[:, 0:8])
+    fills = ((T.pk[:, 2:120:3], 1.0), (T.pk[:, 0:120:3], 0.0), (T.pt[:, 77:992:48], 0.0), (T.mm[:, 0:W:2], 0.0), (T.f1[:, 17:16 + W:2], 0.0))
+    for k, (view, value) in enumerate(fills):
+        vec("z%d" % k, [], V.memset, view, value)
+    ONE = T.pk[:, 2:3]
+    vec("kf", ["ki"], V.tensor_copy, T.kf[:], T.ki[:])
+    vec("kl", ["ki"], V.tensor_scalar, T.kl[:], T.ki[:], 15.0, None, A.is_equal)
+    for k, x, y in (("scl", 1.0, 1 / BIG), ("sc2", 2.0, 2 / BIG), ("big", 1.0, BIG)):
+        vec(k, ["kl"], V.tensor_scalar, T[k][:], T.kl[:], x - y, y, A.mult, A.add)
+    vec("cw", ["m16", "kf"], V.tensor_scalar, T.cw[:], T.m16[:], T.kf[:, 0:1], None, A.add)
+    vec("d8", ["dj", "m8"], V.tensor_scalar, T.e8[:, 3:515:4], T.dj[:], 0.0, 0.125, A.is_equal, A.mult)
+    vec("cx", ["cw", "big"], V.tensor_scalar, T.cx[:], T.cw[:], float(MID), T.big[:, 0:1], A.subtract, A.mult)
 
-    m8 = run("v", [], V.memset, T.e8[:], 0.0)
-    gap = run("v", [], V.memset, T.pp[:, 1:3 * W:2], LOW)
-    ki = run("v", [k_pi], V.tensor_scalar, T.ki[:], T.pi[:, 0:1], 15, None, A.bitwise_and)
-    ko = run("v", [k_pi], V.tensor_copy, T.ko[:], T.pi[:])
-    uo = run("v", [k_m16], V.tensor_copy, T.uo[:], T.m16[:, 0:8])
-    tiny = run("v", [], V.memset, T.tiny[:], 2.0 ** -100)
-    for view in (T.sa[:], T.pk[:], T.ps[:, 29:989:16]):
-        run("v", [], V.memset, view, 0.0)
-    kf = run("v", [ki], V.tensor_copy, T.kf[:], T.ki[:])
-    last = [(T.scl, 1.0, 1 / BIG), (T.sc2, 2.0, 2 / BIG), (T.thr, 0.5, BIG / 2)]
-    a = [run("v", [ki], V.tensor_scalar, buf[:], T.ki[:], 15.0, x - y, A.is_equal, A.mult) for buf, x, y in last]
-    cw = run("v", [k_m16, kf], V.tensor_scalar, T.cw[:], T.m16[:], T.kf[:, 0:1], None, A.add)
-    sc = [run("v", a, V.tensor_scalar, buf[:], buf[:], y, None, A.add) for buf, x, y in last][-1]
-    d8 = run("v", [k_dj, m8], V.tensor_scalar, T.e8[:, 3:515:4], T.dj[:], 0.0, 0.125, A.is_equal, A.mult)
-    a = run("v", [cw, sc], V.tensor_scalar, T.cx[:], T.cw[:], float(MID), T.thr[:, 0:1], A.subtract, A.mult)
+    vec("d1_", ["E%d" % b for b in range(4) if b != HELD], V.tensor_scalar, T.e8[:, 3:515:4], T.dj[:], 0.0, None, A.is_equal)
+    for b in range(4):
+        vec("E%d" % b, ["d1_" if b == HELD else "d8"], V.quantize_mx, mov(T.qe8, b), mov(T.se8, b), T.e8[:, 3 - b:515 - b])
+    for k, buf in enumerate((T.n1, T.r1)):
+        vec("far%d" % k, ["iof"], g.affine_select, buf[:, 1:2 * W:2], T.iof[:], [[0, W]], A.not_equal, FAR_LOW, 0, 0)
+    vec("qu", [("ldu", 16)], V.quantize_mx, T.qu[:, 0:128], T.su[:, 0:128], T.uin[:])
+    vec("qup", ["qu", "uo"], V.tensor_copy, T.qup[:, 0:128].bitcast(dt.uint32), T.qu[:, 0:128].bitcast(dt.uint32).indirect(T.uo[:, 0:8]))
+    vec("qus", ["qu", "uo"], S.activation, T.sup[:, 0:128], T.su[:, 0:128].indirect(T.uo[:, 0:8]), COPY)
+    call("kk", ["kd2", "ko"], pick, T.kk[:], T.kd[:, 0:128].indirect(T.ko[:, 0:20]))
+    for k in "ab":
+        call("y" + k, [("ldx", 16)], quant, T.q0, T.s0, T.xin, k)
+    DW, P, HI, LO = T.pk[:, 1:60:3], T.po[:, 2:60:3], T.ps[:, 61:992:48], T.ps[:, 77:992:48]
+    vec("dw0", [("ldl", 32)], V.tensor_tensor, DW, T.lai[:], T.lbi[:], A.subtract)
+    vec("md0", [("ldl", 32)], V.tensor_tensor, T.mid[:], T.lai[:], T.lbi[:], A.add)
+    vec("dw1", ["dw0", "scl"], V.tensor_scalar, DW, DW, T.scl[:, 0:1], None, A.mult)
+    call("ms", ["md0"], pick, T.mso[:], T.mid[:])
+    vec("md1", ["ms"], V.tensor_scalar, T.mid[:], T.mid[:], 0.5, 0.25, A.mult, A.add)
+    call("mh", ["md1"], pick, HI, T.mid[:])
+    vec("ml", ["mh"], V.tensor_tensor, LO, T.mid[:], HI, A.subtract)
+    vec("mf", ["ms", "iof", "z0"], S.activation, T.dm[:, 1:W:2], T.iof[:, 0:W].indirect(T.mso[:, 0:20]), SAME, scale=0.5, bias=ONE)
 
-    def unpacker(b):
-        return run("v", [d8], V.quantize_mx, mov(T.qe8, b), mov(T.se8, b), T.e8[:, 3 - b:515 - b])
+    def difference(dep):
+        vec("ek", [dep, "big"], V.tensor_scalar, T.dko[:], DW, T.big[:, 0:1], float(C), A.mult, A.add)
+        call("df", ["ek", "iof"], pick, T.dm[:, 0:W:2], T.iof[:, 0:W].indirect(T.dko[:, 0:20]))
 
-    unpacker(0)
-    run("v", [a], V.tensor_scalar, T.cx[:], T.cx[:], 2.0, None, A.mult)
-    a = run("v", [("ldu", 16)], V.quantize_mx, T.qu[:, 0:128], T.su[:, 0:128], T.uin[:])
-    unpacker(1)
-    qup = run("v", [a, uo], V.tensor_copy, T.qup[:, 0:128].bitcast(dt.uint32), T.qu[:, 0:128].bitcast(dt.uint32).indirect(T.uo[:, 0:8]))
-    qus = run("s", [a, uo], S.activation, T.sup[:, 0:128], T.su[:, 0:128].indirect(T.uo[:, 0:8]), COPY)
-    kk = pick("s", [kk, ko], T.kk[:], T.kd[:, 0:128].indirect(T.ko[:, 0:20]))
-    tq = [quant("v", [("ldx", 16)], T.q0, T.s0, T.xin, k) for k in "ab"]
-    DW, DWA, MIDL, P = T.pk[:, 2:60:3], T.pk[:, 2:3 * (CUT // 16):3], T.ps[:, 61:1008:48], T.po[:, 2:60:3]
-    a = run("v", [("ldl", 32)], V.tensor_tensor, DW, T.lai[:], T.lbi[:], A.subtract)
-    b = run("v", [("ldl", 32)], V.tensor_tensor, MIDL, T.lai[:], T.lbi[:], A.add)
-    unpacker(2)
-    a = run("v", [a], V.tensor_scalar, DW, DW, T.scl[:, 0:1], None, A.mult)
-    run("v", [b], V.tensor_scalar, MIDL, MIDL, 0.5, 0.25, A.mult, A.add)
-    qe8 = unpacker(3)
-    dw = run("v", [a], V.tensor_scalar, DWA, DWA, 0.5, None, A.mult)
+    issue(START, calls)
+    done["e1"] = done["dw1"]
 
     left = 0
     for i, d in enumerate(STEP):
@@ -185,145 +234,163 @@ def rank_program(g, core, T, topo):
         rid, pid, _ = topo.addr(dst)
         mask = topo.mask(core, dst)
         ne, na = len(topo.engines(core, dst)), len(topo.engines(src, core))
-
-        def send(dep, out, in_, sem):
-            need("g", dep)
-            g.remote_dma(out, in_, T.sem["%s%d" % (sem, i)], T.sem.left, pid, rid, mask)
-
-        send(tq[1], lq[:, 0:C].bitcast(dt.uint8), q[:, 0:C].bitcast(dt.uint8), "aq")
-        send(tq[1], lp[:, 0:C], s[:, 0:C], "aq")
-        if i == 0:
-            run("g", [], g.iota, T.iot[:], [[1, C]], -MID, 0, **SMALL)
-            k_if = run("g", [], g.iota, T.iof[:], [[1, C]], 0, 0, **SMALL)
-
-        sbank = [bank(T.pss, 0, CUT), bank(T.psf, 0, C - CUT)]
-        ts = [mm("t", [tq[h], qup, qus], sbank[h], T.qup[:, 0:128], T.sup[:, 0:128], q, s, "ab"[h]) for h in (0, 1)]
-        m = [run("s", [ts[0], tiny], S.activation, T.mm[:, 0:CUT], sbank[0], SIGN, bias=T.tiny[:, 0:1]),
-             run("v", [ts[1]], V.tensor_scalar, T.mm[:, CUT:C], sbank[1], 0.0, 0.5, A.is_ge, A.subtract)]
-        a = [scan("v", [m[h], kk], T.ps[:, 3 * lo:3 * hi:3], T.kk[:, lo:hi], T.mm[:, lo:hi]) for h, (lo, hi) in enumerate((PART["a"], PART["b"]))][1]
-        a = scan("v", [a, dw], T.po[:], T.pk[:], T.ps[:, 29:989:16])
-        o = run("v", [a], V.tensor_scalar, off(0), P, 2.0, 0.25, A.mult, A.subtract)
-        pick("v", [], T.sb[:, 1:40:2], P)
-        sf = [pick("s", [m[h]], blk(T.sf, 0, *PART["ab"[h]]), sbank[h]) for h in (0, 1)][1]
-
-        a, win = [o, k_io, gap], T.iot2[:, 0:W]
-        for k in range(3):
-            a = [pick(e, a, even(T.pp, k, lo, hi), win.indirect(off(0, lo, hi))) for e, lo, hi in (("v", 0, C // 2), ("s", C // 2, C))]
-            win = wide(T.pp, k)
-            if k == 0:
-                run("v", [], V.tensor_tensor, T.sa[:, 1:40:2], T.cw[:], P, A.subtract)
-        b = run("v", [], V.tensor_tensor_scan, wide(T.l2, 0), wide(T.pp, 0), wide(T.pp, 1), LOW, A.max, A.min)
-        a = scan("v", a, T.sca[:], T.kk[:], even(T.pp, 2))
-        lowt = run("v", [b], V.tensor_tensor_scan, wide(T.l2, 1), wide(T.l2, 0), wide(T.pp, 2), LOW, A.max, A.min)
-        ak = o = run("v", [a], V.tensor_scalar, off(1), w20(T.sca), T.sc2[:, 0:1], 2 * MID + 0.25, A.mult, A.add)
-        dup = pick("v", [lowt], T.ld[:], even(T.l2, 1))
-        link, low, n = wide(T.pp, 2), wide(T.l2, 1), 0
-        for k in range(1, len(RADIX)):
-            for j in range(RADIX[k] - 1):
-                spaced = k == 1 and j < RADIX[k] - 2
-                ak = pick("s", [ak, o], even(T.pp, 0) if spaced else blk(T.aw, n % 2), link.indirect(off(k)))
-                lowt = run("v", [lowt, o, dup], V.tensor_tensor, even(T.l2, 0) if spaced else blk(T.low, n % 2), low.indirect(off(k)), T.ld[:], A.min)
-                link, low = (wide(T.pp, 0), wide(T.l2, 0)) if spaced else (blk(T.aw, n % 2), blk(T.low, n % 2))
-                n += 1
-            dup = pick("s", [lowt], T.ld[:, DV:C], blk(T.low, (n - 1) % 2, DV, C))
-            a = scan("v", [ak], T.sca[:], T.kk[:], link)
-            pick("v", [lowt], T.ld[:, 0:DV], blk(T.low, (n - 1) % 2, 0, DV))
-            o = place("v", [a], off(k + 1), w20(T.sca))
-        far = off(len(RADIX))
-        a = run("v", [lowt, o, dup], V.tensor_tensor, blk(T.low, n % 2), low.indirect(far), T.ld[:], A.min)
-        a = scan("v", [a], T.sca[:], T.kk[:], blk(T.low, n % 2))
-        a = run("v", [a], V.tensor_tensor, T.sb[:, 0:40:2], w20(T.sca), T.cx[:], A.is_equal)
-        a = scan("v", [a], T.so[:], T.sa[:], T.sb[:])
-        tt = run("v", [a], V.tensor_scalar, ta[:, 0:20], T.so[:, 1:40:2], 0.125, None, A.add)
-
         at, ab = [("%s%d" % (k, i), na) for k in ("at", "ab")]
-        calls = {}
+        if i:
+            calls.clear()
 
-        def call(name, deps, fn, *a):
-            calls[name] = (deps, fn, a)
+        def send(k, deps, out, in_, sem, local):
+            need(k, *deps)
+            g.remote_dma(out, in_, T.sem["%s%d" % (sem, i)], T.sem[local], pid, rid, mask)
 
-        def vec(name, deps, fn, *a):
-            calls[name] = (deps, lambda q, deps: run(q, deps, fn, *a), ())
+        first = "left" if i else "gone"
+        call(">q", ["^yb"], send, lq[:, 0:C].bitcast(dt.uint8), q[:, 0:C].bitcast(dt.uint8), "aq", first)
+        call(">s", ["^yb"], send, lp[:, 0:C], s[:, 0:C], "aq", first)
+        call(">a", ["tt"], send, la[:, 0:20], ta[:, 0:20], "at", "left")
+        call(">b", ["pb", "pc"], send, lb[:, 0:40 if SCANNED else 20], tb[:, 0:40 if SCANNED else 20], "ab", "left")
+        left += (4 if i else 2) * ne
+        if i == 0:
+            need("y", ("gone", 2 * ne))
+            g.sync.dma_start(T.wq[:, 0:512].bitcast(dt.uint8), T.wc[:, :]).then_inc(T.sem.ldw, 16)
+            g.sync.dma_start(T.wsq[:, 0:512], T.ws[:, :]).then_inc(T.sem.ldw, 16)
+            g.sync.dma_start(T.vin[:], T.v[:, :]).then_inc(T.sem.ldv, 16)
+            vec("qv", [("ldv", 16)], V.quantize_mx, T.qv[:, 0:128], T.sv[:, 0:128], T.vin[:])
+
+        sbank = {"a": bank(T.pss, 0, 0, CUT), "b": bank(T.psf, 0, 0, C - CUT)}
+        for k in "ab":
+            lo, hi = PART[k]
+            call("S" + k, ["^y" + k, "qup", "qus"], mm, sbank[k], T.qup[:, 0:128], T.sup[:, 0:128], q, s, k)
+            vec("sg" + k, ["S" + k], V.tensor_scalar, T.mm[:, 2 * lo + 1:2 * hi:2], sbank[k], 0.0, 0.5, A.is_ge, A.subtract)
+            call("sf" + k, ["sg" + k], pick, blk(T.sf, 0, lo, hi), sbank[k])
+        call("sc", ["sga", "sgb", "kk"], scan, T.ps[:, 0:3 * C:3], T.kk[:], T.mm[:, 1:W:2])
+        call("s2", ["sc", "^e1", "ml", "z0", "z1"], scan, T.po[:], T.pk[:, 0:60], T.ps[:, 45:992:16])
+        vec("p1", ["s2"], V.tensor_scalar, off(1), P, 2.0, 0.25, A.mult, A.subtract)
+        if i:
+            for h, (lo, hi) in THIRD.items():
+                call("T1" + h, ["sga", "^df", "mf", "z3"] + ["sgb"] * (hi > CUT), scan, T.f1[:, 15 + 2 * lo:15 + 2 * hi], T.mm[:, 2 * lo:2 * hi], T.dm[:, 2 * lo:2 * hi])
+        else:
+            call("p0", ["s2"], pick, T.lwo[:], P)
+            vec("T1x", ["p0", "iof"], V.tensor_scalar, T.f1[:, 16:16 + C:2], T.iof[:, C // 2:W].indirect(T.lwo[:, 0:10]), 1.0, None, A.add)
+            vec("T1y", ["p0", "iof"], S.activation, T.f1[:, 16 + C:16 + W:2], T.iof[:, C // 2:W].indirect(T.lwo[:, 10:20]), SAME, bias=ONE)
+        vec("cp", ["s2"], V.tensor_scalar, T.pt[:, 61:992:48], P, MID + 0.25, None, A.subtract)
+        vec("dp", ["s2", "cw"], V.tensor_tensor, T.dp[:], T.cw[:], P, A.subtract)
+        vec("dq", ["dp"], V.tensor_scalar, T.dp[:], T.dp[:], T.scl[:, 0:1], None, A.mult)
+
+        one = T.f1[:, 16:16 + W]
+        for k, win in ((2, one), (3, wide(T.pp, 0))):
+            for h, (lo, hi) in HALF.items():
+                call("T%d%s" % (k, h), ["p1", "gap"] + ["T%d%s" % (k - 1, y) for y in "abcxy"], pick, even(T.pp, k - 2, lo, hi), win.indirect(off(1, lo, hi)))
+        for k, x in ((2, T.f1[:, 16:15 + W]), (3, T.l2[:, 0:W - 1])):
+            vec("L%d" % k, ["L%d" % (k - 1), "T%da" % k, "T%db" % k, "z4"], V.tensor_tensor_scan, T.l2[:, W * (k - 2):W * (k - 1) - 1], x,
+                T.pp[:, W * (k - 2):W * (k - 1) - 1], LOW, A.max, A.min)
+        call("c3", ["T3a", "T3b"], scan, T.sca[:], T.kk[:], even(T.pp, 1))
+        vec("p3", ["c3", "sc2"], V.tensor_scalar, off(3), w20(T.sca), T.sc2[:, 0:1], 2 * MID + 0.25, A.mult, A.add)
+        link, low = wide(T.pp, 1), T.l2[:, W:2 * W - 1]
+        call("k3", ["L3"], pick, T.ld[:], even(T.l2, 1))
+        for j, (n, a) in enumerate(LINKS):
+            m = n - a
+            to = (lambda x, y, lo, hi: even(x, 0, lo, hi)) if j == 0 else (lambda x, y, lo, hi: blk(y, j % 2, lo, hi))
+            for h, (lo, hi) in SHARE.items():
+                call("T%d%s" % (n, h), ["T%d%s" % (m, k) for k in SHARE] + ["p%d" % a, "L3"], pick, to(T.pp, T.aw, lo, hi), link.indirect(off(a, lo, hi)))
+            vec("L%d" % n, ["L%d" % m, "p%d" % a] + ["k%d%s" % (a, k) for k in SPLIT], V.tensor_tensor, to(T.l2, T.low, 0, C), low.indirect(off(a)), T.ld[:], A.min)
+            link, low = (wide(T.pp, 0), T.l2[:, 0:W - 1]) if j == 0 else (blk(T.aw, j % 2), blk(T.low, j % 2))
+            if n in LISTS:
+                ends = T.scc if n == FAR else T.sca
+                call("c%d" % n, ["T%d%s" % (n, k) for k in SHARE], scan, ends[:], T.kk[:], link)
+                call("p%d" % n, ["c%d" % n], place, off(n), w20(ends))
+                for h, (lo, hi) in SPLIT.items():
+                    call("k%d%s" % (n, h), ["L%d" % n], pick, blk(T.ld, 0, lo, hi), blk(T.low, j % 2, lo, hi))
+            if n == LAST:
+                vec("fg", ["L%d" % n, "p%d" % n], V.tensor_tensor, T.fg[:], low.indirect(off(n)), T.iof[:, C - MID:W - MID], A.is_equal)
+                call("bv", ["L%d" % n, "p%d" % n], pick, T.bv[:], low.indirect(off(n)))
+                call("ca", ["L%d" % n], scan, T.sce[:], T.kk[:], low)
+        vec("ga", ["ca", "cx"], V.tensor_tensor, T.ga[:], w20(T.sce), T.cx[:], A.is_ge)
+        vec("dd", ["ga", "dq"], V.tensor_tensor, T.pk[:, 61:120:3], T.ga[:], T.dp[:], A.mult)
+        call("cf", ["fg"], scan, T.pt[:, 0:3 * C:3], T.kk[:], T.fg[:])
+        call("st", ["cf", "dd", "cp", "z2"], scan, T.so[:], T.pk[:, 60:120], T.pt[:, 45:992:16])
+        vec("tt", ["st"], V.tensor_scalar, ta[:, 0:20], T.so[:, 2:60:3], MID + 0.125, None, A.add)
 
         for b in range(4):
-            call("F%d" % b, [("aq%d" % i, 2 * na), qe8], mm, bank(T.psa, b), mov(T.qe8, b), mov(T.se8, b), lq, lp, "")
-            call("w%d" % b, ["F%d" % b], pick, blk(T.fw, b), bank(T.psa, b))
-            call("O%d" % b, [qe8, "o%d" % (b - 2)], mm, bank(T.psf, 1 + b % 2), mov(T.qe8, b), mov(T.se8, b), q, s, "")
-            call("o%d" % b, ["O%d" % b], pick, blk(T.fo, b), bank(T.psf, 1 + b % 2), 8.0)
+            call("F%d" % b, [("aq%d" % i, 2 * na), "E%d" % b], mm, bank(T.psa, b), mov(T.qe8, b), mov(T.se8, b), lq, lp, "")
+            call("O%d" % b, ["E%d" % b, "^yb"] + ["o%d%s" % (AFTER[b], h) for h in HALF if b in AFTER], mm, bank(T.psf, OWN[b]), mov(T.qe8, b), mov(T.se8, b), q, s, "")
+            for h, (lo, hi) in HALF.items():
+                call("w%d%s" % (b, h), ["F%d" % b], pick, blk(T.fw, b, lo, hi), bank(T.psa, b, lo, hi), 0.125 if b == HELD else None)
+                call("o%d%s" % (b, h), ["O%d" % b], pick, blk(T.fo, b, lo, hi), bank(T.psf, OWN[b], lo, hi), 1.0 if b == HELD else 8.0)
         for b in (0, 1):
-            call("d%d" % b, ["w%d" % b], pick, blk(T.fd, b), blk(T.fw, b))
-        call("t1", [tt, k_if], pick, T.t1[:], T.iot[:, 0:C].indirect(ta[:, 0:20]))
+            call("d%d" % b, ["w%d%s" % (b, h) for h in HALF], pick, blk(T.fd, b), blk(T.fw, b))
+        vec("t1", ["tt"], S.activation, T.t1[:], T.iof[:, C // 2:W].indirect(ta[:, 0:20]), SAME, bias=ONE)
         call("t2", ["t1"], pick, T.t2[:], T.t1[:, 0:C].indirect(ta[:, 0:20]))
         call("sb", ["t2"], scan, T.scb[:], T.kk[:], T.t2[:])
         call("pb", ["sb"], place, tb[:, 0:20], w20(T.scb))
-        call("lw", [], place, T.lwo[:], w20(T.sca))
-        call("g1", ["lw", sf], pick, blk(T.sg, 0), T.sf[:, 0:C].indirect(T.lwo[:, 0:20]))
-        call("g2", ["g1"], pick, blk(T.sg, 1), blk(T.sg, 0).indirect(far))
-        vec("fl", ["g2"], V.tensor_tensor, T.fl[:], blk(T.sg, 1).indirect(far), T.sf[:], A.is_gt)
+        vec("pc", ["sb"], V.tensor_scalar, tb[:, 20:40], w20(T.scb), T.sc2[:, 0:1], 2 * MID + 0.25, A.mult, A.add)
+        call("cb", ["bv"], scan, T.scd[:], T.kk[:], T.bv[:])
+        vec("mn", ["cb", "ca"], V.tensor_tensor, T.mn[:], w20(T.sce), w20(T.scd), A.min)
+        call("lw", ["mn"], place, T.lwo[:], T.mn[:])
+        call("g1", ["lw", "sfa", "sfb"], pick, T.sg[:], T.sf[:, 0:C].indirect(T.lwo[:, 0:20]))
+        vec("fl", ["g1", "p%d" % FAR], V.tensor_tensor, T.fl[:], T.sg[:, 0:C].indirect(off(FAR)), T.sf[:], A.is_le)
         call("sx", ["fl"], scan, T.scx[:], T.kk[:], T.fl[:])
-        vec("ex", ["sx"], V.tensor_scalar, T.ex[:], w20(T.scx), T.thr[:, 0:1], 0.5, A.is_le, A.subtract)
+        vec("ex", ["sx"], V.tensor_scalar, T.ex[:], w20(T.scx), T.sc2[:, 0:1], 1.0, A.mult, A.subtract)
         vec("e1", ["ex"], V.tensor_tensor, DW, DW, T.ex[:], A.mult)
         if i < 2:
-            vec("e2", ["e1"], V.tensor_scalar, DW, DW, 2.0, None, A.mult)
+            difference("e1")
         else:
-            vec("e2", ["e1"], V.tensor_scalar, DWA, DWA, 2.0, None, A.mult)
-            vec("e3", ["e2"], V.tensor_scalar, T.ed[:], DW, T.thr[:, 0:1], 2.0, A.mult, A.mult)
-            vec("e4", ["e3"], V.tensor_tensor, T.l0w[:], MIDL, T.ed[:], A.add)
-            vec("e5", ["e3"], V.tensor_tensor, T.l1w[:], MIDL, T.ed[:], A.subtract)
+            vec("e3", ["e1"], V.tensor_scalar, T.ed[:], DW, T.big[:, 0:1], 0.5, A.mult, A.mult)
+            vec("e4", ["e3"], V.tensor_tensor, T.l0w[:], T.mid[:], T.ed[:], A.add)
+            vec("e5", ["e3"], V.tensor_tensor, T.l1w[:], T.mid[:], T.ed[:], A.subtract)
             call("e6", ["e4"], pick, T.l0o[:], T.l0w[:])
             call("e7", ["e5"], pick, T.l1o[:], T.l1w[:])
-            call("l0", ["e6"], pick, blk(T.lsf, 0), T.iof[:, 0:C].indirect(T.l0o[:, 0:20]))
-            call("l1", ["e7"], pick, blk(T.lsf, 1), T.iof[:, 0:C].indirect(T.l1o[:, 0:20]))
-        if i == 0:
-            vec("qv", [("ldv", 16)], V.quantize_mx, T.qv[:, 0:128], T.sv[:, 0:128], T.vin[:])
+            call("l0", ["e6"], pick, blk(T.lsf, 0), T.iof[:, C:W].indirect(T.l0o[:, 0:20]))
+            call("l1", ["e7"], pick, blk(T.lsf, 1), T.iof[:, C:W].indirect(T.l1o[:, 0:20]))
         for b in range(4):
-            if b < 2:
-                vec("a%d" % b, [at, "d%d" % b], V.tensor_tensor, blk(T.z1, b), blk(T.fw, b).indirect(la[:, 0:20]), blk(T.fd, b), A.add)
+            ws = ["w%d%s" % (b, h) for h in HALF]
+            z1 = even(T.n1, b - 2) if b in SCANNED else blk(T.z1, b)
+            if b < FUSED:
+                vec("a%d" % b, [at, "d%d" % b], V.tensor_tensor, z1, blk(T.fw, b).indirect(la[:, 0:20]), blk(T.fd, b), A.add)
             else:
-                call("u%d" % b, [at, "w%d" % b], pick, blk(T.tmp, b - 2), blk(T.fw, b).indirect(la[:, 0:20]))
-                vec("a%d" % b, ["u%d" % b], V.tensor_tensor, blk(T.z1, b), blk(T.tmp, b - 2), bank(T.psa, b), A.add)
-            call("A%d" % b, ["a%d" % b], pick, blk(T.y1, b), blk(T.z1, b).indirect(la[:, 0:20]))
-            vec("b%d" % b, ["A%d" % b], V.tensor_tensor, blk(T.z2, b), blk(T.y1, b).indirect(la[:, 0:20]), blk(T.z1, b), A.add)
-            call("B%d" % b, [ab, "b%d" % b], pick, blk(T.y2, b), blk(T.z2, b).indirect(lb[:, 0:20]))
+                call("u%d" % b, [at] + ws, pick, blk(T.tmp, b - 1), blk(T.fw, b).indirect(la[:, 0:20]))
+                vec("a%d" % b, ["u%d" % b], V.tensor_tensor, z1, blk(T.tmp, b - 1), bank(T.psa, b), A.add)
+            if b in SCANNED:
+                call("A%d" % b, ["a%d" % b, ab, "far0", "far1"], pick, even(T.r1, b - 2), wide(T.n1, b - 2).indirect(lb[:, 20:40]))
+                vec("b%d" % b, ["A%d" % b], V.tensor_tensor_scan, wide(T.n2, b - 2), wide(T.r1, b - 2), wide(T.n1, b - 2), FAR_LOW, A.max, A.add)
+            elif b in DIRECT:
+                call("A%d" % b, ["a%d" % b], pick, blk(T.y1, b), z1)
+                vec("b%d" % b, ["A%d" % b, ab], V.tensor_tensor, blk(T.z2, b), blk(T.y1, b).indirect(lb[:, 0:20]), z1, A.add)
+            else:
+                call("A%d" % b, ["a%d" % b], pick, blk(T.y1, b), z1.indirect(la[:, 0:20]))
+                vec("b%d" % b, ["A%d" % b], V.tensor_tensor, blk(T.z2, b), blk(T.y1, b).indirect(la[:, 0:20]), z1, A.add)
+            call("B%d" % b, [ab, "b%d" % b], pick, blk(T.y2, b), wide(T.n2, b - 2).indirect(lb[:, 20:40]) if b in SCANNED else blk(T.z2, b).indirect(lb[:, 0:20]))
             for k, (lo, hi) in PART.items():
-                vec("c%d%s" % (b, k), [ab, "B%d" % b], V.tensor_tensor, T.z3[:, 4 * lo + b:4 * hi:4], blk(T.y2, b).indirect(lb[:, lo // 16:hi // 16]),
-                    blk(T.z2, b, lo, hi), A.add)
-        for k, hb in (("a", bank(T.psa, 0, CUT)), ("b", bank(T.pss, 0, C - CUT))):
-            call("z" + k, ["c2", "c3" + k], quant, T.qz, T.sz, T.z3, k)
+                vec("c%d%s" % (b, k or "_" * (b == 3)), [ab, "B%d" % b], V.tensor_tensor, T.z3[:, 4 * lo + b:4 * hi:4],
+                    blk(T.y2, b).indirect(lb[:, lo // 16:hi // 16]), even(T.n2, b - 2, lo, hi) if b in SCANNED else blk(T.z2, b, lo, hi), A.add)
+        for k, hb in (("a", bank(T.psa, 0, 0, CUT)), ("b", bank(T.pss, 0, 0, C - CUT))):
+            call("z" + k, ["c0", "c1", "c2", "c3_", "c2" + k, "c3" + k], quant, T.qz, T.sz, T.z3, k)
             call("H0" + k, ["z" + k, ("ldw", 32)], mm, hb, mov(T.wq, 0), mov(T.wsq, 0), T.qz, T.sz, k)
             call("h0" + k, ["H0" + k], pick, blk(T.hw, 0, *PART[k]), hb, 0.03125)
-            call("y" + k, ["x2", "x3" + k], quant, T["q%d" % (i + 1)], T["s%d" % (i + 1)], T.xt, k)
+            call("y" + k, ["x%d%s" % (b, h) for b in range(4) for h in ("", k)], quant, T["q%d" % (i + 1)], T["s%d" % (i + 1)], T.xt, k)
         for b in range(4):
             call("H%d" % b, ["zb"], mm, bank(T.psa, b), mov(T.wq, b), mov(T.wsq, b), T.qz, T.sz, "")
             call("h%d" % b, ["H%d" % b], pick, blk(T.hw, b), bank(T.psa, b), 0.03125)
             for k, (lo, hi) in PART.items():
-                vec("x%d%s" % (b, k), ["o%d" % b, "h%d" % b, "h%da" % b, "h%db" % b], V.tensor_tensor, T.xt[:, 4 * lo + b:4 * hi:4],
-                    blk(T.hw, b).indirect(ta[:, lo // 16:hi // 16]), blk(T.fo, b, lo, hi), A.add)
-        order = {k: [x for x in ORDER[k].split() if x in calls] for k in "vstg"}
-        done = {x: ("c" + k, cnt[k] + 1 + j) for k in "vstg" for j, x in enumerate(order[k])}
-        sends = {">a": (tt, la[:, 0:20], ta[:, 0:20], "at"), ">b": (done["pb"], lb[:, 0:20], tb[:, 0:20], "ab")}
-        for k in "vstg":
-            for x in ORDER[k].split():
-                if x in sends:
-                    send(*sends[x])
-                elif x in calls:
-                    deps, fn, a = calls[x]
-                    fn(k, [done.get(y, y) for y in deps if y in done or isinstance(y, tuple)], *a)
-        left += 4 * ne
-        dw, tq = done["e2"], [done["ya"], done["yb"]]
+                if b == HELD and k in HELDP:
+                    call("j" + k, ["h%d" % b], pick, blk(T.tmp, 0, lo, hi), blk(T.hw, b).indirect(ta[:, lo // 16:hi // 16]))
+                    vec("x%d%s" % (b, k), ["j", "j" + k, "O%d" % b], V.tensor_tensor, T.xt[:, 4 * lo + b:4 * hi:4], blk(T.tmp, 0, lo, hi), bank(T.psf, OWN[b], lo, hi), A.add)
+                else:
+                    vec("x%d%s" % (b, k), ["%s%d%s" % (y, b, h) for y in "oh" for h in HALF], V.tensor_tensor, T.xt[:, 4 * lo + b:4 * hi:4],
+                        blk(T.hw, b).indirect(ta[:, lo // 16:hi // 16]), blk(T.fo, b, lo, hi), A.add)
+        issue(ORDER, calls, i)
         if i == 0:
-            qv = done["qv"]
+            gone = 2 * ne
 
-    ybank = [bank(T.psa, 0, CUT), bank(T.psa, 1, C - CUT)]
-    yy = [mm("t", [tq[h], qv], ybank[h], T.qv[:, 0:128], T.sv[:, 0:128], T.q3, T.s3, "ab"[h]) for h in (0, 1)]
-    need("y", done["l1"])
-    g.sync.dma_start(T.ls[:, :], T.lsf[0:128:16, :]).then_inc(T.sem.sto, 16)
+    tq = [done["ya"], done["yb"]]
+    ybank = [bank(T.psa, 0, 0, CUT), bank(T.psa, 1, 0, C - CUT)]
+    yy = [mm("t", [tq[h], done["qv"]], ybank[h], T.qv[:, 0:128], T.sv[:, 0:128], T.q3, T.s3, "ab"[h]) for h in (0, 1)]
     yb = [pick("v", [yy[h]], blk(T.yf, 0, *PART["ab"[h]]), ybank[h]) for h in (0, 1)][1]
     need("y", tq[1])
     g.sync.dma_start(T.oc[:, :], T.q3[:, 0:C].bitcast(dt.uint8)).then_inc(T.sem.sto, 16)
     need("s", tq[1])
     for k in range(4):
         (g.sync, g.scalar)[k % 2].dma_start(T.osc[4 * k:4 * k + 4, :], T.s3[32 * k:32 * k + 4, 0:C]).then_inc(T.sem[("sto", "stc")[k % 2]], 16)
+    need("y", done["l1"])
+    g.sync.dma_start(T.ls[:, :], T.lsf[0:128:16, :]).then_inc(T.sem.sto, 16)
     need("s", yb)
     g.scalar.dma_start(T.y[:, :], T.yf[:]).then_inc(T.sem.stc, 16)
-    need("g", ("cv", cnt["v"]), ("cs", cnt["s"]), ("ct", cnt["t"]), ("cg", cnt["g"]), ("left", left), ("sto", 64), ("stc", 48))
+    need("g", ("cv", cnt["v"]), ("cs", cnt["s"]), ("ct", cnt["t"]), ("cg", cnt["g"]), ("left", left), ("gone", gone), ("sto", 64), ("stc", 48))

@@ -6,15 +6,20 @@ CUT = 192
 PART = {"": (0, C), "a": (0, CUT), "b": (CUT, C)}
 HALF = {"": (0, C), "a": (0, C // 2), "b": (C // 2, C)}
 THIRD = {"a": (0, 128), "b": (128, 256), "c": (256, C)}
-SHARE = {"": (0, C), "a": (0, 32), "b": (32, C)}
-SPLIT = {"": (0, C), "a": (0, 192), "b": (192, C)}
-LINKS = [(6, 3), (9, 3), (18, 9), (27, 9), (54, 27), (81, 27), (162, 81), (324, 162)]
+EARLY = {"a": (0, 160), "b": (160, C)}
+FINAL = {"a": (0, 160), "b": (160, C)}
+SHARE = [{"": (0, C), "a": (0, n), "b": (n, C)} for n in (64, 64)]
+SPLIT = {"": (0, C), "a": (0, 256), "b": (256, C)}
+LINKS = [(6, 3), (9, 3), (18, 9), (27, 9), (54, 27), (81, 27), (162, 81), (243, 81), (324, 81)]
 LAST, FAR = LINKS[-1][1], LINKS[-1][0]
 FUSED = 2
-DIRECT = (2, 3)
-SCANNED = (2,)
+LEVEL2, LEVEL3 = "ddss", "hhhh"
+SPARE = 2
 HELD = 1
+LOADS = [("s", "u", "ldu"), ("y", "x", "ldx"), ("y", "la", "ldl"), ("s", "lb", "ldl")]
 HELDP = ["b"]
+TWICE = True
+ENOUGH = 162
 OWN, AFTER = {0: 1, 2: 2, 3: 1, 1: 2}, {3: 0, 1: 2}
 FAR_LOW = -2.0 ** 90
 STEP = [1, 2, 4]
@@ -23,17 +28,17 @@ MID = 159
 LOW = -256.0
 BF, F32, I32, U16 = "bfloat16", "float32", "int32", "uint16"
 
-START = dict(v="gap z4 ki z0 ko uo kl z1 m8 scl big kf sc2 z2 cw qu d8 cx qup E0 ya yb md0 dw0 ms dw1 md1",
-             s="qus kk",
-             g="pi m16 kd0 dj kd1 kd2 iof")
-ORDER = dict(v="sga sgb mh T1a sc ml T1b s2 T1c E2 p0 p1 cp dp T1x z3 T2a dq E3 T3a L2 c3 L3 p3 k3 L6 d1_ L9 c9 k9a p9 E1 T18a L18 T27a L27 c27 k27a p27 "
-               "T54a L54 T81a L81 c81 k81a p81 T162a L162 c162 ca p162 ga fg dd cf cb st mn tt lw c324 g1 p324 fl sb sx pb pc "
-               "a0 a1 a3 a2 b0 b1 b3 b2 c0 c1 c3_ c2a c2b za zb "
-               "ex qv e1 h0b ek e3 x0 x2 e4 e5 x3 e6 e7 x1a x1b ya yb",
-             s="sfa sfb T1y T2b T3b o0 o2 T6 T9 o3 k9b T18b T27b o1 k27b T54b T81b w0 k81b T162b w1 bv T324 w3 "
-               "t1 w2a t2 w2b u3 u2 A0 A1 A3 A2 B0 B1 B3 B2 h0a h2 h3 h1 jb mf df l0 l1",
+START = dict(v="m8 gap z4 ki z0 ko uo kl z1 scl big kf sc2 z2 cw qu cx qup E0 ya yb md0 dw0 mh md1 dw1",
+             s="qus kk cy",
+             g="pi kd0 m16 kd1 d8 kd2 iof")
+ORDER = dict(v="sga sgb ml sca scb T1b ms s2 E2 T1a p0@0 z3 T1c p1 T1x dp T2a E3 T3a L2a L2b c3 L3a p3 L3b k3a z5 k3b L6a L6b d1_ L9 c9 E1 p9 "
+               "q0 T18a L18 T27a L27 c27 q2 p27 q3 q4 T54a L54 T81a L81 c81 k81a p81 L162 Ua ca bva ga T243a cb eq mn r4 st lw r2 tt "
+               "nf fc d1 c324 s3 p324 pc pb fl a0 a1 a3 sx a2 b0 b3 b1 b2 c0 c3_ c1 c2a c2b za zb "
+               "e1 e3 qv ek h0b e4 e5 x0 x2 e6 x3a x1a x3b x1b ya yb",
+             s="sfb cp T1y T2b sfa T3b o0 o2 T6 T9 o3a k9 T18b T27b q1 o3b k27 T54b T81b o1 k81b w0 T162 Ub w1b bvb T243b w1a T324 g1 "
+               "w3 w2 u3 u2 A0 A3 A2 B0 B3 B1 B2 ex h0a h2 h3 h1 jb mf df l1",
              t="Sa Sb O0 O2 O3 O1 F0 F1 F3 F2 H0a H0b H2 H3 H1",
-             g=">q >s far0 far1 d0 d1 >a >b")
+             g=">q >s far0 far1 d0 >a >b A1")
 
 SCRATCH = {}
 
@@ -43,13 +48,13 @@ def _sb(dtype, **kw):
         SCRATCH[k] = ("sbuf", [128, n], dtype)
 
 
-_sb(BF, xin=1280, uin=512, vin=512, e8=516, kd=128, kk=C, sca=C, scb=C, scc=C, scd=C, sce=C, scx=C, mm=W, ps=992, pt=992, ex=20,
-    f1=W + 16, pp=2 * W, l2=2 * W, aw=2 * C, low=2 * C, ld=C, bv=C, fg=C, t1=C, t2=C, fl=C,
-    fw=1280, fd=W, fo=1280, hw=1280, tmp=3 * C, r1=2 * W, n1=2 * W, n2=2 * W, z1=1280, z2=1280, y1=1280, y2=1280, z3=1280, xt=1280)
-_sb(F32, iof=W, dm=W, dj=128, m16=20, kf=1, scl=1, sc2=1, big=1, kl=1, cw=20, cx=20, mid=20, sf=C, sg=C, pk=120, po=60,
-    so=60, dp=20, ga=20, mn=20, ed=20, l0w=20, l1w=20, lsf=2 * C, yf=C)
-_sb(I32, lai=20, lbi=20, pi=20, ki=1)
-_sb(U16, uo=8, ko=20, offs=140, lwo=20, l0o=20, l1o=20, dko=20, mso=20)
+_sb(BF, xin=1280, uin=512, vin=512, e8=516, kd=128, kk=C, sca=C, scb=C, scc=C, scd=C, sce=C, scx=C, mm=W, ps=992, ex=20,
+    f1=W + 16, pp=2 * W, l2=2 * W, aw=2 * C, low=2 * C, ld=C, bv=C, fl=C,
+    fw=1280, fd=W, fo=1280, hw=1280, tmp=3 * C, sp=12 * W, z1=1280, z2=1280, y1=1280, y2=1280, z3=1280, xt=1280)
+_sb(F32, iof=W, dm=W, m16=20, kf=1, scl=1, sc2=1, big=1, kl=1, cw=20, cx=20, mid=20, sf=C, sg=C, pk=120, po=60,
+    pu=164, s3_=80, cy=20, so=60, pt=60, mn=20, ed=20, lw_=40, lsf=2 * C, yf=C)
+_sb(I32, lain=20, lbin=20, pi=20, ki=1)
+_sb(U16, uo=8, ko=20, offs=140, lwo=20, pwo=20, lo_=40, dko=20, mso=20)
 _sb("float8_e4m3fn_x4", wq=512, qu=128, qup=128, qv=128, qe8=512, qz=C)
 _sb("uint8", wsq=512, su=128, sup=128, sv=128, se8=512, sz=C)
 for _i in range(4):
@@ -104,6 +109,7 @@ def rank_program(g, core, T, topo):
         for x in named:
             done.pop(x, None)
         while any(todo.values()):
+            assert any(v and all(y in done for y in calls[v[0]][0] if y in named) for v in todo.values()), "an order in which queues wait for each other"
             for k in todo:
                 while todo[k] and all(y in done for y in calls[todo[k][0]][0] if y in named):
                     x = todo[k].pop(0)
@@ -144,6 +150,11 @@ def rank_program(g, core, T, topo):
             return run(q, deps, V.tensor_copy, out, in_) if q == "v" else run(q, deps, S.activation, out, in_, COPY)
         return run(q, deps, V.tensor_scalar, out, in_, scale, None, A.mult) if q == "v" else run(q, deps, S.activation, out, in_, COPY, scale=scale)
 
+    def affine(q, deps, out, in_, scale, bias):
+        if q == "v":
+            return run(q, deps, V.tensor_scalar, out, in_, scale, bias, A.mult, A.add)
+        return run(q, deps, S.activation, out, in_, SAME, scale=scale, bias=bias)
+
     def mm(q, deps, out, side, plane, codes, scales, part):
         lo, hi = PART[part]
         return run(q, deps, TE.matmul_mx, out, side, plane, codes[:, lo:hi], scales[:, lo:hi], True, True)
@@ -158,6 +169,9 @@ def rank_program(g, core, T, topo):
     def place(q, deps, out, ends):
         return run(q, deps, V.tensor_scalar, out, ends, T.scl[:, 0:1], MID + 0.25, A.mult, A.add)
 
+    def meet(name, parts=HALF, lo=0, hi=C):
+        return [name + h for h, (x, y) in parts.items() if x < hi and lo < y]
+
     calls = {}
 
     def call(name, deps, fn, *a):
@@ -166,25 +180,23 @@ def rank_program(g, core, T, topo):
     def vec(name, deps, fn, *a, **kw):
         calls[name] = (deps, lambda q, deps: run(q, deps, fn, *a, **kw), ())
 
-    g.scalar.dma_start(T.uin[:], T.u[:, :]).then_inc(T.sem.ldu, 16)
-    g.sync.dma_start(T.xin[:], T.x[:, :]).then_inc(T.sem.ldx, 16)
-    g.sync.dma_start(T.lai[:], T.la[:, :]).then_inc(T.sem.ldl, 16)
-    g.scalar.dma_start(T.lbi[:], T.lb[:, :]).then_inc(T.sem.ldl, 16)
+    for k, name, sem in LOADS:
+        eng[k].dma_start(T[name + "in"][:], T[name][:, :]).then_inc(T.sem[sem], 16)
 
     SMALL = {"allow_small_or_imprecise_dtypes": True}
     vec("pi", [], g.iota, T.pi[:], [[0, 20]], 0, 1)
     vec("m16", [], g.iota, T.m16[:], [[16, 20]], 0, 0, **SMALL)
-    vec("dj", [], g.iota, T.dj[:], [[1, 128]], 0, -1, **SMALL)
     vec("kd0", [], g.iota, T.kd[:], [[0, 128]], 1, 0, **SMALL)
     for at, fill in enumerate((0.0, BIG)):
         vec("kd%d" % (at + 1), ["kd%d" % at], g.affine_select, T.kd[:], T.kd[:], [[1, 128]], A.not_equal, fill, -at, -1)
     vec("iof", [], g.iota, T.iof[:], [[1, W]], -C, 0, **SMALL)
     vec("m8", [], V.memset, T.e8[:], 0.0)
-    vec("gap", [], V.memset, T.pp[:, 1:2 * W:2], LOW)
+    vec("gap", [], V.memset, T.pp[:, 1:(LINKS[0][1] - 1) * W:2], LOW)
     vec("ki", ["pi"], V.tensor_scalar, T.ki[:], T.pi[:, 0:1], 15, None, A.bitwise_and)
     vec("ko", ["pi"], V.tensor_copy, T.ko[:], T.pi[:])
     vec("uo", ["m16"], V.tensor_copy, T.uo[:], T.m16[:, 0:8])
-    fills = ((T.pk[:, 2:120:3], 1.0), (T.pk[:, 0:120:3], 0.0), (T.pt[:, 77:992:48], 0.0), (T.mm[:, 0:W:2], 0.0), (T.f1[:, 17:16 + W:2], 0.0))
+    fills = ((T.pk[:, 2:60:3], 1.0), (T.pk[:, 0:120:3], 0.0), (T.pt[:, 1:60:3], 0.0), (T.mm[:, 0:W:2], 0.0), (T.f1[:, 17:16 + W:2], 0.0),
+             (T.pu[:, 0:164:4], 0.0))
     for k, (view, value) in enumerate(fills):
         vec("z%d" % k, [], V.memset, view, value)
     ONE = T.pk[:, 2:3]
@@ -193,14 +205,24 @@ def rank_program(g, core, T, topo):
     for k, x, y in (("scl", 1.0, 1 / BIG), ("sc2", 2.0, 2 / BIG), ("big", 1.0, BIG)):
         vec(k, ["kl"], V.tensor_scalar, T[k][:], T.kl[:], x - y, y, A.mult, A.add)
     vec("cw", ["m16", "kf"], V.tensor_scalar, T.cw[:], T.m16[:], T.kf[:, 0:1], None, A.add)
-    vec("d8", ["dj", "m8"], V.tensor_scalar, T.e8[:, 3:515:4], T.dj[:], 0.0, 0.125, A.is_equal, A.mult)
+    vec("d8", ["m8"], g.affine_select, T.e8[:, 3:515:4], T.e8[:, 3:515:4], [[1, 128]], A.not_equal, 0.125, 0, -1)
     vec("cx", ["cw", "big"], V.tensor_scalar, T.cx[:], T.cw[:], float(MID), T.big[:, 0:1], A.subtract, A.mult)
 
-    vec("d1_", ["E%d" % b for b in range(4) if b != HELD], V.tensor_scalar, T.e8[:, 3:515:4], T.dj[:], 0.0, None, A.is_equal)
+    call("cy", ["cw"], affine, T.cy[:], T.cw[:], 1.0, -float(MID))
+    vec("d1_", ["E%d" % b for b in range(4) if b != HELD], V.tensor_scalar, T.e8[:, 3:515:4], T.e8[:, 3:515:4], 8.0, None, A.mult)
     for b in range(4):
         vec("E%d" % b, ["d1_" if b == HELD else "d8"], V.quantize_mx, mov(T.qe8, b), mov(T.se8, b), T.e8[:, 3 - b:515 - b])
-    for k, buf in enumerate((T.n1, T.r1)):
-        vec("far%d" % k, ["iof"], g.affine_select, buf[:, 1:2 * W:2], T.iof[:], [[0, W]], A.not_equal, FAR_LOW, 0, 0)
+    keys = [("1", b) for b in range(4) if LEVEL2[b] == "s"] + [("2", b) for b in range(4) if LEVEL2[b] != "s" and LEVEL3[b] != "h"]
+    fars = ["far%d" % k for k in range((len(keys) + SPARE + 1) // 2)]
+    for k, name in enumerate(fars):
+        vec(name, ["iof"], g.affine_select, T.sp[:, 2 * W * k + 1:2 * W * (k + 1):2], T.iof[:], [[0, W]], A.not_equal, FAR_LOW, 0, 0)
+    keys += [("2", b) for b in range(4) if LEVEL2[b] == "s"]
+    slot = {x: k + SPARE for k, x in enumerate(keys)}
+    scans = [x for x in ORDER["v"].split() if x in ["b%d" % b for b in range(4) if LEVEL2[b] == "s"] + ["c%d" % b for b in range(4) if LEVEL3[b] == "s"]]
+
+    def spare(name):
+        k = scans.index(name)
+        return k % SPARE, fars + scans[max(k - SPARE, 0):max(k - SPARE + 1, 0)]
     vec("qu", [("ldu", 16)], V.quantize_mx, T.qu[:, 0:128], T.su[:, 0:128], T.uin[:])
     vec("qup", ["qu", "uo"], V.tensor_copy, T.qup[:, 0:128].bitcast(dt.uint32), T.qu[:, 0:128].bitcast(dt.uint32).indirect(T.uo[:, 0:8]))
     vec("qus", ["qu", "uo"], S.activation, T.sup[:, 0:128], T.su[:, 0:128].indirect(T.uo[:, 0:8]), COPY)
@@ -208,21 +230,21 @@ def rank_program(g, core, T, topo):
     for k in "ab":
         call("y" + k, [("ldx", 16)], quant, T.q0, T.s0, T.xin, k)
     DW, P, HI, LO = T.pk[:, 1:60:3], T.po[:, 2:60:3], T.ps[:, 61:992:48], T.ps[:, 77:992:48]
-    vec("dw0", [("ldl", 32)], V.tensor_tensor, DW, T.lai[:], T.lbi[:], A.subtract)
-    vec("md0", [("ldl", 32)], V.tensor_tensor, T.mid[:], T.lai[:], T.lbi[:], A.add)
+    vec("dw0", [("ldl", 32)], V.tensor_tensor, DW, T.lain[:], T.lbin[:], A.subtract)
+    vec("md0", [("ldl", 32)], V.tensor_tensor, T.ed[:], T.lain[:], T.lbin[:], A.add)
     vec("dw1", ["dw0", "scl"], V.tensor_scalar, DW, DW, T.scl[:, 0:1], None, A.mult)
-    call("ms", ["md0"], pick, T.mso[:], T.mid[:])
-    vec("md1", ["ms"], V.tensor_scalar, T.mid[:], T.mid[:], 0.5, 0.25, A.mult, A.add)
-    call("mh", ["md1"], pick, HI, T.mid[:])
-    vec("ml", ["mh"], V.tensor_tensor, LO, T.mid[:], HI, A.subtract)
+    call("ms", ["md0"], pick, T.mso[:], T.ed[:])
+    call("md1", ["md0"], affine, T.mid[:], T.ed[:], 0.5, 0.25)
+    call("mh", ["md0"], affine, HI, T.ed[:], 0.5, 0.25)
+    vec("ml", ["mh", "md1"], V.tensor_tensor, LO, T.mid[:], HI, A.subtract)
     vec("mf", ["ms", "iof", "z0"], S.activation, T.dm[:, 1:W:2], T.iof[:, 0:W].indirect(T.mso[:, 0:20]), SAME, scale=0.5, bias=ONE)
 
     def difference(dep):
         vec("ek", [dep, "big"], V.tensor_scalar, T.dko[:], DW, T.big[:, 0:1], float(C), A.mult, A.add)
         call("df", ["ek", "iof"], pick, T.dm[:, 0:W:2], T.iof[:, 0:W].indirect(T.dko[:, 0:20]))
 
+    difference("dw1")
     issue(START, calls)
-    done["e1"] = done["dw1"]
 
     left = 0
     for i, d in enumerate(STEP):
@@ -246,7 +268,7 @@ def rank_program(g, core, T, topo):
         call(">q", ["^yb"], send, lq[:, 0:C].bitcast(dt.uint8), q[:, 0:C].bitcast(dt.uint8), "aq", first)
         call(">s", ["^yb"], send, lp[:, 0:C], s[:, 0:C], "aq", first)
         call(">a", ["tt"], send, la[:, 0:20], ta[:, 0:20], "at", "left")
-        call(">b", ["pb", "pc"], send, lb[:, 0:40 if SCANNED else 20], tb[:, 0:40 if SCANNED else 20], "ab", "left")
+        call(">b", ["pb", "pc"], send, lb[:, 0:40], tb[:, 0:40], "ab", "left")
         left += (4 if i else 2) * ne
         if i == 0:
             need("y", ("gone", 2 * ne))
@@ -261,52 +283,62 @@ def rank_program(g, core, T, topo):
             call("S" + k, ["^y" + k, "qup", "qus"], mm, sbank[k], T.qup[:, 0:128], T.sup[:, 0:128], q, s, k)
             vec("sg" + k, ["S" + k], V.tensor_scalar, T.mm[:, 2 * lo + 1:2 * hi:2], sbank[k], 0.0, 0.5, A.is_ge, A.subtract)
             call("sf" + k, ["sg" + k], pick, blk(T.sf, 0, lo, hi), sbank[k])
-        call("sc", ["sga", "sgb", "kk"], scan, T.ps[:, 0:3 * C:3], T.kk[:], T.mm[:, 1:W:2])
-        call("s2", ["sc", "^e1", "ml", "z0", "z1"], scan, T.po[:], T.pk[:, 0:60], T.ps[:, 45:992:16])
+        for k, (lo, hi) in PART.items():
+            call("sc" + k, ["sga", "kk"] + ["sgb"] * (hi > CUT), scan, T.ps[:, 3 * lo:3 * hi:3], T.kk[:, lo:hi], T.mm[:, 2 * lo + 1:2 * hi:2])
+        call("s2", ["sc", "sca", "scb", "^e1", "dw1", "ml", "z0", "z1"], scan, T.po[:], T.pk[:, 0:60], T.ps[:, 45:992:16])
         vec("p1", ["s2"], V.tensor_scalar, off(1), P, 2.0, 0.25, A.mult, A.subtract)
-        if i:
+        if i or "df" in START["s"] + START["v"]:
             for h, (lo, hi) in THIRD.items():
                 call("T1" + h, ["sga", "^df", "mf", "z3"] + ["sgb"] * (hi > CUT), scan, T.f1[:, 15 + 2 * lo:15 + 2 * hi], T.mm[:, 2 * lo:2 * hi], T.dm[:, 2 * lo:2 * hi])
         else:
-            call("p0", ["s2"], pick, T.lwo[:], P)
-            vec("T1x", ["p0", "iof"], V.tensor_scalar, T.f1[:, 16:16 + C:2], T.iof[:, C // 2:W].indirect(T.lwo[:, 0:10]), 1.0, None, A.add)
-            vec("T1y", ["p0", "iof"], S.activation, T.f1[:, 16 + C:16 + W:2], T.iof[:, C // 2:W].indirect(T.lwo[:, 10:20]), SAME, bias=ONE)
-        vec("cp", ["s2"], V.tensor_scalar, T.pt[:, 61:992:48], P, MID + 0.25, None, A.subtract)
-        vec("dp", ["s2", "cw"], V.tensor_tensor, T.dp[:], T.cw[:], P, A.subtract)
-        vec("dq", ["dp"], V.tensor_scalar, T.dp[:], T.dp[:], T.scl[:, 0:1], None, A.mult)
+            vec("T1x", ["p0", "iof"], V.tensor_scalar, T.f1[:, 16:16 + C:2], T.iof[:, C // 2:W].indirect(T.pwo[:, 0:10]), 1.0, None, A.add)
+            vec("T1y", ["p0", "iof"], S.activation, T.f1[:, 16 + C:16 + W:2], T.iof[:, C // 2:W].indirect(T.pwo[:, 10:20]), SAME, bias=ONE)
+        call("p0", ["s2"], pick, T.pwo[:], P)
+        call("cp", ["s2"], affine, T.pt[:, 2:60:3], P, 1.0, -MID - 0.25)
+        vec("dp", ["s2", "cw"], V.tensor_tensor, T.pk[:, 62:120:3], T.cw[:], P, A.subtract)
 
-        one = T.f1[:, 16:16 + W]
-        for k, win in ((2, one), (3, wide(T.pp, 0))):
+        F = LINKS[0][1]
+        link = low = T.f1[:, 16:15 + W]
+        for k in range(2, F + 1):
+            for h, (lo, hi) in EARLY.items():
+                call("T%d%s" % (k, h), ["p1", "gap"] + ["T%d%s" % (k - 1, y) for y in "abcxy"], pick, even(T.pp, k - 2, lo, hi), link.indirect(off(1, lo, hi)))
+            link = T.pp[:, W * (k - 2):W * (k - 1) - 1]
             for h, (lo, hi) in HALF.items():
-                call("T%d%s" % (k, h), ["p1", "gap"] + ["T%d%s" % (k - 1, y) for y in "abcxy"], pick, even(T.pp, k - 2, lo, hi), win.indirect(off(1, lo, hi)))
-        for k, x in ((2, T.f1[:, 16:15 + W]), (3, T.l2[:, 0:W - 1])):
-            vec("L%d" % k, ["L%d" % (k - 1), "T%da" % k, "T%db" % k, "z4"], V.tensor_tensor_scan, T.l2[:, W * (k - 2):W * (k - 1) - 1], x,
-                T.pp[:, W * (k - 2):W * (k - 1) - 1], LOW, A.max, A.min)
-        call("c3", ["T3a", "T3b"], scan, T.sca[:], T.kk[:], even(T.pp, 1))
-        vec("p3", ["c3", "sc2"], V.tensor_scalar, off(3), w20(T.sca), T.sc2[:, 0:1], 2 * MID + 0.25, A.mult, A.add)
-        link, low = wide(T.pp, 1), T.l2[:, W:2 * W - 1]
-        call("k3", ["L3"], pick, T.ld[:], even(T.l2, 1))
+                x = T.f1[:, 16 + 2 * lo:15 + 2 * hi] if k == 2 else T.l2[:, W * (1 - k % 2) + 2 * lo:W * (1 - k % 2) + 2 * hi - 1]
+                vec("L%d%s" % (k, h), meet("L%d" % (k - 1), HALF, lo, hi) + ["T%da" % k, "T%db" % k, "z4"], V.tensor_tensor_scan,
+                    T.l2[:, W * (k % 2) + 2 * lo:W * (k % 2) + 2 * hi - 1], x, T.pp[:, W * (k - 2) + 2 * lo:W * (k - 2) + 2 * hi - 1], LOW, A.max, A.min)
+            low = T.l2[:, W * (k % 2):W * (k % 2 + 1) - 1]
+        call("c%d" % F, ["T%da" % F, "T%db" % F], scan, T.sca[:], T.kk[:], even(T.pp, F - 2))
+        vec("p%d" % F, ["c%d" % F, "sc2"], V.tensor_scalar, off(F), w20(T.sca), T.sc2[:, 0:1], 2 * MID + 0.25, A.mult, A.add)
+        for h, (lo, hi) in HALF.items():
+            call("k%d%s" % (F, h), meet("L%d" % F, HALF, lo, hi), pick, blk(T.ld, 0, lo, hi), even(T.l2, F % 2, lo, hi))
         for j, (n, a) in enumerate(LINKS):
             m = n - a
-            to = (lambda x, y, lo, hi: even(x, 0, lo, hi)) if j == 0 else (lambda x, y, lo, hi: blk(y, j % 2, lo, hi))
-            for h, (lo, hi) in SHARE.items():
-                call("T%d%s" % (n, h), ["T%d%s" % (m, k) for k in SHARE] + ["p%d" % a, "L3"], pick, to(T.pp, T.aw, lo, hi), link.indirect(off(a, lo, hi)))
-            vec("L%d" % n, ["L%d" % m, "p%d" % a] + ["k%d%s" % (a, k) for k in SPLIT], V.tensor_tensor, to(T.l2, T.low, 0, C), low.indirect(off(a)), T.ld[:], A.min)
-            link, low = (wide(T.pp, 0), T.l2[:, 0:W - 1]) if j == 0 else (blk(T.aw, j % 2), blk(T.low, j % 2))
+            for h, (lo, hi) in SHARE[j % 2].items():
+                call("T%d%s" % (n, h), meet("T%d" % m) + ["p%d" % a] + meet("L2"), pick, T.f1[:, 16 + 2 * lo:16 + 2 * hi:2] if j == 0 else blk(T.aw, j % 2, lo, hi),
+                     link.indirect(off(a, lo, hi)))
+            for h, (lo, hi) in HALF.items():
+                vec("L%d%s" % (n, h), meet("L%d" % m) + ["p%d" % a] + meet("k%d" % a, HALF if a == F else SPLIT, lo, hi), V.tensor_tensor,
+                    even(T.l2, 1 - F % 2, lo, hi) if j == 0 else blk(T.low, j % 2, lo, hi), low.indirect(off(a, lo, hi)), blk(T.ld, 0, lo, hi), A.min)
+            link, low = (T.f1[:, 16:15 + W], T.l2[:, W * (1 - F % 2):W * (2 - F % 2) - 1]) if j == 0 else (blk(T.aw, j % 2), blk(T.low, j % 2))
             if n in LISTS:
                 ends = T.scc if n == FAR else T.sca
-                call("c%d" % n, ["T%d%s" % (n, k) for k in SHARE], scan, ends[:], T.kk[:], link)
+                call("c%d" % n, meet("T%d" % n), scan, ends[:], T.kk[:], link)
                 call("p%d" % n, ["c%d" % n], place, off(n), w20(ends))
                 for h, (lo, hi) in SPLIT.items():
-                    call("k%d%s" % (n, h), ["L%d" % n], pick, blk(T.ld, 0, lo, hi), blk(T.low, j % 2, lo, hi))
-            if n == LAST:
-                vec("fg", ["L%d" % n, "p%d" % n], V.tensor_tensor, T.fg[:], low.indirect(off(n)), T.iof[:, C - MID:W - MID], A.is_equal)
-                call("bv", ["L%d" % n, "p%d" % n], pick, T.bv[:], low.indirect(off(n)))
-                call("ca", ["L%d" % n], scan, T.sce[:], T.kk[:], low)
-        vec("ga", ["ca", "cx"], V.tensor_tensor, T.ga[:], w20(T.sce), T.cx[:], A.is_ge)
-        vec("dd", ["ga", "dq"], V.tensor_tensor, T.pk[:, 61:120:3], T.ga[:], T.dp[:], A.mult)
-        call("cf", ["fg"], scan, T.pt[:, 0:3 * C:3], T.kk[:], T.fg[:])
-        call("st", ["cf", "dd", "cp", "z2"], scan, T.so[:], T.pk[:, 60:120], T.pt[:, 45:992:16])
+                    call("k%d%s" % (n, h), meet("L%d" % n, HALF, lo, hi), pick, blk(T.ld, 0, lo, hi), blk(T.low, j % 2, lo, hi))
+            if n == ENOUGH:
+                for h, (lo, hi) in FINAL.items():
+                    if TWICE:
+                        call("U" + h, meet("L%d" % n), pick, blk(T.ld, 0, lo, hi), low.indirect(off(a, lo, hi)))
+                        call("bv" + h, ["Ua", "Ub"], pick, blk(T.bv, 0, lo, hi), T.ld[:, 0:C].indirect(off(a, lo, hi)))
+                    else:
+                        call("bv" + h, meet("L%d" % n) + ["p%d" % LAST], pick, blk(T.bv, 0, lo, hi), low.indirect(off(LAST, lo, hi)))
+                call("ca", meet("L%d" % n), scan, T.sce[:], T.kk[:], low)
+        call("cb", ["bva", "bvb"], scan, T.scd[:], T.kk[:], T.bv[:])
+        vec("ga", ["ca", "cx"], V.tensor_tensor, T.pk[:, 61:120:3], w20(T.sce), T.cx[:], A.is_ge)
+        vec("eq", ["cb", "cx"], V.tensor_tensor, T.pt[:, 0:60:3], w20(T.scd), T.cx[:], A.is_equal)
+        call("st", ["eq", "ga", "dp", "cp", "z2"], scan, T.so[:], T.pk[:, 60:120], T.pt[:])
         vec("tt", ["st"], V.tensor_scalar, ta[:, 0:20], T.so[:, 2:60:3], MID + 0.125, None, A.add)
 
         for b in range(4):
@@ -317,50 +349,60 @@ def rank_program(g, core, T, topo):
                 call("o%d%s" % (b, h), ["O%d" % b], pick, blk(T.fo, b, lo, hi), bank(T.psf, OWN[b], lo, hi), 1.0 if b == HELD else 8.0)
         for b in (0, 1):
             call("d%d" % b, ["w%d%s" % (b, h) for h in HALF], pick, blk(T.fd, b), blk(T.fw, b))
-        vec("t1", ["tt"], S.activation, T.t1[:], T.iof[:, C // 2:W].indirect(ta[:, 0:20]), SAME, bias=ONE)
-        call("t2", ["t1"], pick, T.t2[:], T.t1[:, 0:C].indirect(ta[:, 0:20]))
-        call("sb", ["t2"], scan, T.scb[:], T.kk[:], T.t2[:])
-        call("pb", ["sb"], place, tb[:, 0:20], w20(T.scb))
-        vec("pc", ["sb"], V.tensor_scalar, tb[:, 20:40], w20(T.scb), T.sc2[:, 0:1], 2 * MID + 0.25, A.mult, A.add)
-        call("cb", ["bv"], scan, T.scd[:], T.kk[:], T.bv[:])
+        PW, LEADS = T.pt[:, 2:60:3], T.so[:, 1:60:3]
+        times, plus = [T.pu[:, k:80:4] for k in range(4)], [T.pu[:, 83 + k:163:4] for k in range(4)]
+        call("q0", ["T2a", "T2b"], scan, T.scb[:], T.kk[:], even(T.pp, 0))
+        call("q1", ["q0", "z5"], pick, plus[2], w20(T.scb), T.scl[:, 0:1])
+        vec("q2", ["q1", "cp"], V.tensor_tensor, times[2], PW, plus[2], A.subtract)
+        vec("q3", ["cp", "z5"], V.tensor_scalar, times[1], PW, 0.5, T.big[:, 0:1], A.subtract, A.mult)
+        vec("q4", ["cp", "z5"], V.tensor_scalar, plus[0], PW, 0.5, T.big[:, 0:1], A.add, A.mult)
+        vec("r2", ["mn", "q3"], V.tensor_tensor, times[1], T.mn[:], times[1], A.is_ge)
+        vec("r4", ["cb", "q4"], V.tensor_tensor, plus[0], w20(T.scd), plus[0], A.is_le)
+        call("nf", ["st"], affine, times[3], LEADS, -1.0, 1.0)
+        vec("fc", ["st", "cy"], V.tensor_tensor, plus[3], LEADS, T.cy[:], A.mult)
+        call("s3", ["r2", "r4", "nf", "fc", "q2"], scan, T.s3_[:], T.pu[:, 0:80], T.pu[:, 83:163])
+        vec("pb", ["s3"], V.tensor_scalar, tb[:, 0:20], T.s3_[:, 3:80:4], MID + 0.25, None, A.add)
+        vec("pc", ["s3"], V.tensor_scalar, tb[:, 20:40], T.s3_[:, 3:80:4], 2.0, 2 * MID + 0.25, A.mult, A.add)
         vec("mn", ["cb", "ca"], V.tensor_tensor, T.mn[:], w20(T.sce), w20(T.scd), A.min)
         call("lw", ["mn"], place, T.lwo[:], T.mn[:])
         call("g1", ["lw", "sfa", "sfb"], pick, T.sg[:], T.sf[:, 0:C].indirect(T.lwo[:, 0:20]))
         vec("fl", ["g1", "p%d" % FAR], V.tensor_tensor, T.fl[:], T.sg[:, 0:C].indirect(off(FAR)), T.sf[:], A.is_le)
         call("sx", ["fl"], scan, T.scx[:], T.kk[:], T.fl[:])
-        vec("ex", ["sx"], V.tensor_scalar, T.ex[:], w20(T.scx), T.sc2[:, 0:1], 1.0, A.mult, A.subtract)
+        call("ex", ["sx"], affine, T.ex[:], w20(T.scx), T.sc2[:, 0:1], -1.0)
         vec("e1", ["ex"], V.tensor_tensor, DW, DW, T.ex[:], A.mult)
         if i < 2:
             difference("e1")
         else:
             vec("e3", ["e1"], V.tensor_scalar, T.ed[:], DW, T.big[:, 0:1], 0.5, A.mult, A.mult)
-            vec("e4", ["e3"], V.tensor_tensor, T.l0w[:], T.mid[:], T.ed[:], A.add)
-            vec("e5", ["e3"], V.tensor_tensor, T.l1w[:], T.mid[:], T.ed[:], A.subtract)
-            call("e6", ["e4"], pick, T.l0o[:], T.l0w[:])
-            call("e7", ["e5"], pick, T.l1o[:], T.l1w[:])
-            call("l0", ["e6"], pick, blk(T.lsf, 0), T.iof[:, C:W].indirect(T.l0o[:, 0:20]))
-            call("l1", ["e7"], pick, blk(T.lsf, 1), T.iof[:, C:W].indirect(T.l1o[:, 0:20]))
+            vec("e4", ["e3"], V.tensor_tensor, T.lw_[:, 0:20], T.mid[:], T.ed[:], A.add)
+            vec("e5", ["e3"], V.tensor_tensor, T.lw_[:, 20:40], T.mid[:], T.ed[:], A.subtract)
+            call("e6", ["e4", "e5"], pick, T.lo_[:], T.lw_[:])
+            call("l1", ["e6"], pick, T.lsf[:], T.iof[:, C:W].indirect(T.lo_[:, 0:40]))
         for b in range(4):
             ws = ["w%d%s" % (b, h) for h in HALF]
-            z1 = even(T.n1, b - 2) if b in SCANNED else blk(T.z1, b)
+            two, three = LEVEL2[b], LEVEL3[b]
+            spaced = two == "s" or three != "h"
+            z1 = even(T.sp, slot["1", b]) if two == "s" else blk(T.z1, b)
+            z2 = (lambda lo, hi: even(T.sp, slot["2", b], lo, hi)) if spaced else (lambda lo, hi: blk(T.z2, b, lo, hi))
             if b < FUSED:
                 vec("a%d" % b, [at, "d%d" % b], V.tensor_tensor, z1, blk(T.fw, b).indirect(la[:, 0:20]), blk(T.fd, b), A.add)
             else:
                 call("u%d" % b, [at] + ws, pick, blk(T.tmp, b - 1), blk(T.fw, b).indirect(la[:, 0:20]))
                 vec("a%d" % b, ["u%d" % b], V.tensor_tensor, z1, blk(T.tmp, b - 1), bank(T.psa, b), A.add)
-            if b in SCANNED:
-                call("A%d" % b, ["a%d" % b, ab, "far0", "far1"], pick, even(T.r1, b - 2), wide(T.n1, b - 2).indirect(lb[:, 20:40]))
-                vec("b%d" % b, ["A%d" % b], V.tensor_tensor_scan, wide(T.n2, b - 2), wide(T.r1, b - 2), wide(T.n1, b - 2), FAR_LOW, A.max, A.add)
-            elif b in DIRECT:
+            if two == "s":
+                k, deps = spare("b%d" % b)
+                call("A%d" % b, ["a%d" % b, ab] + deps, pick, even(T.sp, k), wide(T.sp, slot["1", b]).indirect(lb[:, 20:40]))
+                vec("b%d" % b, ["A%d" % b], V.tensor_tensor_scan, wide(T.sp, slot["2", b]), wide(T.sp, k), wide(T.sp, slot["1", b]), FAR_LOW, A.max, A.add)
+            elif two == "d":
                 call("A%d" % b, ["a%d" % b], pick, blk(T.y1, b), z1)
-                vec("b%d" % b, ["A%d" % b, ab], V.tensor_tensor, blk(T.z2, b), blk(T.y1, b).indirect(lb[:, 0:20]), z1, A.add)
+                vec("b%d" % b, ["A%d" % b, ab], V.tensor_tensor, z2(0, C), blk(T.y1, b).indirect(lb[:, 0:20]), z1, A.add)
             else:
                 call("A%d" % b, ["a%d" % b], pick, blk(T.y1, b), z1.indirect(la[:, 0:20]))
-                vec("b%d" % b, ["A%d" % b], V.tensor_tensor, blk(T.z2, b), blk(T.y1, b).indirect(la[:, 0:20]), z1, A.add)
-            call("B%d" % b, [ab, "b%d" % b], pick, blk(T.y2, b), wide(T.n2, b - 2).indirect(lb[:, 20:40]) if b in SCANNED else blk(T.z2, b).indirect(lb[:, 0:20]))
+                vec("b%d" % b, ["A%d" % b], V.tensor_tensor, z2(0, C), blk(T.y1, b).indirect(la[:, 0:20]), z1, A.add)
+            call("B%d" % b, [ab, "b%d" % b], pick, blk(T.y2, b), wide(T.sp, slot["2", b]).indirect(lb[:, 20:40]) if spaced else blk(T.z2, b).indirect(lb[:, 0:20]))
             for k, (lo, hi) in PART.items():
                 vec("c%d%s" % (b, k or "_" * (b == 3)), [ab, "B%d" % b], V.tensor_tensor, T.z3[:, 4 * lo + b:4 * hi:4],
-                    blk(T.y2, b).indirect(lb[:, lo // 16:hi // 16]), even(T.n2, b - 2, lo, hi) if b in SCANNED else blk(T.z2, b, lo, hi), A.add)
+                    blk(T.y2, b).indirect(lb[:, lo // 16:hi // 16]), z2(lo, hi), A.add)
         for k, hb in (("a", bank(T.psa, 0, 0, CUT)), ("b", bank(T.pss, 0, 0, C - CUT))):
             call("z" + k, ["c0", "c1", "c2", "c3_", "c2" + k, "c3" + k], quant, T.qz, T.sz, T.z3, k)
             call("H0" + k, ["z" + k, ("ldw", 32)], mm, hb, mov(T.wq, 0), mov(T.wsq, 0), T.qz, T.sz, k)

from concourse.mybir import dt, AluOpType, ActivationFunctionType

C = 320
W = 2 * C
CUT = 192
PART = {"": (0, C), "a": (0, CUT), "b": (CUT, C)}
HALF = {"": (0, C), "a": (0, C // 2), "b": (C // 2, C)}
THIRD = {"a": (0, 128), "b": (128, 256), "c": (256, C)}
EARLY = {"a": (0, 160), "b": (160, C)}
FINAL = {"a": (0, 160), "b": (160, C)}
SHARE = [{"": (0, C), "a": (0, n), "b": (n, C)} for n in (64, 64)]
SPLIT = {"": (0, C), "a": (0, 256), "b": (256, C)}
LINKS = [(6, 3), (9, 3), (18, 9), (27, 9), (54, 27), (81, 27), (162, 81), (243, 81), (324, 81)]
LAST, FAR = LINKS[-1][1], LINKS[-1][0]
FUSED = 2
LEVEL2, LEVEL3 = "ddss", "hhhh"
SPARE = 2
HELD = 1
LOADS = [("s", "u", "ldu"), ("y", "x", "ldx"), ("y", "la", "ldl"), ("s", "lb", "ldl")]
HELDP = ["b"]
TWICE = True
ENOUGH = 162
OWN, AFTER = {0: 1, 2: 2, 3: 1, 1: 2}, {3: 0, 1: 2}
FAR_LOW = -2.0 ** 90
STEP = [1, 2, 4]
BIG = 2.0 ** 24
MID = 159
LOW = -256.0
BF, F32, I32, U16 = "bfloat16", "float32", "int32", "uint16"

START = dict(v="m8 gap z4 ki z0 ko uo kl z1 scl big kf sc2 z2 cw qu cx qup E0 ya yb md0 dw0 mh md1 dw1",
             s="qus kk cy",
             g="pi kd0 m16 kd1 d8 kd2 iof")
ORDER = dict(v="sga sgb ml sca scb T1b ms s2 E2 T1a p0@0 z3 T1c p1 T1x dp T2a E3 T3a L2a L2b c3 L3a p3 L3b k3a z5 k3b L6a L6b d1_ L9 c9 E1 p9 "
               "q0 T18a L18 T27a L27 c27 q2 p27 q3 q4 T54a L54 T81a L81 c81 k81a p81 L162 Ua ca bva ga T243a cb eq mn r4 st lw r2 tt "
               "nf fc d1 c324 s3 p324 pc pb fl a0 a1 a3 sx a2 b0 b3 b1 b2 c0 c3_ c1 c2a c2b za zb "
               "e1 e3 qv ek h0b e4 e5 x0 x2 e6 x3a x1a x3b x1b ya yb",
             s="sfb cp T1y T2b sfa T3b o0 o2 T6 T9 o3a k9 T18b T27b q1 o3b k27 T54b T81b o1 k81b w0 T162 Ub w1b bvb T243b w1a T324 g1 "
               "w3 w2 u3 u2 A0 A3 A2 B0 B3 B1 B2 ex h0a h2 h3 h1 jb mf df l1",
             t="Sa Sb O0 O2 O3 O1 F0 F1 F3 F2 H0a H0b H2 H3 H1",
             g=">q >s far0 far1 d0 >a >b A1")

SCRATCH = {}


def _sb(dtype, **kw):
    for k, n in kw.items():
        SCRATCH[k] = ("sbuf", [128, n], dtype)


_sb(BF, xin=1280, uin=512, vin=512, e8=516, kd=128, kk=C, sca=C, scb=C, scc=C, scd=C, sce=C, scx=C, mm=W, ps=992, ex=20,
    f1=W + 16, pp=2 * W, l2=2 * W, aw=2 * C, low=2 * C, ld=C, bv=C, fl=C,
    fw=1280, fd=W, fo=1280, hw=1280, tmp=3 * C, sp=12 * W, z1=1280, z2=1280, y1=1280, y2=1280, z3=1280, xt=1280)
_sb(F32, iof=W, dm=W, m16=20, kf=1, scl=1, sc2=1, big=1, kl=1, cw=20, cx=20, mid=20, sf=C, sg=C, pk=120, po=60,
    pu=164, s3_=80, cy=20, so=60, pt=60, mn=20, ed=20, lw_=40, lsf=2 * C, yf=C)
_sb(I32, lain=20, lbin=20, pi=20, ki=1)
_sb(U16, uo=8, ko=20, offs=140, lwo=20, pwo=20, lo_=40, dko=20, mso=20)
_sb("float8_e4m3fn_x4", wq=512, qu=128, qup=128, qv=128, qe8=512, qz=C)
_sb("uint8", wsq=512, su=128, sup=128, sv=128, se8=512, sz=C)
for _i in range(4):
    SCRATCH["q%d" % _i] = ("sbuf", [128, C], "float8_e4m3fn_x4")
    SCRATCH["s%d" % _i] = ("sbuf", [128, C], "uint8")
for _i in range(3):
    SCRATCH["lq%d" % _i] = ("sbuf", [128, C], "float8_e4m3fn_x4")
    SCRATCH["lp%d" % _i] = ("sbuf", [128, C], "uint8")
    for _k in ("ta", "tb", "la_", "lb_"):
        SCRATCH["%s%d" % (_k, _i)] = ("sbuf", [128, 40 if "b" in _k else 20], U16)
SCRATCH["psa"] = ("psum", [128, 2048], F32)
SCRATCH["psf"] = ("psum", [128, 1536], F32)
SCRATCH["pss"] = ("psum", [128, 512], F32)

SEMAPHORES = ["cv", "cs", "ct", "cg", "left", "gone", "ldx", "ldu", "ldv", "ldl", "ldw", "sto", "stc"]
SEMAPHORES += ["%s%d" % (k, i) for k in ("aq", "at", "ab") for i in range(3)]


def rank_program(g, core, T, topo):
    rank = T.rank_of(core)
    if rank is None:
        return
    N = len(T.cores)
    A = AluOpType
    COPY, SAME = ActivationFunctionType.Copy, ActivationFunctionType.Identity
    eng = {"v": g.vector, "s": g.scalar, "t": g.tensor, "g": g, "y": g.sync}
    cnt = {"v": 0, "s": 0, "t": 0, "g": 0}
    seen = {k: {} for k in eng}
    knew = {}

    def need(q, *toks):
        for tok in sorted(set(toks), key=lambda x: -len(knew.get(x, ()))):
            if seen[q].get(tok[0], 0) < tok[1] and not any(y != tok and knew.get(y, {}).get(tok[0], 0) >= tok[1] for y in toks):
                eng[q].wait_ge(T.sem[tok[0]], tok[1])
                for name, n in knew.get(tok, {tok[0]: tok[1]}).items():
                    seen[q][name] = max(n, seen[q].get(name, 0))

    def run(q, deps, fn, *a, **kw):
        need(q, *deps)
        cnt[q] += 1
        fn(*a, **kw).then_inc(T.sem["c" + q], 1)
        tok = ("c" + q, cnt[q])
        knew[tok] = {**knew.get(("c" + q, cnt[q] - 1), {}), **seen[q], tok[0]: tok[1]}
        return tok

    done = {}

    def issue(order, calls, i=0):
        before = dict(done)
        todo = {k: [x for x, _, r in (y.partition("@") for y in order[k].split()) if x in calls and (not r or str(i) in r)] for k in order}
        named = {x for k in todo for x in todo[k]}
        for x in named:
            done.pop(x, None)
        while any(todo.values()):
            assert any(v and all(y in done for y in calls[v[0]][0] if y in named) for v in todo.values()), "an order in which queues wait for each other"
            for k in todo:
                while todo[k] and all(y in done for y in calls[todo[k][0]][0] if y in named):
                    x = todo[k].pop(0)
                    deps, fn, a = calls[x]
                    toks = [y if isinstance(y, tuple) else before.get(y[1:]) if y[0] == "^" else done.get(y) for y in deps]
                    done[x] = fn(k, [y for y in toks if y], *a)

    V, S, TE = g.vector, g.scalar, g.tensor

    def w20(buf):
        return buf[:, 15:C:16]

    def blk(buf, b, lo=0, hi=C):
        return buf[:, C * b + lo:C * b + hi]

    def wide(buf, k):
        return buf[:, W * k:W * k + W]

    def even(buf, k, lo=0, hi=C):
        return buf[:, W * k + 2 * lo:W * k + 2 * hi:2]

    def mov(buf, b):
        return buf[:, 128 * b:128 * b + 128]

    def bank(buf, b, lo=0, hi=C):
        return buf[:, 512 * b + lo:512 * b + hi]

    LISTS = sorted({1} | {a for n, a in LINKS}) + [FAR]

    def off(a, lo=0, hi=C):
        k = LISTS.index(a)
        return T.offs[:, 20 * k + lo // 16:20 * k + hi // 16]

    def pick(q, deps, out, in_, scale=None):
        if q == "g":
            return run(q, deps, g.affine_select, out, in_, [[0, C]], A.is_equal, 0.0, 0, 0)
        if scale is None:
            return run(q, deps, V.tensor_copy, out, in_) if q == "v" else run(q, deps, S.activation, out, in_, COPY)
        return run(q, deps, V.tensor_scalar, out, in_, scale, None, A.mult) if q == "v" else run(q, deps, S.activation, out, in_, COPY, scale=scale)

    def affine(q, deps, out, in_, scale, bias):
        if q == "v":
            return run(q, deps, V.tensor_scalar, out, in_, scale, bias, A.mult, A.add)
        return run(q, deps, S.activation, out, in_, SAME, scale=scale, bias=bias)

    def mm(q, deps, out, side, plane, codes, scales, part):
        lo, hi = PART[part]
        return run(q, deps, TE.matmul_mx, out, side, plane, codes[:, lo:hi], scales[:, lo:hi], True, True)

    def quant(q, deps, codes, plane, tile, part):
        lo, hi = PART[part]
        return run(q, deps, V.quantize_mx, codes[:, lo:hi], plane[:, lo:hi], tile[:, 4 * lo:4 * hi])

    def scan(q, deps, out, factors, numbers):
        return run(q, deps, V.tensor_tensor_scan, out, factors, numbers, 0.0, A.mult, A.add)

    def place(q, deps, out, ends):
        return run(q, deps, V.tensor_scalar, out, ends, T.scl[:, 0:1], MID + 0.25, A.mult, A.add)

    def meet(name, parts=HALF, lo=0, hi=C):
        return [name + h for h, (x, y) in parts.items() if x < hi and lo < y]

    calls = {}

    def call(name, deps, fn, *a):
        calls[name] = (deps, fn, a)

    def vec(name, deps, fn, *a, **kw):
        calls[name] = (deps, lambda q, deps: run(q, deps, fn, *a, **kw), ())

    for k, name, sem in LOADS:
        eng[k].dma_start(T[name + "in"][:], T[name][:, :]).then_inc(T.sem[sem], 16)

    SMALL = {"allow_small_or_imprecise_dtypes": True}
    vec("pi", [], g.iota, T.pi[:], [[0, 20]], 0, 1)
    vec("m16", [], g.iota, T.m16[:], [[16, 20]], 0, 0, **SMALL)
    vec("kd0", [], g.iota, T.kd[:], [[0, 128]], 1, 0, **SMALL)
    for at, fill in enumerate((0.0, BIG)):
        vec("kd%d" % (at + 1), ["kd%d" % at], g.affine_select, T.kd[:], T.kd[:], [[1, 128]], A.not_equal, fill, -at, -1)
    vec("iof", [], g.iota, T.iof[:], [[1, W]], -C, 0, **SMALL)
    vec("m8", [], V.memset, T.e8[:], 0.0)
    vec("gap", [], V.memset, T.pp[:, 1:(LINKS[0][1] - 1) * W:2], LOW)
    vec("ki", ["pi"], V.tensor_scalar, T.ki[:], T.pi[:, 0:1], 15, None, A.bitwise_and)
    vec("ko", ["pi"], V.tensor_copy, T.ko[:], T.pi[:])
    vec("uo", ["m16"], V.tensor_copy, T.uo[:], T.m16[:, 0:8])
    fills = ((T.pk[:, 2:60:3], 1.0), (T.pk[:, 0:120:3], 0.0), (T.pt[:, 1:60:3], 0.0), (T.mm[:, 0:W:2], 0.0), (T.f1[:, 17:16 + W:2], 0.0),
             (T.pu[:, 0:164:4], 0.0))
    for k, (view, value) in enumerate(fills):
        vec("z%d" % k, [], V.memset, view, value)
    ONE = T.pk[:, 2:3]
    vec("kf", ["ki"], V.tensor_copy, T.kf[:], T.ki[:])
    vec("kl", ["ki"], V.tensor_scalar, T.kl[:], T.ki[:], 15.0, None, A.is_equal)
    for k, x, y in (("scl", 1.0, 1 / BIG), ("sc2", 2.0, 2 / BIG), ("big", 1.0, BIG)):
        vec(k, ["kl"], V.tensor_scalar, T[k][:], T.kl[:], x - y, y, A.mult, A.add)
    vec("cw", ["m16", "kf"], V.tensor_scalar, T.cw[:], T.m16[:], T.kf[:, 0:1], None, A.add)
    vec("d8", ["m8"], g.affine_select, T.e8[:, 3:515:4], T.e8[:, 3:515:4], [[1, 128]], A.not_equal, 0.125, 0, -1)
    vec("cx", ["cw", "big"], V.tensor_scalar, T.cx[:], T.cw[:], float(MID), T.big[:, 0:1], A.subtract, A.mult)

    call("cy", ["cw"], affine, T.cy[:], T.cw[:], 1.0, -float(MID))
    vec("d1_", ["E%d" % b for b in range(4) if b != HELD], V.tensor_scalar, T.e8[:, 3:515:4], T.e8[:, 3:515:4], 8.0, None, A.mult)
    for b in range(4):
        vec("E%d" % b, ["d1_" if b == HELD else "d8"], V.quantize_mx, mov(T.qe8, b), mov(T.se8, b), T.e8[:, 3 - b:515 - b])
    keys = [("1", b) for b in range(4) if LEVEL2[b] == "s"] + [("2", b) for b in range(4) if LEVEL2[b] != "s" and LEVEL3[b] != "h"]
    fars = ["far%d" % k for k in range((len(keys) + SPARE + 1) // 2)]
    for k, name in enumerate(fars):
        vec(name, ["iof"], g.affine_select, T.sp[:, 2 * W * k + 1:2 * W * (k + 1):2], T.iof[:], [[0, W]], A.not_equal, FAR_LOW, 0, 0)
    keys += [("2", b) for b in range(4) if LEVEL2[b] == "s"]
    slot = {x: k + SPARE for k, x in enumerate(keys)}
    scans = [x for x in ORDER["v"].split() if x in ["b%d" % b for b in range(4) if LEVEL2[b] == "s"] + ["c%d" % b for b in range(4) if LEVEL3[b] == "s"]]

    def spare(name):
        k = scans.index(name)
        return k % SPARE, fars + scans[max(k - SPARE, 0):max(k - SPARE + 1, 0)]
    vec("qu", [("ldu", 16)], V.quantize_mx, T.qu[:, 0:128], T.su[:, 0:128], T.uin[:])
    vec("qup", ["qu", "uo"], V.tensor_copy, T.qup[:, 0:128].bitcast(dt.uint32), T.qu[:, 0:128].bitcast(dt.uint32).indirect(T.uo[:, 0:8]))
    vec("qus", ["qu", "uo"], S.activation, T.sup[:, 0:128], T.su[:, 0:128].indirect(T.uo[:, 0:8]), COPY)
    call("kk", ["kd2", "ko"], pick, T.kk[:], T.kd[:, 0:128].indirect(T.ko[:, 0:20]))
    for k in "ab":
        call("y" + k, [("ldx", 16)], quant, T.q0, T.s0, T.xin, k)
    DW, P, HI, LO = T.pk[:, 1:60:3], T.po[:, 2:60:3], T.ps[:, 61:992:48], T.ps[:, 77:992:48]
    vec("dw0", [("ldl", 32)], V.tensor_tensor, DW, T.lain[:], T.lbin[:], A.subtract)
    vec("md0", [("ldl", 32)], V.tensor_tensor, T.ed[:], T.lain[:], T.lbin[:], A.add)
    vec("dw1", ["dw0", "scl"], V.tensor_scalar, DW, DW, T.scl[:, 0:1], None, A.mult)
    call("ms", ["md0"], pick, T.mso[:], T.ed[:])
    call("md1", ["md0"], affine, T.mid[:], T.ed[:], 0.5, 0.25)
    call("mh", ["md0"], affine, HI, T.ed[:], 0.5, 0.25)
    vec("ml", ["mh", "md1"], V.tensor_tensor, LO, T.mid[:], HI, A.subtract)
    vec("mf", ["ms", "iof", "z0"], S.activation, T.dm[:, 1:W:2], T.iof[:, 0:W].indirect(T.mso[:, 0:20]), SAME, scale=0.5, bias=ONE)

    def difference(dep):
        vec("ek", [dep, "big"], V.tensor_scalar, T.dko[:], DW, T.big[:, 0:1], float(C), A.mult, A.add)
        call("df", ["ek", "iof"], pick, T.dm[:, 0:W:2], T.iof[:, 0:W].indirect(T.dko[:, 0:20]))

    difference("dw1")
    issue(START, calls)

    left = 0
    for i, d in enumerate(STEP):
        q, s = T["q%d" % i], T["s%d" % i]
        lq, lp = T["lq%d" % i], T["lp%d" % i]
        ta, tb, la, lb = [T["%s%d" % (k, i)] for k in ("ta", "tb", "la_", "lb_")]
        dst = T.cores[(rank + d) % N]
        src = T.cores[(rank - d) % N]
        rid, pid, _ = topo.addr(dst)
        mask = topo.mask(core, dst)
        ne, na = len(topo.engines(core, dst)), len(topo.engines(src, core))
        at, ab = [("%s%d" % (k, i), na) for k in ("at", "ab")]
        if i:
            calls.clear()

        def send(k, deps, out, in_, sem, local):
            need(k, *deps)
            g.remote_dma(out, in_, T.sem["%s%d" % (sem, i)], T.sem[local], pid, rid, mask)

        first = "left" if i else "gone"
        call(">q", ["^yb"], send, lq[:, 0:C].bitcast(dt.uint8), q[:, 0:C].bitcast(dt.uint8), "aq", first)
        call(">s", ["^yb"], send, lp[:, 0:C], s[:, 0:C], "aq", first)
        call(">a", ["tt"], send, la[:, 0:20], ta[:, 0:20], "at", "left")
        call(">b", ["pb", "pc"], send, lb[:, 0:40], tb[:, 0:40], "ab", "left")
        left += (4 if i else 2) * ne
        if i == 0:
            need("y", ("gone", 2 * ne))
            g.sync.dma_start(T.wq[:, 0:512].bitcast(dt.uint8), T.wc[:, :]).then_inc(T.sem.ldw, 16)
            g.sync.dma_start(T.wsq[:, 0:512], T.ws[:, :]).then_inc(T.sem.ldw, 16)
            g.sync.dma_start(T.vin[:], T.v[:, :]).then_inc(T.sem.ldv, 16)
            vec("qv", [("ldv", 16)], V.quantize_mx, T.qv[:, 0:128], T.sv[:, 0:128], T.vin[:])

        sbank = {"a": bank(T.pss, 0, 0, CUT), "b": bank(T.psf, 0, 0, C - CUT)}
        for k in "ab":
            lo, hi = PART[k]
            call("S" + k, ["^y" + k, "qup", "qus"], mm, sbank[k], T.qup[:, 0:128], T.sup[:, 0:128], q, s, k)
            vec("sg" + k, ["S" + k], V.tensor_scalar, T.mm[:, 2 * lo + 1:2 * hi:2], sbank[k], 0.0, 0.5, A.is_ge, A.subtract)
            call("sf" + k, ["sg" + k], pick, blk(T.sf, 0, lo, hi), sbank[k])
        for k, (lo, hi) in PART.items():
            call("sc" + k, ["sga", "kk"] + ["sgb"] * (hi > CUT), scan, T.ps[:, 3 * lo:3 * hi:3], T.kk[:, lo:hi], T.mm[:, 2 * lo + 1:2 * hi:2])
        call("s2", ["sc", "sca", "scb", "^e1", "dw1", "ml", "z0", "z1"], scan, T.po[:], T.pk[:, 0:60], T.ps[:, 45:992:16])
        vec("p1", ["s2"], V.tensor_scalar, off(1), P, 2.0, 0.25, A.mult, A.subtract)
        if i or "df" in START["s"] + START["v"]:
            for h, (lo, hi) in THIRD.items():
                call("T1" + h, ["sga", "^df", "mf", "z3"] + ["sgb"] * (hi > CUT), scan, T.f1[:, 15 + 2 * lo:15 + 2 * hi], T.mm[:, 2 * lo:2 * hi], T.dm[:, 2 * lo:2 * hi])
        else:
            vec("T1x", ["p0", "iof"], V.tensor_scalar, T.f1[:, 16:16 + C:2], T.iof[:, C // 2:W].indirect(T.pwo[:, 0:10]), 1.0, None, A.add)
            vec("T1y", ["p0", "iof"], S.activation, T.f1[:, 16 + C:16 + W:2], T.iof[:, C // 2:W].indirect(T.pwo[:, 10:20]), SAME, bias=ONE)
        call("p0", ["s2"], pick, T.pwo[:], P)
        call("cp", ["s2"], affine, T.pt[:, 2:60:3], P, 1.0, -MID - 0.25)
        vec("dp", ["s2", "cw"], V.tensor_tensor, T.pk[:, 62:120:3], T.cw[:], P, A.subtract)

        F = LINKS[0][1]
        link = low = T.f1[:, 16:15 + W]
        for k in range(2, F + 1):
            for h, (lo, hi) in EARLY.items():
                call("T%d%s" % (k, h), ["p1", "gap"] + ["T%d%s" % (k - 1, y) for y in "abcxy"], pick, even(T.pp, k - 2, lo, hi), link.indirect(off(1, lo, hi)))
            link = T.pp[:, W * (k - 2):W * (k - 1) - 1]
            for h, (lo, hi) in HALF.items():
                x = T.f1[:, 16 + 2 * lo:15 + 2 * hi] if k == 2 else T.l2[:, W * (1 - k % 2) + 2 * lo:W * (1 - k % 2) + 2 * hi - 1]
                vec("L%d%s" % (k, h), meet("L%d" % (k - 1), HALF, lo, hi) + ["T%da" % k, "T%db" % k, "z4"], V.tensor_tensor_scan,
                    T.l2[:, W * (k % 2) + 2 * lo:W * (k % 2) + 2 * hi - 1], x, T.pp[:, W * (k - 2) + 2 * lo:W * (k - 2) + 2 * hi - 1], LOW, A.max, A.min)
            low = T.l2[:, W * (k % 2):W * (k % 2 + 1) - 1]
        call("c%d" % F, ["T%da" % F, "T%db" % F], scan, T.sca[:], T.kk[:], even(T.pp, F - 2))
        vec("p%d" % F, ["c%d" % F, "sc2"], V.tensor_scalar, off(F), w20(T.sca), T.sc2[:, 0:1], 2 * MID + 0.25, A.mult, A.add)
        for h, (lo, hi) in HALF.items():
            call("k%d%s" % (F, h), meet("L%d" % F, HALF, lo, hi), pick, blk(T.ld, 0, lo, hi), even(T.l2, F % 2, lo, hi))
        for j, (n, a) in enumerate(LINKS):
            m = n - a
            for h, (lo, hi) in SHARE[j % 2].items():
                call("T%d%s" % (n, h), meet("T%d" % m) + ["p%d" % a] + meet("L2"), pick, T.f1[:, 16 + 2 * lo:16 + 2 * hi:2] if j == 0 else blk(T.aw, j % 2, lo, hi),
                     link.indirect(off(a, lo, hi)))
            for h, (lo, hi) in HALF.items():
                vec("L%d%s" % (n, h), meet("L%d" % m) + ["p%d" % a] + meet("k%d" % a, HALF if a == F else SPLIT, lo, hi), V.tensor_tensor,
                    even(T.l2, 1 - F % 2, lo, hi) if j == 0 else blk(T.low, j % 2, lo, hi), low.indirect(off(a, lo, hi)), blk(T.ld, 0, lo, hi), A.min)
            link, low = (T.f1[:, 16:15 + W], T.l2[:, W * (1 - F % 2):W * (2 - F % 2) - 1]) if j == 0 else (blk(T.aw, j % 2), blk(T.low, j % 2))
            if n in LISTS:
                ends = T.scc if n == FAR else T.sca
                call("c%d" % n, meet("T%d" % n), scan, ends[:], T.kk[:], link)
                call("p%d" % n, ["c%d" % n], place, off(n), w20(ends))
                for h, (lo, hi) in SPLIT.items():
                    call("k%d%s" % (n, h), meet("L%d" % n, HALF, lo, hi), pick, blk(T.ld, 0, lo, hi), blk(T.low, j % 2, lo, hi))
            if n == ENOUGH:
                for h, (lo, hi) in FINAL.items():
                    if TWICE:
                        call("U" + h, meet("L%d" % n), pick, blk(T.ld, 0, lo, hi), low.indirect(off(a, lo, hi)))
                        call("bv" + h, ["Ua", "Ub"], pick, blk(T.bv, 0, lo, hi), T.ld[:, 0:C].indirect(off(a, lo, hi)))
                    else:
                        call("bv" + h, meet("L%d" % n) + ["p%d" % LAST], pick, blk(T.bv, 0, lo, hi), low.indirect(off(LAST, lo, hi)))
                call("ca", meet("L%d" % n), scan, T.sce[:], T.kk[:], low)
        call("cb", ["bva", "bvb"], scan, T.scd[:], T.kk[:], T.bv[:])
        vec("ga", ["ca", "cx"], V.tensor_tensor, T.pk[:, 61:120:3], w20(T.sce), T.cx[:], A.is_ge)
        vec("eq", ["cb", "cx"], V.tensor_tensor, T.pt[:, 0:60:3], w20(T.scd), T.cx[:], A.is_equal)
        call("st", ["eq", "ga", "dp", "cp", "z2"], scan, T.so[:], T.pk[:, 60:120], T.pt[:])
        vec("tt", ["st"], V.tensor_scalar, ta[:, 0:20], T.so[:, 2:60:3], MID + 0.125, None, A.add)

        for b in range(4):
            call("F%d" % b, [("aq%d" % i, 2 * na), "E%d" % b], mm, bank(T.psa, b), mov(T.qe8, b), mov(T.se8, b), lq, lp, "")
            call("O%d" % b, ["E%d" % b, "^yb"] + ["o%d%s" % (AFTER[b], h) for h in HALF if b in AFTER], mm, bank(T.psf, OWN[b]), mov(T.qe8, b), mov(T.se8, b), q, s, "")
            for h, (lo, hi) in HALF.items():
                call("w%d%s" % (b, h), ["F%d" % b], pick, blk(T.fw, b, lo, hi), bank(T.psa, b, lo, hi), 0.125 if b == HELD else None)
                call("o%d%s" % (b, h), ["O%d" % b], pick, blk(T.fo, b, lo, hi), bank(T.psf, OWN[b], lo, hi), 1.0 if b == HELD else 8.0)
        for b in (0, 1):
            call("d%d" % b, ["w%d%s" % (b, h) for h in HALF], pick, blk(T.fd, b), blk(T.fw, b))
        PW, LEADS = T.pt[:, 2:60:3], T.so[:, 1:60:3]
        times, plus = [T.pu[:, k:80:4] for k in range(4)], [T.pu[:, 83 + k:163:4] for k in range(4)]
        call("q0", ["T2a", "T2b"], scan, T.scb[:], T.kk[:], even(T.pp, 0))
        call("q1", ["q0", "z5"], pick, plus[2], w20(T.scb), T.scl[:, 0:1])
        vec("q2", ["q1", "cp"], V.tensor_tensor, times[2], PW, plus[2], A.subtract)
        vec("q3", ["cp", "z5"], V.tensor_scalar, times[1], PW, 0.5, T.big[:, 0:1], A.subtract, A.mult)
        vec("q4", ["cp", "z5"], V.tensor_scalar, plus[0], PW, 0.5, T.big[:, 0:1], A.add, A.mult)
        vec("r2", ["mn", "q3"], V.tensor_tensor, times[1], T.mn[:], times[1], A.is_ge)
        vec("r4", ["cb", "q4"], V.tensor_tensor, plus[0], w20(T.scd), plus[0], A.is_le)
        call("nf", ["st"], affine, times[3], LEADS, -1.0, 1.0)
        vec("fc", ["st", "cy"], V.tensor_tensor, plus[3], LEADS, T.cy[:], A.mult)
        call("s3", ["r2", "r4", "nf", "fc", "q2"], scan, T.s3_[:], T.pu[:, 0:80], T.pu[:, 83:163])
        vec("pb", ["s3"], V.tensor_scalar, tb[:, 0:20], T.s3_[:, 3:80:4], MID + 0.25, None, A.add)
        vec("pc", ["s3"], V.tensor_scalar, tb[:, 20:40], T.s3_[:, 3:80:4], 2.0, 2 * MID + 0.25, A.mult, A.add)
        vec("mn", ["cb", "ca"], V.tensor_tensor, T.mn[:], w20(T.sce), w20(T.scd), A.min)
        call("lw", ["mn"], place, T.lwo[:], T.mn[:])
        call("g1", ["lw", "sfa", "sfb"], pick, T.sg[:], T.sf[:, 0:C].indirect(T.lwo[:, 0:20]))
        vec("fl", ["g1", "p%d" % FAR], V.tensor_tensor, T.fl[:], T.sg[:, 0:C].indirect(off(FAR)), T.sf[:], A.is_le)
        call("sx", ["fl"], scan, T.scx[:], T.kk[:], T.fl[:])
        call("ex", ["sx"], affine, T.ex[:], w20(T.scx), T.sc2[:, 0:1], -1.0)
        vec("e1", ["ex"], V.tensor_tensor, DW, DW, T.ex[:], A.mult)
        if i < 2:
            difference("e1")
        else:
            vec("e3", ["e1"], V.tensor_scalar, T.ed[:], DW, T.big[:, 0:1], 0.5, A.mult, A.mult)
            vec("e4", ["e3"], V.tensor_tensor, T.lw_[:, 0:20], T.mid[:], T.ed[:], A.add)
            vec("e5", ["e3"], V.tensor_tensor, T.lw_[:, 20:40], T.mid[:], T.ed[:], A.subtract)
            call("e6", ["e4", "e5"], pick, T.lo_[:], T.lw_[:])
            call("l1", ["e6"], pick, T.lsf[:], T.iof[:, C:W].indirect(T.lo_[:, 0:40]))
        for b in range(4):
            ws = ["w%d%s" % (b, h) for h in HALF]
            two, three = LEVEL2[b], LEVEL3[b]
            spaced = two == "s" or three != "h"
            z1 = even(T.sp, slot["1", b]) if two == "s" else blk(T.z1, b)
            z2 = (lambda lo, hi: even(T.sp, slot["2", b], lo, hi)) if spaced else (lambda lo, hi: blk(T.z2, b, lo, hi))
            if b < FUSED:
                vec("a%d" % b, [at, "d%d" % b], V.tensor_tensor, z1, blk(T.fw, b).indirect(la[:, 0:20]), blk(T.fd, b), A.add)
            else:
                call("u%d" % b, [at] + ws, pick, blk(T.tmp, b - 1), blk(T.fw, b).indirect(la[:, 0:20]))
                vec("a%d" % b, ["u%d" % b], V.tensor_tensor, z1, blk(T.tmp, b - 1), bank(T.psa, b), A.add)
            if two == "s":
                k, deps = spare("b%d" % b)
                call("A%d" % b, ["a%d" % b, ab] + deps, pick, even(T.sp, k), wide(T.sp, slot["1", b]).indirect(lb[:, 20:40]))
                vec("b%d" % b, ["A%d" % b], V.tensor_tensor_scan, wide(T.sp, slot["2", b]), wide(T.sp, k), wide(T.sp, slot["1", b]), FAR_LOW, A.max, A.add)
            elif two == "d":
                call("A%d" % b, ["a%d" % b], pick, blk(T.y1, b), z1)
                vec("b%d" % b, ["A%d" % b, ab], V.tensor_tensor, z2(0, C), blk(T.y1, b).indirect(lb[:, 0:20]), z1, A.add)
            else:
                call("A%d" % b, ["a%d" % b], pick, blk(T.y1, b), z1.indirect(la[:, 0:20]))
                vec("b%d" % b, ["A%d" % b], V.tensor_tensor, z2(0, C), blk(T.y1, b).indirect(la[:, 0:20]), z1, A.add)
            call("B%d" % b, [ab, "b%d" % b], pick, blk(T.y2, b), wide(T.sp, slot["2", b]).indirect(lb[:, 20:40]) if spaced else blk(T.z2, b).indirect(lb[:, 0:20]))
            for k, (lo, hi) in PART.items():
                vec("c%d%s" % (b, k or "_" * (b == 3)), [ab, "B%d" % b], V.tensor_tensor, T.z3[:, 4 * lo + b:4 * hi:4],
                    blk(T.y2, b).indirect(lb[:, lo // 16:hi // 16]), z2(lo, hi), A.add)
        for k, hb in (("a", bank(T.psa, 0, 0, CUT)), ("b", bank(T.pss, 0, 0, C - CUT))):
            call("z" + k, ["c0", "c1", "c2", "c3_", "c2" + k, "c3" + k], quant, T.qz, T.sz, T.z3, k)
            call("H0" + k, ["z" + k, ("ldw", 32)], mm, hb, mov(T.wq, 0), mov(T.wsq, 0), T.qz, T.sz, k)
            call("h0" + k, ["H0" + k], pick, blk(T.hw, 0, *PART[k]), hb, 0.03125)
            call("y" + k, ["x%d%s" % (b, h) for b in range(4) for h in ("", k)], quant, T["q%d" % (i + 1)], T["s%d" % (i + 1)], T.xt, k)
        for b in range(4):
            call("H%d" % b, ["zb"], mm, bank(T.psa, b), mov(T.wq, b), mov(T.wsq, b), T.qz, T.sz, "")
            call("h%d" % b, ["H%d" % b], pick, blk(T.hw, b), bank(T.psa, b), 0.03125)
            for k, (lo, hi) in PART.items():
                if b == HELD and k in HELDP:
                    call("j" + k, ["h%d" % b], pick, blk(T.tmp, 0, lo, hi), blk(T.hw, b).indirect(ta[:, lo // 16:hi // 16]))
                    vec("x%d%s" % (b, k), ["j", "j" + k, "O%d" % b], V.tensor_tensor, T.xt[:, 4 * lo + b:4 * hi:4], blk(T.tmp, 0, lo, hi), bank(T.psf, OWN[b], lo, hi), A.add)
                else:
                    vec("x%d%s" % (b, k), ["%s%d%s" % (y, b, h) for y in "oh" for h in HALF], V.tensor_tensor, T.xt[:, 4 * lo + b:4 * hi:4],
                        blk(T.hw, b).indirect(ta[:, lo // 16:hi // 16]), blk(T.fo, b, lo, hi), A.add)
        issue(ORDER, calls, i)
        if i == 0:
            gone = 2 * ne

    tq = [done["ya"], done["yb"]]
    ybank = [bank(T.psa, 0, 0, CUT), bank(T.psa, 1, 0, C - CUT)]
    yy = [mm("t", [tq[h], done["qv"]], ybank[h], T.qv[:, 0:128], T.sv[:, 0:128], T.q3, T.s3, "ab"[h]) for h in (0, 1)]
    yb = [pick("v", [yy[h]], blk(T.yf, 0, *PART["ab"[h]]), ybank[h]) for h in (0, 1)][1]
    need("y", tq[1])
    g.sync.dma_start(T.oc[:, :], T.q3[:, 0:C].bitcast(dt.uint8)).then_inc(T.sem.sto, 16)
    need("s", tq[1])
    for k in range(4):
        (g.sync, g.scalar)[k % 2].dma_start(T.osc[4 * k:4 * k + 4, :], T.s3[32 * k:32 * k + 4, 0:C]).then_inc(T.sem[("sto", "stc")[k % 2]], 16)
    need("y", done["l1"])
    g.sync.dma_start(T.ls[:, :], T.lsf[0:128:16, :]).then_inc(T.sem.sto, 16)
    need("s", yb)
    g.scalar.dma_start(T.y[:, :], T.yf[:]).then_inc(T.sem.stc, 16)
    need("g", ("cv", cnt["v"]), ("cs", cnt["s"]), ("ct", cnt["t"]), ("cg", cnt["g"]), ("left", left), ("gone", gone), ("sto", 64), ("stc", 48))
